import numpy as np, ml_dtypes
CORES = [16,17,18,19,32,33,34,35]
N = 8
import mx_ref
BF = ml_dtypes.bfloat16
def gcols(t, e):
    v = np.concatenate([t.reshape(8, 16, -1, 4), np.zeros((8, 16, 1, 4), BF)], axis=2)
    return np.ascontiguousarray(np.stack([v[g][:, e[g]] for g in range(8)])).reshape(128, -1)
def tile(rs):
    return np.stack(rs, axis=2).reshape(128, -1).astype(BF)
def cut(t, i, w=512):
    return t[:, w * i:w * i + w]
def pick(q, e):
    c = np.concatenate([q[0].reshape(128, -1, 4), np.zeros((128, 1, 4), np.uint8)], axis=1); s = np.concatenate([q[1], np.ones((16, 1), np.uint8)], axis=1)
    return (np.ascontiguousarray(c[:, e].reshape(128, -1)), np.ascontiguousarray(s[:, e]))
def join(*qs):
    return (np.concatenate([q[0] for q in qs], axis=1), np.concatenate([q[1] for q in qs], axis=1))
def put(q, e, v):
    c, s = q[0].reshape(128, -1, 4).copy(), q[1].copy(); c[:, e] = v[0].reshape(128, -1, 4); s[:, e] = v[1]
    return (c.reshape(128, -1), s)
def pk(c, s):
    return (np.ascontiguousarray(c), mx_ref.live(s))
def emit(q):
    return q[0], q[1]
def packed(v, rng):
    q = [mx_ref.quantize(np.ascontiguousarray(v[r])) for r in range(N)]
    return np.stack([a for a, b in q]), np.stack([mx_ref.plane(b, rng) for a, b in q])
def values_of_codes():
    e, c = np.zeros((128, 128, 4), np.float32), np.zeros((128, 2, 4), np.uint8)
    e[np.arange(128), np.arange(128), 0] = 1
    c[:127, :, 0] = np.arange(256).reshape(2, 128).T[:127]
    return mx_ref.matmul(mx_ref.quantize(e.reshape(128, 512).astype(BF)), (c.reshape(128, 8), np.full((16, 2), 127, np.uint8))).T.reshape(-1).astype(np.float64)
CODE_VALUE, SCALE_VALUE = values_of_codes(), 2.0 ** (np.arange(256) - 127.0)
def decode(q):
    return (CODE_VALUE[q[0]].reshape(16, 8, -1, 4) * SCALE_VALUE[q[1]][:, None, :, None] + 0.0).reshape(128, -1).astype(np.float32)
def f(rng, *shape):
    return mx_ref.flush((rng.standard_normal(shape, dtype=np.float32) * np.exp2(rng.integers(-2, 3, shape[:-1] + (1,)))).astype(BF))
def wide(rng, *shape, cols=0):
    v = rng.standard_normal(shape, dtype=np.float32) * np.exp2(rng.integers(-12, 13, shape)).astype(np.float32)
    if cols: v *= np.repeat(np.exp2(rng.integers(-cols, cols + 1, shape[:-2] + (1, shape[-1] // 4))) * (rng.random(shape[:-2] + (1, shape[-1] // 4)) > 0.0625), 4, axis=-1).astype(np.float32)
    return mx_ref.flush(v.astype(BF))
C, L, R = 384, 64, 3
def order(p, s):
    return np.lexsort((-(s + np.float32(0.0)), -p))
def pairs(p):
    a, b = np.zeros((8, C // 2), np.int64), np.zeros((8, C // 2), np.int64)
    for g in range(8):
        end = [int(np.sum(p[g] >= k)) // 2 * 2 for k in range(3 + R, -1, -1)]
        for i, k in zip(end, end[1:]):
            m = (k - i) // 2
            a[g, i // 2:k // 2] = np.arange(i, i + m)
            b[g, i // 2:k // 2] = np.arange(i + m, k)
    return a, b
def gput(t, e, h):
    a, b = t.reshape(8, 16, -1, 4).copy(), h.reshape(8, 16, -1, 4)
    for g in range(8): a[g][:, e[g]] = b[g]
    return a.reshape(128, -1)
def big(v):
    v = v.astype(np.float32)
    v[np.abs(v) < np.float32(2.0 ** -16)] = 0
    return v.astype(BF)
def numbers_of(rng):
    return {"x": big(f(rng, N, 128, 4 * C)), "u": np.array(f(rng, N, 128, 512)), "v": np.array(f(rng, N, 128, 512))}
def layers(rng):
    return big(f(rng, N, 128, 2048)).reshape(N, 8, 16, 4, 8, 16, 4)
def weights(rng, w):
    c, p = packed(np.ascontiguousarray(w).reshape(N, 128, 2048), rng)
    return {"wc": c, "ws": p}
def signs(rng):
    return np.stack([rng.permutation(8) % 2 * 2.0 - 1.0 for r in range(N)])
def setup_inputs(rng):
    return {**numbers_of(rng), **weights(rng, layers(rng))}
def setup_inputs_ties(rng):
    d = numbers_of(rng)
    e = rng.permutation(N)
    x = d["x"].reshape(N, 8, 16, C, 4)
    for r in range(N):
        k = np.zeros(C, int) if r == e[0] else rng.permutation(C) % 3
        a = x[r][:, :8, :3].copy()
        a[:, :, 2] = 0
        x[r][:, :8] = a[:, :, k]
    x[e[1]] = 0
    u = d["u"].reshape(N, 8, 16, 8, 16, 4)
    u[:, :, 8:, :, :4] = 0
    w = layers(rng)
    w[:, :, 8:, :, :, :8] = 0
    return {"x": x.reshape(N, 128, 4 * C), "u": u.reshape(N, 128, 512), "v": d["v"], **weights(rng, w)}
def setup_inputs_near(rng):
    d = numbers_of(rng)
    x = np.zeros((N, 8, 16, C, 4), np.float32)
    u = d["u"].reshape(N, 128, 128, 4)
    for m in range(4): u[:, :, m::16] = 0
    o, c = rng.permutation(N) % 4, signs(rng)
    upper = np.arange(C) // (C // 2)
    for r in range(N):
        i = (np.arange(C) + rng.integers(0, C, (8, 1))) % C
        if o[r] == 3: i = i % (C // 2) * 2 + upper
        s = (i + 1) // 2
        size = 1.0 if o[r] < 2 else 2.0 ** -4
        g = ((s[:, :, None] >> np.arange(8)) & 1) * np.exp2(np.arange(8) - 23.0) * size
        if o[r] < 2: x[r, :, 0, :, 0] = c[r][:, None]
        if o[r] == 3:
            x[r, :, 0, :, 0] = (8 + upper) * 2.0 ** -33
            x[r, :, 1, :, 0] = (9 - upper) * 2.0 ** -33
        x[r, :, 8] = g[:, :, :4]
        x[r, :, 9] = g[:, :, 4:]
        x[r, :, 10:] = rng.integers(4, 8, (8, 6, C, 4)) * 2.0 ** -20 * size
        x[r, :, 11, :, 0] = rng.integers(-1, 2, (8, C)) * 2.0 ** -18 * size
        x[r, :, 12, :, 0] = 0
        same = (rng.permutation(8) % 2 == 0)[:, None, None]
        x[r, :, 13:, :, 0] = np.where(same, rng.integers(-1, 2, (8, 3, 1)), rng.integers(-1, 2, (8, 3, C))) * 2.0 ** -18 * size
        k = 1.0 if o[r] == 0 else 2.0 ** -30
        for h in range(0, 128, 16):
            u[r, h, h, 0] = 1.125 * k if o[r] == 3 else k
            u[r, h + 1, h, 0] = k
            u[r, h + 8:h + 10, h] = k
            u[r, h + 12, h, 0] = k
            for m in range(3): u[r, h + 13 + m, h + 1 + m, 0] = k
    w = layers(rng)
    w[:, :, :10] = 0
    w[:, :, :, :, :, :2] = 0
    w[:, :, :, :, :, 8:] = 0
    for g in range(8): w[:, g, 11, 0, g, 12, 0] = 0.25
    return {"x": x.reshape(N, 128, 4 * C).astype(BF), "u": u.reshape(N, 128, 512), "v": d["v"], **weights(rng, w)}
def setup_inputs_brackets(rng):
    d = numbers_of(rng)
    x = d["x"].reshape(N, 8, 16, C, 4)
    x[:, :, :8] = 0
    x[:, :, 12] = 0
    q = rng.integers(-1, 2, (N, 8, C))
    for g, m in enumerate(rng.permutation(8)):
        if m < 3: q[:, g] = m - 1
    x[:, :, 13, :, 0] = q.astype(np.float32).astype(BF)
    small = rng.permutation(N) < N // 2
    for r in range(N):
        i, j, k = 2 * rng.integers(0, C // 8, 3) + 1
        n = rng.permutation(np.array([[0, 0, 0, C], [C, 0, 0, 0], [1, 0, 0, C - 1], [C - 1, 0, 0, 1], [1, 1, 1, C - 3], [C - 2 * L, 0, 0, 2 * L], [0, 3, 0, C - 3], [i, j, k, C - i - j - k]]))
        unit = 2.0 ** -30 if small[r] else 0.125
        for g in range(8):
            p = rng.permutation(np.repeat([3, 2, 1, 0], n[g]))
            on = np.argsort(rng.random((3, C)), axis=0) < p
            a = np.where(on, 1.0, -1.0 * rng.integers(0, 2, (3, C)))
            x[r, g, :3, :, 0] = ((8 + np.maximum(a, 0)) * unit).astype(np.float32).astype(BF)
            x[r, g, 3:6, :, 0] = ((8 + np.maximum(-a, 0)) * unit).astype(np.float32).astype(BF)
    u = d["u"].reshape(N, 8, 16, 8, 16, 4)
    b = u.copy()
    s = np.where(small, 2.0 ** -30, 1.0).astype(np.float32)
    u[:, :, :, :, :4] = 0
    w = layers(rng)
    w[:, :, :, :, :, 8:] = 0
    for g in range(8):
        u[:, g, 8:11, g, 0] = b[:, g, 8:11, g, 0]
        u[:, g, 12, g, 0, 0] = 1
        for m in range(3):
            u[:, g, m, g, 1 + m, 0] = s.astype(BF)
            u[:, g, 3 + m, g, 1 + m, 0] = (-s).astype(BF)
        w[:, g, 13, 0, g, 12, 0] = 1
    return {"x": x.reshape(N, 128, 4 * C), "u": u.reshape(N, 128, 512), "v": d["v"], **weights(rng, w)}
def setup_inputs_huge(rng):
    d = numbers_of(rng)
    c = np.stack([rng.permutation(C) % 2 * 2.0 - 1.0 for r in range(N)])
    c[rng.permutation(N) < N // 2] = -1
    x = 2.0 ** 30 * (0.55 + 0.2 * rng.random((N, 128, C, 4))) * c[:, None, :, None]
    u = d["u"].reshape(N, 128, 8, 16, 4)
    k = rng.choice([-1.0, 1.0], (N, 8, 4))
    k[:, :, 0] = signs(rng)
    a = 2.0 ** 30 * (1 - 0.1 * rng.random((N, 128, 8, 4, 4))) * k[:, None, :, :, None]
    u[:, :, :, :4] = a.astype(np.float32).astype(BF)
    w = np.zeros((N, 128, 4, 128, 4), np.float32)
    i = np.arange(128)
    for b in range(4): w[:, i, b, i, b] = -1
    return {"x": x.astype(np.float32).reshape(N, 128, 4 * C).astype(BF), "u": u.reshape(N, 128, 512), "v": d["v"], **weights(rng, w.astype(BF))}
def setup_inputs_spread(rng):
    d = setup_inputs(rng)
    d["x"] = big(wide(rng, N, 128, 4 * C, cols=6))
    return d
def check_inputs(d):
    b = []
    for k in ("x", "u", "v"):
        a = np.abs(d[k].astype(np.float32))
        if not (np.isfinite(a).all() and ((a == 0) | (a >= 2.0 ** -30) & (a <= 2.0 ** 30)).all()): b.append("a value of " + k)
    none, least, most = [emit(mx_ref.quantize(np.full((128, 16), k, np.float32).astype(BF)))[1][0, 0] for k in (0.0, 2.0 ** -30, 2.0 ** 30)]
    for r in range(N):
        if ((d["wc"][r] == 0x7F) | (d["wc"][r] == 0xFF)).any(): b.append("wc: a code that is no number")
        s = mx_ref.live(d["ws"][r])
        if ((s != none) & ((s < least) | (s > most))).any(): b.append("ws: a scale out of range")
    return b
def reference(x, u, v, wc, ws):
    qu = [mx_ref.quantize(u[r]) for r in range(N)]
    lay = [pk(wc[r], ws[r]) for r in range(N)]
    now = [x[r] for r in range(N)]
    points = []
    for t in range(R):
        sent, gone, moved = [], [], []
        for r in range(N):
            s = mx_ref.matmul(qu[r], mx_ref.quantize(now[r]))
            if t == 0: points.append(np.sum(s.reshape(8, 16, C)[:, 1:4] > 0, axis=1))
            o = order(points[r], s[::16])
            i, k = pairs(points[r])
            a, b = np.take_along_axis(o, i, 1), np.take_along_axis(o, k, 1)
            first, second = gcols(now[r], a).astype(np.float32), gcols(now[r], b).astype(np.float32)
            q = mx_ref.quantize(((first + second) * np.float32(0.5)).astype(BF))
            h = tile([mx_ref.matmul(pick(lay[r], np.arange(128 * m, 128 * m + 128)), q) * np.float32(0.03125) for m in range(4)])
            won = mx_ref.matmul(qu[r], mx_ref.quantize(h))[::16] > 0
            h = h.astype(np.float32)
            now[r] = gput(gput(now[r], a, (first + h).astype(BF)), b, (second - h).astype(BF))
            gain = np.zeros((8, C), np.int64)
            np.put_along_axis(gain, a, won.astype(np.int64), 1)
            np.put_along_axis(gain, b, (~won).astype(np.int64), 1)
            points[r] = points[r] + gain
            back = np.take_along_axis(points[r], o, 1)[:, ::-1]
            e = np.take_along_axis(o, C - 1 - np.argsort(back, axis=1, kind="stable")[:, :L], 1)
            gone.append(e)
            moved.append(np.take_along_axis(points[r], e, 1))
            sent.append(mx_ref.quantize(gcols(now[r], e)))
        came = decode(join(*sent)).astype(BF)
        for r in range(N):
            p = (r - 1) % N
            now[r] = gput(now[r], gone[r], cut(came, p, 4 * L))
            np.put_along_axis(points[r], gone[r], moved[p], 1)
    y, pts = np.zeros((N, 128, C), np.float32), np.zeros((N, 8, C), np.float32)
    oc, osc = np.zeros((N, 128, 4 * C), np.uint8), np.zeros((N, 16, C), np.uint8)
    for r in range(N):
        q = mx_ref.quantize(now[r])
        y[r] = mx_ref.matmul(mx_ref.quantize(v[r]), q)
        pts[r] = points[r]
        oc[r], osc[r] = emit(q)
    return {"y": y, "pts": pts, "oc": oc, "osc": osc}

@@ -1,0 +1,503 @@
+from concourse.bass import DstId, RemoteDMATransfer
+from concourse.mybir import dt, AluOpType, ActivationFunctionType
+
+A = AluOpType
+F = ActivationFunctionType
+C, L, R = 384, 64, 3
+BIG = 1e29
+WD = "float16"
+HX = 768
+NS = 4
+TW = [128, 128, 192, 256, 320, 384]
+TO = [sum(TW[:k]) for k in range(6)]
+MWD = sum(TW)
+ZC = [(0, 8), (8, 20), (20, 34), (34, 48)]
+
+
+def _sb(n, d):
+    return ("sbuf", [128, n], d)
+
+
+BF, F32, U16, I32, QX, U8 = "bfloat16", "float32", "uint16", "int32", "float8_e4m3fn_x4", "uint8"
+SCRATCH = {
+    "X": _sb(4 * C, BF), "Xh": _sb(4 * C, BF), "qx": _sb(C, QX), "sx": _sb(C, U8),
+    "ut": _sb(512, BF), "vt": _sb(512, BF), "qu": _sb(128, QX), "su": _sb(128, U8),
+    "qr": _sb(128, QX), "sr": _sb(128, U8), "qv": _sb(128, QX), "sv": _sb(128, U8),
+    "qw": _sb(512, QX), "sw": _sb(512, U8),
+    "one": _sb(512, BF), "cb": _sb(512, BF), "qb": _sb(128, QX), "sb": _sb(128, U8),
+    "ce": _sb(2048, BF), "qe": _sb(512, QX), "se": _sb(512, U8), "zt": _sb(512, BF),
+    "kmin": _sb(C, F32), "d0": _sb(C, F32), "mk": _sb(C, F32), "hold": _sb(C, F32),
+    "dm": _sb(C, BF), "ds": _sb(C, WD), "M": _sb(4 * MWD, BF), "qm": _sb(MWD, QX), "sm": _sb(MWD, U8),
+    "tmpS": _sb(6 * C, BF), "rs": _sb(24, F32), "junk": _sb(2 * C, BF), "jr": _sb(16 * 12 * 23, BF),
+    "Hg": _sb(4 * C, BF),
+    "c16": _sb(3 * C, BF), "c4": _sb(C, BF), "wr": _sb(3 * C, WD), "wr4": _sb(C, WD), "wrc": _sb(C, WD),
+    "ci": _sb(16, I32), "cf": _sb(32, F32), "x16": _sb(16, F32), "k16": _sb(16, F32), "p16": _sb(16, F32),
+    "p4": _sb(8, F32), "t16": _sb(16, F32), "i16": _sb(24, F32), "rp": _sb(24, F32), "al32": _sb(32, F32),
+    "oRep": _sb(8, U16), "oQ": _sb(24, U16), "oQ4": _sb(24, U16), "oHalf": _sb(2, U16),
+    "oK": _sb(24, U16), "oP": _sb(24, U16), "oPos": _sb(24, U16), "oPos4": _sb(96, U16), "oAB4": _sb(96, U16),
+    "oPP": _sb(24, U16), "oL": _sb(24, U16), "oL4": _sb(16, U16), "oL16": _sb(4, U16), "oC4": _sb(16, U16),
+    "oC16": _sb(4, U16), "oM": _sb(2, U16),
+    "base": _sb(24, F32), "kk": _sb(24, F32), "sm1": _sb(24, F32),
+    "cnt": _sb(2, F32), "tn": _sb(16, F32),
+    "rep": _sb(32, F32), "rpt": _sb(32, F32), "dat": _sb(32, BF), "tpl": _sb(1200, BF), "MW": _sb(1200, BF),
+    "Wt": _sb(6 * C, BF), "Pt": _sb(6 * C, BF), "half": _sb(C, BF), "iotaC": _sb(C, BF),
+    "plrow": _sb(C, BF), "porow": _sb(C, BF), "PT": _sb(C, BF), "AB": _sb(C, BF),
+    "ABh": _sb(4 * C, BF), "Z": _sb(2 * C, BF), "qz": _sb(192, QX), "sz": _sb(192, U8),
+    "Hpm": _sb(4 * C, BF), "qh": _sb(192, QX), "sh": _sb(192, U8),
+    "WL": _sb(C, BF), "gain": _sb(C, BF), "cat": _sb(3 * C, BF), "LW": _sb(C, BF), "crow": _sb(L, BF),
+    "sab": _sb(4 * L, BF), "ST": _sb(512, BF), "qs": _sb(256, QX), "ss": _sb(256, U8),
+    "pp": _sb(C, BF), "sp": _sb(L, BF), "Dt": _sb(4 * L, BF), "yo": _sb(C, F32),
+}
+for _t in range(R):
+    SCRATCH["ql%d" % _t] = _sb(192, QX)
+    SCRATCH["sl%d" % _t] = _sb(384, U8)
+    SCRATCH["lp%d" % _t] = _sb(L, BF)
+for _b in range(8):
+    SCRATCH["P%d" % _b] = ("psum", [128, 512], F32)
+
+NDMA = 24
+SEMAPHORES = (["nv", "na", "np_", "ng", "ls", "gw", "go", "ga", "gb"] + ["d%d" % k for k in range(NDMA)]
+              + ["arc%d" % t for t in range(R)] + ["arp%d" % t for t in range(R)])
+NAMES = ("cQ cQM cO cOC cH cHM cQ4 cO4 cFL cR1 cR2 cK cTH cTL cNF cMID cBE cTHE cGJ cJ cEP "
+         "cB1 cX1 cT1 cT2 cT3 cM1 cM2 cQ5 cN1 cN2 cJ2").split()
+
+
+def rank_program(g, core, T, topo):
+    rank = T.rank_of(core)
+    if rank is None:
+        return
+    n = len(T.cores)
+    nxt, prv = T.cores[(rank + 1) % n], T.cores[(rank - 1) % n]
+    V, S, P = g.vector, g.scalar, g.tensor
+    Q = {"v": V, "a": S, "p": P, "g": g, "s": g.sync}
+    CS = {"v": "nv", "a": "na", "p": "np_", "g": "ng"}
+    total, lastw, readers = {}, {}, {}
+    waited = {q: {} for q in Q}
+    ndma = [0]
+
+    def wait(q, tok):
+        if waited[q].get(tok[0], 0) < tok[1]:
+            Q[q].wait_ge(T.sem[tok[0]], tok[1])
+            waited[q][tok[0]] = tok[1]
+
+    def deps(q, reads, writes):
+        need = {}
+        toks = []
+        for k in reads:
+            toks.append(lastw.get(k))
+            if k[0] == "P" and k[1:].isdigit():
+                toks += [t for t in readers.get(k, []) if t[0] != CS.get(q)]
+        for k in writes:
+            if not (q == "p" and lastw.get(k) and lastw[k][0] == "np_"):
+                toks.append(lastw.get(k))
+            toks += readers.get(k, [])
+        for t in toks:
+            if t is not None:
+                need[t[0]] = max(need.get(t[0], 0), t[1])
+        for s in need:
+            wait(q, (s, need[s]))
+
+    def note(tok, reads, writes):
+        for k in reads:
+            readers.setdefault(k, []).append(tok)
+        for k in writes:
+            lastw[k] = tok
+            readers[k] = []
+
+    def op(q, reads, writes, fn):
+        reads, writes = reads.split(), writes.split()
+        deps(q, reads, writes)
+        s = CS[q]
+        total[s] = total.get(s, 0) + 1
+        fn().then_inc(T.sem[s], 1)
+        note((s, total[s]), reads, writes)
+
+    def dma(q, reads, writes, out, in_, sem=None, **kw):
+        reads, writes = reads.split(), writes.split()
+        deps(q, reads, writes)
+        if sem is None:
+            sem = "d%d" % ndma[0]
+            ndma[0] += 1
+        total[sem] = total.get(sem, 0) + 16
+        Q[q].dma_start(out, in_, **kw).then_inc(T.sem[sem], 16)
+        note((sem, total[sem]), reads, writes)
+
+    def ts(r, w, out, in0, s1, o0, s2=None, o1=None):
+        if s2 is None:
+            op("v", r, w, lambda: V.tensor_scalar(out, in0, s1, None, o0))
+        else:
+            op("v", r, w, lambda: V.tensor_scalar(out, in0, s1, s2, o0, o1))
+
+    def tt(r, w, out, in0, in1, o):
+        op("v", r, w, lambda: V.tensor_tensor(out, in0, in1, o))
+
+    def cp(r, w, out, in_):
+        op("v", r, w, lambda: V.tensor_copy(out, in_))
+
+    def scan(r, w, out, d0, d1, init, o0, o1):
+        op("v", r, w, lambda: V.tensor_tensor_scan(out, d0, d1, init, o0, o1))
+
+    def mset(w, ap, val):
+        op("v", "", w, lambda: V.memset(ap, val))
+
+    def quant(r, w, q, s, in_):
+        op("v", r, w, lambda: V.quantize_mx(q, s, in_))
+
+    def act(r, w, out, in_, f, **kw):
+        op("a", r, w, lambda: S.activation(out, in_, f, **kw))
+
+    def mm(r, w, out, lq, ls_, rq, rs_, start=True, stop=True):
+        op("p", r, w, lambda: P.matmul_mx(out, lq, ls_, rq, rs_, start, stop))
+
+    def iota(w, out, pat, base, cm, fl=True):
+        if fl:
+            op("g", "", w, lambda: g.iota(out, pat, base, cm, allow_small_or_imprecise_dtypes=True))
+        else:
+            op("g", "", w, lambda: g.iota(out, pat, base, cm))
+
+    def col(name):
+        k = NAMES.index(name)
+        return T.cf[:, k:k + 1]
+
+    def lin(w, a, scale=1.0, bias=0.0):
+        rd = " ".join(k for k in (a, scale, bias) if isinstance(k, str))
+        act(rd, w, col(w), col(a), F.Identity, scale=col(scale) if isinstance(scale, str) else scale,
+            bias=col(bias) if isinstance(bias, str) else bias)
+
+    def wrap16(r, w, out, src, m, buf="wr"):
+        scan(r + (" c16 c16b" if m > C else " c16"), buf, T[buf][:, 0:m], src, T.c16[:, 0:m], -2048.0, A.max, A.add)
+        if out is not None:
+            ts(buf + " cOC", w, out, T[buf][:, 15:m:16], col("cOC"), A.subtract)
+
+    def wrap4(r, w, out, src, m):
+        scan(r + " c4", "wr4", T.wr4[:, 0:m], src, T.c4[:, 0:m], -2048.0, A.max, A.add)
+        ts("wr4 cO4", w, out, T.wr4[:, 3:m:4], 4.0, A.mult, col("cO4"), A.add)
+
+    def mrow(i, m):
+        k, e = (i - 1) // 4, (i - 1) % 4
+        return T.M[:, 4 * TO[k] + e:4 * (TO[k] + m):4]
+
+    def qtile(k):
+        a, b = TO[k], TO[k] + TW[k]
+        rd = " ".join("m%d" % i for i in range(4 * k + 1, 4 * k + 5)) + " mz"
+        quant(rd, "qm%d" % k, T.qm[:, a:b], T.sm[:, a:b], T.M[:, 4 * a:4 * b])
+        mm("qb qm%d" % k, "P2", T.P2[:, 0:TW[k]], T.qb[:], T.sb[:], T.qm[:, a:b], T.sm[:, a:b], k == 5, k == 0)
+
+    dma("a", "", "ut", T.ut[:], T.u[:])
+    dma("s", "", "X", T.X[:], T.x[:])
+    iota("ci0", T.ci[:, 0:1], [[0, 1]], 0, 1, False)
+    iota("ci8", T.ci[:, 8:16], [[16, 8]], 0, 0, False)
+    iota("x16", T.x16[:], [[1, 16]], 0, 0)
+    mset("one", T.one[:], 1.0)
+    mset("zt", T.zt[:], 0.0)
+    op("g", "one", "cb", lambda: g.affine_select(T.cb[:], T.one[:], [[-16, 8], [0, 64]], A.is_ge, 0.0, 0, 1))
+    op("g", "cb", "cb", lambda: g.affine_select(T.cb[:], T.cb[:], [[16, 8], [0, 64]], A.is_ge, 0.0, 15, -1))
+    iota("dm", T.dm[:], [[16, 24], [-512, 16]], 0, 0)
+    dma("g", "", "", T.qw[:].bitcast(dt.uint8), T.wc[:], "gw")
+    dma("g", "", "qw", T.sw[:], T.ws[:], "gw")
+    iota("i16", T.i16[:], [[16, 24]], 0, 0)
+    iota("Wt", T.Wt[:, 0:4 * C], [[0, 4 * C]], 0, 0)
+    iota("iotaC", T.iotaC[:], [[1, C]], -192, 0)
+    iota("tpl3", T.tpl[:, 800:1200], [[0, 400]], 512, 0)
+    for b in range(4):
+        op("g", "one", "ce%d" % b, lambda: g.affine_select(
+            T.ce[:, 512 * b:512 * b + 512], T.one[:], [[-1, 512]], A.is_equal, 0.0, b, 4))
+    dma("s", "zt", "", T.M[:, 0:512], T.zt[:], "d23")
+    for k in range(1, 5):
+        e = 4 * (TO[k] + TW[k])
+        dma("s", "zt", "", T.M[:, e - 192:e], T.zt[:, 0:192], "d23")
+    dma("s", "zt", "mz STz", T.ST[:, 256:512], T.zt[:, 0:256], "d23")
+
+    ts("ci0", "ci1", T.ci[:, 1:2], T.ci[:, 0:1], 15, A.bitwise_and)
+    ts("ci0", "ci2", T.ci[:, 2:3], T.ci[:, 0:1], 3, A.bitwise_and)
+    ts("ci0", "ci3", T.ci[:, 3:4], T.ci[:, 0:1], 31, A.bitwise_and)
+    cp("ci8", "oRep", T.oRep[:], T.ci[:, 8:16])
+    cp("ci1", "cQ", col("cQ"), T.ci[:, 1:2])
+    cp("ci2", "cQ4", col("cQ4"), T.ci[:, 2:3])
+    cp("ci3", "oHalf", T.oHalf[:, 0:1], T.ci[:, 3:4])
+    ts("one cQ", "oQ", T.oQ[:], T.one[:, 0:24], col("cQ"), A.mult)
+    ts("x16 cQ", "k16", T.k16[:], T.x16[:], col("cQ"), A.is_equal)
+    ts("one cQ4", "oQ4", T.oQ4[:], T.one[:, 0:24], col("cQ4"), A.mult)
+    act("k16 oQ", "kmin", T.kmin[:], T.k16[:].indirect(T.oQ[:]), F.Identity, scale=2 * BIG, bias=-BIG)
+    ts("k16", "p16", T.p16[:], T.k16[:], 1024.0, A.mult)
+    ts("k16", "t16a", T.t16[:, 0:15], T.k16[:, 1:16], -2048.0, A.mult)
+    ts("k16", "t16b", T.t16[:, 15:16], T.k16[:, 0:1], -2048.0, A.mult)
+    ts("cQ", "cT1", col("cT1"), col("cQ"), 0.0, A.is_gt)
+    tt("p16 t16a t16b", "p16", T.p16[:], T.p16[:], T.t16[:], A.add)
+    ts("cQ", "cR1", col("cR1"), col("cQ"), 4.5, A.is_gt)
+    ts("cQ", "cR2", col("cR2"), col("cQ"), 10.5, A.is_gt)
+    ts("cQ cT1", "cFL", col("cFL"), col("cQ"), 3.5, A.is_lt, col("cT1"), A.mult)
+    mset("m21 m22 m23 m24", T.M[:, 4 * TO[5]:4 * MWD], 0.0)
+    mset("d0", T.d0[:], BIG)
+    mset("rs0", T.rs[:, 0:1], 0.0)
+    mset("d0", T.d0[:, 0:C:16], -BIG)
+    act("p16 oQ", "c16", T.c16[:, 0:C], T.p16[:].indirect(T.oQ[:]), F.Copy)
+    quant("ut", "qu", T.qu[:], T.su[:], T.ut[:])
+    cp("qu oRep", "qr", T.qr[:].bitcast(dt.uint32), T.qu[:].bitcast(dt.uint32).indirect(T.oRep[:]))
+    dma("s", "c16", "", T.c16[:, C:2 * C], T.c16[:, 0:C], "d22")
+    dma("s", "c16", "c16b", T.c16[:, 2 * C:3 * C], T.c16[:, 0:C], "d22")
+    dma("s", "", "vt", T.vt[:], T.v[:])
+    lin("cO", "cT1", 2048.0, -1024.0)
+    lin("cT2", "cR1", -5.0, "cQ")
+    lin("cH", "cQ", -1.0, 15.0)
+    lin("cK", "cR2", -6.0, "cT2")
+    lin("cOC", "cO", 1.0, -192.0)
+    lin("cB1", "cO", 383.0, "cH")
+    lin("cTH", "cK", -1.0, 0.5)
+    lin("cTL", "cK", -1.0, -0.5)
+    act("qu oRep", "sr", T.sr[:], T.su[:].indirect(T.oRep[:]), F.Copy)
+    lin("cMID", "cR2", -1.0, "cR1")
+    lin("cTHE", "cR2", -1.0, 1.0)
+    lin("cJ", "cQ", 1.0, 784.0)
+    lin("cN1", "cR1", -1.0, 1.0)
+    lin("cN2", "cR1", 1.0, -1.0)
+    lin("cJ2", "cQ", 1.0, 1184.0)
+    lin("cHM", "cR2", -95.5)
+    lin("cM2", "cR1", -16777216.0)
+    lin("cM1", "cR1", 16777216.0, 0.5)
+    lin("cBE", "cMID", 0.5)
+    lin("cEP", "cMID", 96.5, "cHM")
+    lin("cQM", "cJ", -1.0, 800.0)
+    lin("cEP", "cN1", 193.0, "cEP")
+    lin("cNF", "cMID", -0.25)
+    lin("cGJ", "cR1", -400.0, "cQM")
+    act("one cNF", "al32", T.al32[:], T.one[:, 0:32], F.Identity, scale=col("cNF"))
+    quant("zt", "qs2", T.qs[:, 128:256], T.ss[:, 128:256], T.zt[:])
+    quant("zt", "zl0", T.ql0[:, 0:128], T.sl0[:, 0:128], T.zt[:])
+    mset("half", T.half[:], 0.5)
+    mset("tpl", T.tpl[:, 0:400], 1.0)
+    quant("cb", "qb", T.qb[:], T.sb[:], T.cb[:])
+
+    def latest_constants():
+        lin("cT2", "cQ4", -1.0, "cQ")
+        lin("cX1", "cO", -513.0, 191.0 - 512.0)
+        lin("cT3", "cO", -1.0, "cH")
+        lin("cT2", "cT2", -0.25)
+        lin("cQ5", "cQ4", 1.0, 4096.0 + 768.0)
+        lin("cT3", "cT3", 1.0, 368.0)
+        act("x16 cT2", "t16a", T.t16[:, 0:4], T.x16[:, 0:4], F.Abs, bias=col("cT2"))
+        act("cT2", "cT1", col("cT1"), col("cT2"), F.Sign)
+        act("i16 cT3", "rp", T.rp[:], T.i16[:], F.Identity, scale=-1.0, bias=col("cT3"))
+        act("t16a", "t16a", T.t16[:, 0:4], T.t16[:, 0:4], F.Relu, scale=-1024.0, bias=1024.0)
+        lin("cO4", "cT1", 8192.0, "cQ5")
+        for k in range(4):
+            act("t16a", "p4%d" % k, T.p4[:, k:k + 1], T.t16[:, (k + 1) % 4:(k + 1) % 4 + 1], F.Identity, scale=-2.0,
+                bias=T.t16[:, k:k + 1])
+
+    eng = topo.engines(core, nxt)
+    ne, ne_in = len(eng), len(topo.engines(prv, core))
+    lo_mask = sum(1 << e for e in eng[:ne // 2])
+    hi_mask = sum(1 << e for e in eng[ne // 2:])
+    rid, pid = topo.addr(nxt)[0], topo.addr(nxt)[1]
+    HH = "H0 H1 H2 H3"
+
+    for t in range(R):
+        top = 3 + t
+        tw = (top + 1) * C
+        quant("X", "qx", T.qx[:], T.sx[:], T.X[:])
+        mm("qr sr qx", "P0", T.P0[:, 0:C], T.qr[:], T.sr[:], T.qx[:], T.sx[:])
+        mm("qr sr qx", "P1", T.P1[:, 0:C], T.qr[:], T.sr[:], T.qx[:], T.sx[:])
+        if t == 0:
+            mm("qu qx", "P3", T.P3[:, 0:C], T.qu[:], T.su[:], T.qx[:], T.sx[:])
+            mset("tpl2", T.tpl[:, 400:800], 0.5)
+            mset("dat0", T.dat[:, 16:32], 0.0)
+        else:
+            cp("lp%d oC16 pp" % (t - 1), "pp", T.pp[:].indirect(T.oC16[:]), T["lp%d" % (t - 1)][:])
+        e = 16 * (24 - NS)
+        for a, b, h in ((e, C, "hi"), (0, e, "lo")):
+            tt("P0 kmin", "mk" + h, T.mk[:, a:b], T.P0[:, a:b], T.kmin[:, a:b], A.min)
+            scan("d0 mk" + h, h, T.hold[:, a:b], T.d0[:, a:b], T.mk[:, a:b], -BIG, A.min, A.max)
+
+        def pass1(k):
+            i = 23 - k
+            act("P1 hi", "tmp%d" % k, T.tmpS[:, C * k:C * k + 16 * i], T.P1[:, 0:16 * i], F.Sign,
+                scale=-1.0, bias=T.hold[:, 16 * i + 15:16 * i + 16])
+
+        def pass2(k):
+            i = 23 - k
+            act("tmp%d mz" % k, "m%d rs%d" % (i, i), mrow(i, 16 * i), T.tmpS[:, C * k:C * k + 16 * i], F.Relu,
+                accum_out=T.rs[:, i:i + 1])
+        if t == 0:
+            a = TO[5]
+            for k in range(NS):
+                pass1(k)
+            ts("P3 cFL", "m24", mrow(24, C), T.P3[:, 0:C], 0.0, A.is_gt, col("cFL"), A.mult)
+            quant("m21 m22 m23 m24", "qm5", T.qm[:, a:MWD], T.sm[:, a:MWD], T.M[:, 4 * a:4 * MWD])
+            mm("qb qm5", "P4", T.P4[:, 0:C], T.qb[:], T.sb[:], T.qm[:, a:MWD], T.sm[:, a:MWD])
+            for k in range(NS):
+                pass2(k)
+            act("P4", "pp", T.pp[:], T.P4[:, 0:C], F.Copy)
+        else:
+            pass1(0)
+            for k in range(NS):
+                if k + 1 < NS:
+                    pass1(k + 1)
+                pass2(k)
+        tt("P0 hi lo", "m24", mrow(24, C), T.hold[:], T.P0[:, 0:C], A.is_ge)
+        if t == 0:
+            dma("s", "tpl tpl2 tpl3", "MW", T.MW[:], T.tpl[:])
+        for i in range(23 - NS, 0, -1):
+            ts("P0 lo mz", "m%d" % i, mrow(i, 16 * i), T.P0[:, 0:16 * i], T.hold[:, 16 * i + 15:16 * i + 16], A.is_lt)
+            act("m%d" % i, "rs%d jr%d" % (i, i), T.jr[:, 8 * i * (i - 1):8 * i * (i + 1)], mrow(i, 16 * i), F.Copy,
+                accum_out=T.rs[:, i:i + 1])
+            if i == 17:
+                scan("m24 dm", "ds", T.ds[:], T.dm[:], mrow(24, C), 0.0, A.max, A.subtract)
+            if i == 13:
+                qtile(5)
+                qtile(4)
+            if i == 11:
+                qtile(3)
+            if i % 4 == 1 and i <= 9:
+                qtile((i - 1) // 4)
+            if i == 2:
+                wrap16("pp", "", None, T.pp[:], C, "wrc")
+        ts("wrc cB1", "base", T.base[:], T.wrc[:, 15:C:16], -384.0, A.mult, col("cB1"), A.add)
+        tt("base ds", "base", T.base[:], T.base[:], T.ds[:, 15:C:16], A.add)
+        rd = " ".join("rs%d" % i for i in range(24))
+        tt("base " + rd, "base", T.base[:], T.base[:], T.rs[:], A.subtract)
+        wrap16("P2", "", None, T.P2[:, 0:C], C)
+        tt("wr base", "kk", T.kk[:], T.wr[:, 15:C:16], T.base[:], A.add)
+        ts("kk", "oK", T.oK[:], T.kk[:], float(C * top), A.add)
+        tn = lambda k: T.tn[:, k:k + 1]
+        act("pp cTH", "junk0 cnt0", T.junk[:, 0:C], T.pp[:], F.Sign, bias=col("cTH"), accum_out=T.cnt[:, 0:1])
+        act("pp cTL", "junk1 cnt1", T.junk[:, C:], T.pp[:], F.Sign, bias=col("cTL"), accum_out=T.cnt[:, 1:2])
+        act("cnt0 cnt1", "tn0", T.tn[:, 0:2], T.cnt[:], F.Identity, scale=0.5, bias=191.5)
+        act("tn0 cM1", "tn2", T.tn[:, 2:4], T.tn[:, 0:2], F.Identity, bias=col("cM1"))
+        act("tn2 cM2", "tn4", T.tn[:, 4:6], T.tn[:, 2:4], F.Identity, bias=col("cM2"))
+        act("tn4", "tn6", tn(6), tn(5), F.Identity, scale=-1.0, bias=tn(4))
+        act("tn4 cTHE", "tn7", tn(7), tn(5), F.Sign, bias=col("cTHE"))
+        act("tn6 tn4 cBE", "tn8", tn(8), tn(6), F.Identity, scale=col("cBE"), bias=tn(5))
+        act("tn6 tn7", "tn9", tn(9), tn(6), F.Sign, scale=tn(7))
+        act("tn4 cN2 cEP", "tn12", tn(12), tn(5), F.Identity, scale=col("cN2"), bias=col("cEP"))
+        act("tn4 cJ2", "tn13", tn(13), tn(5), F.Identity, scale=-1.0, bias=col("cJ2"))
+        act("tn9 cN2", "tn14", tn(14), tn(9), F.Identity, scale=col("cN2"))
+        act("al32 tn6 tn12", "rep", T.rep[:], T.al32[:], F.Identity, scale=tn(6), bias=tn(12))
+        act("tn13 tn14 cJ2", "tn11", tn(11), tn(13), F.Identity, scale=tn(14), bias=col("cJ2"))
+        act("tn8 cGJ", "tn8", tn(8), tn(8), F.Identity, bias=col("cGJ"))
+        act("tn8 tn9 cJ", "tn10", tn(10), tn(8), F.Identity, scale=tn(9), bias=col("cJ"))
+        if t == 0:
+            latest_constants()
+        cp("oK half Wt", "Wt", T.Wt[:, 0:tw].indirect(T.oK[:]), T.half[:])
+        scan("Wt", "Pt", T.Pt[:, 0:tw], T.Wt[:, 0:tw], T.Wt[:, 0:tw], -193.0, A.add, A.add)
+        act("Pt oK", "plrow", T.plrow[:], T.Pt[:, 0:tw].indirect(T.oK[:]), F.Copy)
+        if t == 0:
+            act("p40 p41 p42 p43 oQ4", "c4", T.c4[:], T.p4[:, 0:4].indirect(T.oQ4[:]), F.Copy)
+        op("v", "rep", "rpt", lambda: V.transpose(T.rpt[:], T.rep[:]))
+        cp("tn10 tn11", "oM", T.oM[:], T.tn[:, 10:12])
+        cp("rpt oHalf", "dat", T.dat[:, 0:16], T.rpt[:].indirect(T.oHalf[:, 0:1]))
+        cp("dat dat0 oM MW", "MW", T.MW[:].indirect(T.oM[:]), T.dat[:])
+        scan("MW", "PT", T.PT[:], T.MW[:, 400:784], T.MW[:, 400:784], -193.0, A.add, A.add)
+        wrap16("plrow", "oP", T.oP[:], T.plrow[:], C)
+        act("PT oP", "porow", T.porow[:, 0:192], T.PT[:].indirect(T.oP[:, 0:12]), F.Copy)
+        cp("PT oP", "porow2", T.porow[:, 192:C], T.PT[:].indirect(T.oP[:, 12:24]))
+        act("X", "Xh", T.Xh[:], T.X[:], F.Identity, scale=0.5)
+        wrap16("porow porow2", "oPos", T.oPos[:], T.porow[:], C)
+        cp("oPos iotaC", "AB", T.AB[:].indirect(T.oPos[:]), T.iotaC[:])
+        wrap4("AB", "oAB4", T.oAB4[:], T.AB[:], C)
+        for k, (a, b) in enumerate(ZC):
+            act("Xh oAB4", "Bh%d" % k, T.ABh[:, 768 + 16 * a:768 + 16 * b],
+                T.Xh[:].indirect(T.oAB4[:, 48 + a:48 + b]), F.Copy)
+        for k, (a, b) in enumerate(ZC):
+            tt("Xh oAB4 Bh%d" % k, "Z%d" % k, T.Z[:, 16 * a:16 * b],
+               T.Xh[:].indirect(T.oAB4[:, a:b]), T.ABh[:, 768 + 16 * a:768 + 16 * b], A.add)
+        act("Xh oAB4", "Ah0", T.ABh[:, 0:384], T.Xh[:].indirect(T.oAB4[:, 0:24]), F.Copy)
+        quant("Z0 Z1 Z2 Z3", "qz", T.qz[:], T.sz[:], T.Z[:])
+        for b in range(4):
+            mm("qw qz", "P%d" % (4 + b), T["P%d" % (4 + b)][:, 0:192], T.qw[:, 128 * b:128 * b + 128],
+               T.sw[:, 128 * b:128 * b + 128], T.qz[:], T.sz[:])
+        wrap4("porow porow2", "oPos4", T.oPos4[:], T.porow[:], C)
+        for b in range(4):
+            pb = "P%d" % (4 + b)
+            if b % 2 == 0:
+                act(pb, "H%d" % b, T.Hpm[:, b:768:4], T[pb][:, 0:192], F.Identity, scale=0.03125)
+            else:
+                ts(pb, "H%d" % b, T.Hpm[:, b:768:4], T[pb][:, 0:192], 0.03125, A.mult)
+        quant(HH, "qh", T.qh[:], T.sh[:], T.Hpm[:, 0:768])
+        mm("qr sr qh", "P3", T.P3[:, 0:192], T.qr[:], T.sr[:], T.qh[:], T.sh[:])
+        act(HH, "Hm", T.Hpm[:, 768:1536], T.Hpm[:, 0:768], F.Identity, scale=-1.0)
+        wrap16("PT", "oPP", T.oPP[:], T.PT[:], C, "wrc")
+        ts("P3", "WL0", T.WL[:, 0:192], T.P3[:, 0:192], 0.0, A.is_gt)
+        ts("P3", "WL1", T.WL[:, 192:C], T.P3[:, 0:192], 0.0, A.is_le)
+        cp("WL0 WL1 oPP", "win", T.cat[:, 2 * C:2 * C + 192], T.WL[:].indirect(T.oPP[:, 0:12]))
+        act("WL0 WL1 oPP", "win2", T.cat[:, 2 * C + 192:3 * C], T.WL[:].indirect(T.oPP[:, 12:24]), F.Copy)
+        act(HH + " Hm oPos4", "Hg", T.Hg[:, 0:HX], T.Hpm[:].indirect(T.oPos4[:, 0:HX // 16]), F.Copy)
+        dma("g", "Hg Xh qx", "Xa", T.X[:, 0:HX], T.Hg[:, 0:HX], "ga", accum_op=A.add)
+        act("WL0 WL1 oPos", "gain", T.gain[:], T.WL[:].indirect(T.oPos[:]), F.Copy)
+        dma("g", "gain pp", "pp", T.pp[:], T.gain[:], "gb", accum_op=A.add)
+        act("Xh oAB4", "Ah1", T.ABh[:, 384:768], T.Xh[:].indirect(T.oAB4[:, 24:48]), F.Copy)
+        scan("MW win win2", "om", T.cat[:, 2 * C - 1:C - 1:-1], T.MW[:, C:0:-1], T.cat[:, 3 * C - 1:2 * C - 1:-1],
+             0.0, A.mult, A.subtract)
+        scan("MW win win2", "la", T.cat[:, 0:C], T.MW[:, 800:800 + C], T.cat[:, 2 * C:3 * C], 193.0, A.min, A.subtract)
+        wrap16("win win2 om la", "", None, T.cat[:], 3 * C)
+        ts("wr cX1", "sm1", T.sm1[:], T.wr[:, 2 * C + 15:3 * C:16], 512.0, A.mult, col("cX1"), A.add)
+        tt("rp wr", "kk", T.kk[:], T.wr[:, C + 15:2 * C:16], T.rp[:], A.add)
+        tt("wr sm1", "sm1", T.sm1[:], T.sm1[:], T.wr[:, 15:C:16], A.add)
+        tt("kk sm1", "sm1", T.sm1[:], T.sm1[:], T.kk[:], A.max)
+        cp("sm1", "oL", T.oL[:], T.sm1[:])
+        cp("oL PT", "LW", T.LW[:].indirect(T.oL[:]), T.PT[:])
+        wrap4("LW", "oL4", T.oL4[:], T.LW[:, 0:L], L)
+        for k in range(2):
+            act("Ah0 Ah1 Bh0 Bh1 Bh2 Bh3 oL4", "sab%d" % k, T.sab[:, 128 * k:128 * k + 128],
+                T.ABh[:].indirect(T.oL4[:, 8 * k:8 * k + 8]), F.Identity, scale=2.0)
+        wrap16("LW", "oL16", T.oL16[:], T.LW[:, 0:L], L)
+        act("AB oL16", "crow", T.crow[:], T.AB[:].indirect(T.oL16[:]), F.Copy)
+        for k in range(2):
+            tt(HH + " Hm oL4 sab%d" % k, "ST%d" % k, T.ST[:, 128 * k:128 * k + 128],
+               T.Hpm[:].indirect(T.oL4[:, 8 * k:8 * k + 8]), T.sab[:, 128 * k:128 * k + 128], A.add)
+        quant("ST0 ST1 STz", "qs", T.qs[:, 0:128], T.ss[:, 0:128], T.ST[:])
+        deps("g", ["qs", "qs2"], [])
+        g.remote_dma_fused([
+            RemoteDMATransfer(dst_ids=[DstId(rid=rid, pnc=pid)], dma_engine_mask=lo_mask, remote_sem=T.sem["arc%d" % t],
+                              src=T.qs[:, 0:L].bitcast(dt.uint8), dst=T["ql%d" % t][:, 128:192].bitcast(dt.uint8)),
+            RemoteDMATransfer(dst_ids=[DstId(rid=rid, pnc=pid)], dma_engine_mask=hi_mask, remote_sem=T.sem["arc%d" % t],
+                              src=T.ss[:], dst=T["sl%d" % t][:, 128:384]),
+        ], local_sem=T.sem.ls)
+        total["ls"] = total.get("ls", 0) + 2 * ne
+        note(("ls", total["ls"]), ["qs"], [])
+        lastw["land%d" % t] = ("arc%d" % t, ne_in)
+        lastw["lp%d" % t] = ("arp%d" % t, ne_in)
+        total["arc%d" % t] = total["arp%d" % t] = ne_in
+        wrap16("crow", "oC16", T.oC16[:], T.crow[:], L)
+        act("pp oC16", "sp", T.sp[:], T.pp[:].indirect(T.oC16[:]), F.Copy)
+        deps("g", ["sp"], [])
+        g.remote_dma(T["lp%d" % t][:], T.sp[:], T.sem["arp%d" % t], T.sem.ls, pid, rid, lo_mask | hi_mask)
+        note(("ls", total["ls"]), ["sp"], [])
+        wrap4("crow", "oC4", T.oC4[:], T.crow[:], L)
+        tt(HH + " Hm oPos4 X", "X", T.X[:, HX:], T.Hpm[:].indirect(T.oPos4[:, HX // 16:]), T.X[:, HX:], A.add)
+        if t == 0:
+            quant("ce0 ce1 ce2 ce3", "qe", T.qe[:], T.se[:], T.ce[:])
+        if t == 1:
+            quant("vt", "qv", T.qv[:], T.sv[:], T.vt[:])
+        if t + 1 < R:
+            z = "%d" % (t + 1)
+            quant("zt", "zl" + z, T["ql" + z][:, 0:128], T["sl" + z][:, 0:128], T.zt[:])
+            iota("Wt", T.Wt[:, 0:tw + C], [[0, tw + C]], 0, 0)
+            dma("s", "tpl tpl2 tpl3", "MW", T.MW[:], T.tpl[:])
+        ql, sl = T["ql%d" % t], T["sl%d" % t]
+        for b in range(4):
+            pb = "P%d" % (4 + b)
+            mm("qe zl%d land%d" % (t, t), pb, T[pb][:, 0:128], T.qe[:, 128 * b:128 * b + 128],
+               T.se[:, 128 * b:128 * b + 128], ql[:, 64:192], sl[:, 64:192])
+        for b in range(4):
+            pb = "P%d" % (4 + b)
+            if b % 2 == 0:
+                act(pb, "D%d" % b, T.Dt[:, b:256:4], T[pb][:, 64:128], F.Copy)
+            else:
+                cp(pb, "D%d" % b, T.Dt[:, b:256:4], T[pb][:, 64:128])
+        cp("D0 D1 D2 D3 oC4 X Xa", "X", T.X[:].indirect(T.oC4[:]), T.Dt[:])
+
+    quant("X", "qx", T.qx[:], T.sx[:], T.X[:])
+    dma("s", "qx", "", T.oc[:], T.qx[:].bitcast(dt.uint8))
+    h = C // 2
+    mm("qv qx", "P0", T.P0[:, 0:h], T.qv[:], T.sv[:], T.qx[:, 0:h], T.sx[:, 0:h])
+    mm("qv qx", "P1", T.P1[:, 0:h], T.qv[:], T.sv[:], T.qx[:, h:C], T.sx[:, h:C])
+    cp("lp%d oC16 pp" % (R - 1), "pp", T.pp[:].indirect(T.oC16[:]), T["lp%d" % (R - 1)][:])
+    act("P0", "y0", T.yo[:, 0:h], T.P0[:, 0:h], F.Copy)
+    cp("P1", "y1", T.yo[:, h:C], T.P1[:, 0:h])
+    dma("a", "y0", "", T.y[:, 0:h], T.yo[:, 0:h])
+    dma("g", "pp", "", T.pts[:], T.pp[0:128:16, :], "go")
+    for k in range(4):
+        dma("s", "qx", "", T.osc[4 * k:4 * k + 4, :], T.sx[32 * k:32 * k + 4, :])
+    dma("a", "y1", "", T.y[:, h:C], T.yo[:, h:C])
+    for s in total:
+        wait("g", (s, total[s]))

@@ -7,11 +7,12 @@ C, L, R = 384, 64, 3
 BIG = 1e29
 WD = "float16"
 HX = 768
+LA = 256
 NS = 4
 TW = [128, 128, 192, 256, 320, 384]
 TO = [sum(TW[:k]) for k in range(6)]
 MWD = sum(TW)
-ZC = [(0, 8), (8, 20), (20, 34), (34, 48)]
+ZC = [(0, 8), (8, 24), (24, 40), (40, 48)]
 
 
 def _sb(n, d):
@@ -26,12 +27,13 @@ SCRATCH = {
     "qw": _sb(512, QX), "sw": _sb(512, U8),
     "one": _sb(512, BF), "cb": _sb(512, BF), "qb": _sb(128, QX), "sb": _sb(128, U8),
     "ce": _sb(2048, BF), "qe": _sb(512, QX), "se": _sb(512, U8), "zt": _sb(512, BF),
-    "kmin": _sb(C, F32), "d0": _sb(C, F32), "mk": _sb(C, F32), "hold": _sb(C, F32),
+    "kmin": _sb(C, BF), "d0": _sb(C, BF), "mk": _sb(C, F32), "hold": _sb(C, F32), "x16r": _sb(C, BF),
+    "cK16": _sb(C, F32), "wrK": _sb(C, F32), "wr3": _sb(2 * C, WD),
     "dm": _sb(C, BF), "ds": _sb(C, WD), "M": _sb(4 * MWD, BF), "qm": _sb(MWD, QX), "sm": _sb(MWD, U8),
     "tmpS": _sb(6 * C, BF), "rs": _sb(24, F32), "junk": _sb(2 * C, BF), "jr": _sb(16 * 12 * 23, BF),
-    "Hg": _sb(4 * C, BF),
-    "c16": _sb(3 * C, BF), "c4": _sb(C, BF), "wr": _sb(3 * C, WD), "wr4": _sb(C, WD), "wrc": _sb(C, WD),
-    "ci": _sb(16, I32), "cf": _sb(32, F32), "x16": _sb(16, F32), "k16": _sb(16, F32), "p16": _sb(16, F32),
+    "win": _sb(C + 16, BF), "LJ": _sb(C, WD), "c32": _sb(2 * C, WD), "rev": _sb(C, F32),
+    "c16": _sb(C, BF), "c4": _sb(C, BF), "wr": _sb(C, WD), "wr4": _sb(C, WD), "wrc": _sb(C, WD),
+    "ci": _sb(16, I32), "cf": _sb(40, F32), "x16": _sb(16, F32), "k16": _sb(16, F32), "p16": _sb(16, F32),
     "p4": _sb(8, F32), "t16": _sb(16, F32), "i16": _sb(24, F32), "rp": _sb(24, F32), "al32": _sb(32, F32),
     "oRep": _sb(8, U16), "oQ": _sb(24, U16), "oQ4": _sb(24, U16), "oHalf": _sb(2, U16),
     "oK": _sb(24, U16), "oP": _sb(24, U16), "oPos": _sb(24, U16), "oPos4": _sb(96, U16), "oAB4": _sb(96, U16),
@@ -40,11 +42,11 @@ SCRATCH = {
     "base": _sb(24, F32), "kk": _sb(24, F32), "sm1": _sb(24, F32),
     "cnt": _sb(2, F32), "tn": _sb(16, F32),
     "rep": _sb(32, F32), "rpt": _sb(32, F32), "dat": _sb(32, BF), "tpl": _sb(1200, BF), "MW": _sb(1200, BF),
-    "Wt": _sb(6 * C, BF), "Pt": _sb(6 * C, BF), "half": _sb(C, BF), "iotaC": _sb(C, BF),
+    "Wt": _sb(6 * C, BF), "Pt": _sb(6 * C, BF), "iotaC": _sb(C, BF),
     "plrow": _sb(C, BF), "porow": _sb(C, BF), "PT": _sb(C, BF), "AB": _sb(C, BF),
     "ABh": _sb(4 * C, BF), "Z": _sb(2 * C, BF), "qz": _sb(192, QX), "sz": _sb(192, U8),
     "Hpm": _sb(4 * C, BF), "qh": _sb(192, QX), "sh": _sb(192, U8),
-    "WL": _sb(C, BF), "gain": _sb(C, BF), "cat": _sb(3 * C, BF), "LW": _sb(C, BF), "crow": _sb(L, BF),
+    "WL": _sb(C, BF), "gain": _sb(C, BF), "cat": _sb(2 * C + 16, WD), "LW": _sb(2 * C, BF), "crow": _sb(L, BF),
     "sab": _sb(4 * L, BF), "ST": _sb(512, BF), "qs": _sb(256, QX), "ss": _sb(256, U8),
     "pp": _sb(C, BF), "sp": _sb(L, BF), "Dt": _sb(4 * L, BF), "yo": _sb(C, F32),
 }
@@ -59,7 +61,7 @@ NDMA = 24
 SEMAPHORES = (["nv", "na", "np_", "ng", "ls", "gw", "go", "ga", "gb"] + ["d%d" % k for k in range(NDMA)]
               + ["arc%d" % t for t in range(R)] + ["arp%d" % t for t in range(R)])
 NAMES = ("cQ cQM cO cOC cH cHM cQ4 cO4 cFL cR1 cR2 cK cTH cTL cNF cMID cBE cTHE cGJ cJ cEP "
-         "cB1 cX1 cT1 cT2 cT3 cM1 cM2 cQ5 cN1 cN2 cJ2").split()
+         "cB1 cX1 cT1 cT2 cT3 cM1 cM2 cQ5 cN1 cN2 cJ2 cO16 cJK").split()
 
 
 def rank_program(g, core, T, topo):
@@ -165,7 +167,7 @@ def rank_program(g, core, T, topo):
             bias=col(bias) if isinstance(bias, str) else bias)
 
     def wrap16(r, w, out, src, m, buf="wr"):
-        scan(r + (" c16 c16b" if m > C else " c16"), buf, T[buf][:, 0:m], src, T.c16[:, 0:m], -2048.0, A.max, A.add)
+        scan(r + " c16", buf, T[buf][:, 0:m], src, T.c16[:, 0:m], -2048.0, A.max, A.add)
         if out is not None:
             ts(buf + " cOC", w, out, T[buf][:, 15:m:16], col("cOC"), A.subtract)
 
@@ -188,64 +190,60 @@ def rank_program(g, core, T, topo):
     iota("ci0", T.ci[:, 0:1], [[0, 1]], 0, 1, False)
     iota("ci8", T.ci[:, 8:16], [[16, 8]], 0, 0, False)
     iota("x16", T.x16[:], [[1, 16]], 0, 0)
-    mset("one", T.one[:], 1.0)
+    iota("x16r", T.x16r[:], [[0, 24], [1, 16]], 0, 0)
     mset("zt", T.zt[:], 0.0)
+    ts("ci0", "ci1", T.ci[:, 1:2], T.ci[:, 0:1], 15, A.bitwise_and)
+    cp("ci8", "oRep", T.oRep[:], T.ci[:, 8:16])
+    cp("ci1", "cQ", col("cQ"), T.ci[:, 1:2])
+    ts("cQ", "cT1", col("cT1"), col("cQ"), 0.0, A.is_gt)
+    ts("cQ", "cR1", col("cR1"), col("cQ"), 4.5, A.is_gt)
+    ts("cQ", "cR2", col("cR2"), col("cQ"), 10.5, A.is_gt)
+    mset("one", T.one[:], 1.0)
     op("g", "one", "cb", lambda: g.affine_select(T.cb[:], T.one[:], [[-16, 8], [0, 64]], A.is_ge, 0.0, 0, 1))
     op("g", "cb", "cb", lambda: g.affine_select(T.cb[:], T.cb[:], [[16, 8], [0, 64]], A.is_ge, 0.0, 15, -1))
     iota("dm", T.dm[:], [[16, 24], [-512, 16]], 0, 0)
     dma("g", "", "", T.qw[:].bitcast(dt.uint8), T.wc[:], "gw")
     dma("g", "", "qw", T.sw[:], T.ws[:], "gw")
-    iota("i16", T.i16[:], [[16, 24]], 0, 0)
-    iota("Wt", T.Wt[:, 0:4 * C], [[0, 4 * C]], 0, 0)
-    iota("iotaC", T.iotaC[:], [[1, C]], -192, 0)
+    iota("tpl", T.tpl[:, 0:400], [[0, 400]], 1, 0)
     iota("tpl3", T.tpl[:, 800:1200], [[0, 400]], 512, 0)
+    iota("iotaC", T.iotaC[:], [[1, C]], -192, 0)
+    iota("rev", T.rev[:], [[-1, C]], C - 1, 0)
     for b in range(4):
         op("g", "one", "ce%d" % b, lambda: g.affine_select(
             T.ce[:, 512 * b:512 * b + 512], T.one[:], [[-1, 512]], A.is_equal, 0.0, b, 4))
+    for k in range(3):
+        e = 4 * TO[5] + 512 * k
+        dma("s", "zt", "mz5" if k == 2 else "", T.M[:, e:e + 512], T.zt[:], "d21")
     dma("s", "zt", "", T.M[:, 0:512], T.zt[:], "d23")
     for k in range(1, 5):
         e = 4 * (TO[k] + TW[k])
-        dma("s", "zt", "", T.M[:, e - 192:e], T.zt[:, 0:192], "d23")
-    dma("s", "zt", "mz STz", T.ST[:, 256:512], T.zt[:, 0:256], "d23")
+        dma("s", "zt", "mz" if k == 4 else "", T.M[:, e - 192:e], T.zt[:, 0:192], "d23")
 
-    ts("ci0", "ci1", T.ci[:, 1:2], T.ci[:, 0:1], 15, A.bitwise_and)
-    ts("ci0", "ci2", T.ci[:, 2:3], T.ci[:, 0:1], 3, A.bitwise_and)
-    ts("ci0", "ci3", T.ci[:, 3:4], T.ci[:, 0:1], 31, A.bitwise_and)
-    cp("ci8", "oRep", T.oRep[:], T.ci[:, 8:16])
-    cp("ci1", "cQ", col("cQ"), T.ci[:, 1:2])
-    cp("ci2", "cQ4", col("cQ4"), T.ci[:, 2:3])
-    cp("ci3", "oHalf", T.oHalf[:, 0:1], T.ci[:, 3:4])
-    ts("one cQ", "oQ", T.oQ[:], T.one[:, 0:24], col("cQ"), A.mult)
     ts("x16 cQ", "k16", T.k16[:], T.x16[:], col("cQ"), A.is_equal)
-    ts("one cQ4", "oQ4", T.oQ4[:], T.one[:, 0:24], col("cQ4"), A.mult)
-    act("k16 oQ", "kmin", T.kmin[:], T.k16[:].indirect(T.oQ[:]), F.Identity, scale=2 * BIG, bias=-BIG)
     ts("k16", "p16", T.p16[:], T.k16[:], 1024.0, A.mult)
     ts("k16", "t16a", T.t16[:, 0:15], T.k16[:, 1:16], -2048.0, A.mult)
     ts("k16", "t16b", T.t16[:, 15:16], T.k16[:, 0:1], -2048.0, A.mult)
-    ts("cQ", "cT1", col("cT1"), col("cQ"), 0.0, A.is_gt)
+    ts("one cQ", "oQ", T.oQ[:], T.one[:, 0:24], col("cQ"), A.mult)
     tt("p16 t16a t16b", "p16", T.p16[:], T.p16[:], T.t16[:], A.add)
-    ts("cQ", "cR1", col("cR1"), col("cQ"), 4.5, A.is_gt)
-    ts("cQ", "cR2", col("cR2"), col("cQ"), 10.5, A.is_gt)
-    ts("cQ cT1", "cFL", col("cFL"), col("cQ"), 3.5, A.is_lt, col("cT1"), A.mult)
-    mset("m21 m22 m23 m24", T.M[:, 4 * TO[5]:4 * MWD], 0.0)
-    mset("d0", T.d0[:], BIG)
-    mset("rs0", T.rs[:, 0:1], 0.0)
-    mset("d0", T.d0[:, 0:C:16], -BIG)
-    act("p16 oQ", "c16", T.c16[:, 0:C], T.p16[:].indirect(T.oQ[:]), F.Copy)
+    ts("x16r cQ", "kmin", T.kmin[:], T.x16r[:], col("cQ"), A.not_equal, -2 * BIG, A.mult)
+    ts("x16r", "d0", T.d0[:], T.x16r[:], 0.0, A.is_equal, -2 * BIG, A.mult)
     quant("ut", "qu", T.qu[:], T.su[:], T.ut[:])
     cp("qu oRep", "qr", T.qr[:].bitcast(dt.uint32), T.qu[:].bitcast(dt.uint32).indirect(T.oRep[:]))
-    dma("s", "c16", "", T.c16[:, C:2 * C], T.c16[:, 0:C], "d22")
-    dma("s", "c16", "c16b", T.c16[:, 2 * C:3 * C], T.c16[:, 0:C], "d22")
+    for k in range(3):
+        dma("s", "zt", "", T.Wt[:, 512 * k:512 * k + 512], T.zt[:], "d20")
+    dma("s", "zt", "", T.LW[:, 0:512], T.zt[:], "d20")
+    dma("s", "zt", "", T.LW[:, 512:768], T.zt[:, 0:256], "d20")
+    dma("s", "zt", "Wt LW STz", T.ST[:, 256:512], T.zt[:, 0:256], "d20")
     dma("s", "", "vt", T.vt[:], T.v[:])
+    lin("cH", "cQ", -1.0, 15.0)
     lin("cO", "cT1", 2048.0, -1024.0)
     lin("cT2", "cR1", -5.0, "cQ")
-    lin("cH", "cQ", -1.0, 15.0)
     lin("cK", "cR2", -6.0, "cT2")
     lin("cOC", "cO", 1.0, -192.0)
-    lin("cB1", "cO", 383.0, "cH")
+    lin("cB1", "cO", 384.0, "cH")
+    lin("cO16", "cO", 16.0)
     lin("cTH", "cK", -1.0, 0.5)
     lin("cTL", "cK", -1.0, -0.5)
-    act("qu oRep", "sr", T.sr[:], T.su[:].indirect(T.oRep[:]), F.Copy)
     lin("cMID", "cR2", -1.0, "cR1")
     lin("cTHE", "cR2", -1.0, 1.0)
     lin("cJ", "cQ", 1.0, 784.0)
@@ -258,31 +256,32 @@ def rank_program(g, core, T, topo):
     lin("cBE", "cMID", 0.5)
     lin("cEP", "cMID", 96.5, "cHM")
     lin("cQM", "cJ", -1.0, 800.0)
-    lin("cEP", "cN1", 193.0, "cEP")
+    lin("cEP", "cN1", 384.0, "cEP")
     lin("cNF", "cMID", -0.25)
     lin("cGJ", "cR1", -400.0, "cQM")
+    act("qu oRep", "sr", T.sr[:], T.su[:].indirect(T.oRep[:]), F.Copy)
+    act("p16 oQ", "c16", T.c16[:, 0:C], T.p16[:].indirect(T.oQ[:]), F.Copy)
     act("one cNF", "al32", T.al32[:], T.one[:, 0:32], F.Identity, scale=col("cNF"))
-    quant("zt", "qs2", T.qs[:, 128:256], T.ss[:, 128:256], T.zt[:])
-    quant("zt", "zl0", T.ql0[:, 0:128], T.sl0[:, 0:128], T.zt[:])
-    mset("half", T.half[:], 0.5)
-    mset("tpl", T.tpl[:, 0:400], 1.0)
-    quant("cb", "qb", T.qb[:], T.sb[:], T.cb[:])
+    act("p16 cB1", "cB1", col("cB1"), T.p16[:, 15:16], F.Identity, scale=16.0, bias=col("cB1"))
+    act("c16", "cK16", T.cK16[:], T.c16[:, 0:C], F.Identity, scale=16.0)
 
     def latest_constants():
         lin("cT2", "cQ4", -1.0, "cQ")
-        lin("cX1", "cO", -513.0, 191.0 - 512.0)
-        lin("cT3", "cO", -1.0, "cH")
-        lin("cT2", "cT2", -0.25)
         lin("cQ5", "cQ4", 1.0, 4096.0 + 768.0)
-        lin("cT3", "cT3", 1.0, 368.0)
+        lin("cT2", "cT2", -0.25)
         act("x16 cT2", "t16a", T.t16[:, 0:4], T.x16[:, 0:4], F.Abs, bias=col("cT2"))
         act("cT2", "cT1", col("cT1"), col("cT2"), F.Sign)
-        act("i16 cT3", "rp", T.rp[:], T.i16[:], F.Identity, scale=-1.0, bias=col("cT3"))
         act("t16a", "t16a", T.t16[:, 0:4], T.t16[:, 0:4], F.Relu, scale=-1024.0, bias=1024.0)
         lin("cO4", "cT1", 8192.0, "cQ5")
         for k in range(4):
             act("t16a", "p4%d" % k, T.p4[:, k:k + 1], T.t16[:, (k + 1) % 4:(k + 1) % 4 + 1], F.Identity, scale=-2.0,
                 bias=T.t16[:, k:k + 1])
+
+    def pair_constants():
+        ts("x16r cQ", "k384", T.gain[:], T.x16r[:], col("cQ"), A.is_equal)
+        cp("c16", "c32a", T.c32[:, 1:2 * C:2], T.c16[:])
+        tt("k384 rev", "c32b", T.c32[:, 0:2 * C:2], T.gain[:], T.rev[:], A.mult)
+        ts("iotaC", "LJ", T.LJ[:, 0:LA], T.iotaC[:, 0:LA], 192.0 + 512.0, A.add)
 
     eng = topo.engines(core, nxt)
     ne, ne_in = len(eng), len(topo.engines(prv, core))
@@ -299,14 +298,21 @@ def rank_program(g, core, T, topo):
         mm("qr sr qx", "P1", T.P1[:, 0:C], T.qr[:], T.sr[:], T.qx[:], T.sx[:])
         if t == 0:
             mm("qu qx", "P3", T.P3[:, 0:C], T.qu[:], T.su[:], T.qx[:], T.sx[:])
-            mset("tpl2", T.tpl[:, 400:800], 0.5)
+            ts("cQ cT1", "cFL", col("cFL"), col("cQ"), 3.5, A.is_lt, col("cT1"), A.mult)
+            mset("rs0", T.rs[:, 0:1], 0.0)
+            ts("ci0", "ci2", T.ci[:, 2:3], T.ci[:, 0:1], 3, A.bitwise_and)
+            ts("ci0", "ci3", T.ci[:, 3:4], T.ci[:, 0:1], 31, A.bitwise_and)
             mset("dat0", T.dat[:, 16:32], 0.0)
+            mset("tpl2", T.tpl[:, 400:800], 0.5)
         else:
             cp("lp%d oC16 pp" % (t - 1), "pp", T.pp[:].indirect(T.oC16[:]), T["lp%d" % (t - 1)][:])
         e = 16 * (24 - NS)
         for a, b, h in ((e, C, "hi"), (0, e, "lo")):
-            tt("P0 kmin", "mk" + h, T.mk[:, a:b], T.P0[:, a:b], T.kmin[:, a:b], A.min)
-            scan("d0 mk" + h, h, T.hold[:, a:b], T.d0[:, a:b], T.mk[:, a:b], -BIG, A.min, A.max)
+            tt("P0 kmin", "mk" + h, T.mk[:, a:b], T.P0[:, a:b], T.kmin[:, a:b], A.add)
+        for a, b, h in ((e, C, "hi"), (0, e, "lo")):
+            scan("d0 mk" + h, h, T.hold[:, a:b], T.d0[:, a:b], T.mk[:, a:b], 0.0, A.add, A.max)
+        if t > 0:
+            wrap16("pp", "", None, T.pp[:], C, "wrc")
 
         def pass1(k):
             i = 23 - k
@@ -315,14 +321,15 @@ def rank_program(g, core, T, topo):
 
         def pass2(k):
             i = 23 - k
-            act("tmp%d mz" % k, "m%d rs%d" % (i, i), mrow(i, 16 * i), T.tmpS[:, C * k:C * k + 16 * i], F.Relu,
+            act("tmp%d mz mz5" % k, "m%d rs%d" % (i, i), mrow(i, 16 * i), T.tmpS[:, C * k:C * k + 16 * i], F.Relu,
                 accum_out=T.rs[:, i:i + 1])
         if t == 0:
             a = TO[5]
             for k in range(NS):
                 pass1(k)
-            ts("P3 cFL", "m24", mrow(24, C), T.P3[:, 0:C], 0.0, A.is_gt, col("cFL"), A.mult)
-            quant("m21 m22 m23 m24", "qm5", T.qm[:, a:MWD], T.sm[:, a:MWD], T.M[:, 4 * a:4 * MWD])
+            ts("P3 cFL mz5", "m24", mrow(24, C), T.P3[:, 0:C], 0.0, A.is_gt, col("cFL"), A.mult)
+            quant("m21 m22 m23 m24 mz5", "qm5", T.qm[:, a:MWD], T.sm[:, a:MWD], T.M[:, 4 * a:4 * MWD])
+            quant("cb", "qb", T.qb[:], T.sb[:], T.cb[:])
             mm("qb qm5", "P4", T.P4[:, 0:C], T.qb[:], T.sb[:], T.qm[:, a:MWD], T.sm[:, a:MWD])
             for k in range(NS):
                 pass2(k)
@@ -347,17 +354,23 @@ def rank_program(g, core, T, topo):
                 qtile(4)
             if i == 11:
                 qtile(3)
-            if i % 4 == 1 and i <= 9:
-                qtile((i - 1) // 4)
-            if i == 2:
+            if i == 9 and t == 0:
                 wrap16("pp", "", None, T.pp[:], C, "wrc")
-        ts("wrc cB1", "base", T.base[:], T.wrc[:, 15:C:16], -384.0, A.mult, col("cB1"), A.add)
-        tt("base ds", "base", T.base[:], T.base[:], T.ds[:, 15:C:16], A.add)
+            if i == 8:
+                qtile(2)
+            if i == 7:
+                ts("wrc cB1", "base", T.base[:], T.wrc[:, 15:C:16], -384.0, A.mult, col("cB1"), A.add)
+            if i == 3:
+                tt("base ds", "base", T.base[:], T.base[:], T.ds[:, 15:C:16], A.add)
+        qtile(1)
+        qtile(0)
+        if t == 0:
+            cp("ci2", "cQ4", col("cQ4"), T.ci[:, 2:3])
+            cp("ci3", "oHalf", T.oHalf[:, 0:1], T.ci[:, 3:4])
         rd = " ".join("rs%d" % i for i in range(24))
-        tt("base " + rd, "base", T.base[:], T.base[:], T.rs[:], A.subtract)
-        wrap16("P2", "", None, T.P2[:, 0:C], C)
-        tt("wr base", "kk", T.kk[:], T.wr[:, 15:C:16], T.base[:], A.add)
-        ts("kk", "oK", T.oK[:], T.kk[:], float(C * top), A.add)
+        tt("base " + rd, "cK16", T.cK16[:, 15:C:16], T.base[:], T.rs[:], A.subtract)
+        scan("P2 cK16", "wrK", T.wrK[:], T.P2[:, 0:C], T.cK16[:], -65536.0, A.max, A.add)
+        ts("wrK cO16", "oK", T.oK[:], T.wrK[:, 15:C:16], col("cO16"), A.subtract, float(C * top), A.add)
         tn = lambda k: T.tn[:, k:k + 1]
         act("pp cTH", "junk0 cnt0", T.junk[:, 0:C], T.pp[:], F.Sign, bias=col("cTH"), accum_out=T.cnt[:, 0:1])
         act("pp cTL", "junk1 cnt1", T.junk[:, C:], T.pp[:], F.Sign, bias=col("cTL"), accum_out=T.cnt[:, 1:2])
@@ -377,35 +390,43 @@ def rank_program(g, core, T, topo):
         act("tn8 tn9 cJ", "tn10", tn(10), tn(8), F.Identity, scale=tn(9), bias=col("cJ"))
         if t == 0:
             latest_constants()
-        cp("oK half Wt", "Wt", T.Wt[:, 0:tw].indirect(T.oK[:]), T.half[:])
+        cp("oK tpl2 Wt", "Wt", T.Wt[:, 0:tw].indirect(T.oK[:]), T.tpl[:, 400:400 + C])
+        op("v", "rep", "rpt", lambda: V.transpose(T.rpt[:], T.rep[:]))
+        if t == 0:
+            ts("one cQ4", "oQ4", T.oQ4[:], T.one[:, 0:24], col("cQ4"), A.mult)
         scan("Wt", "Pt", T.Pt[:, 0:tw], T.Wt[:, 0:tw], T.Wt[:, 0:tw], -193.0, A.add, A.add)
         act("Pt oK", "plrow", T.plrow[:], T.Pt[:, 0:tw].indirect(T.oK[:]), F.Copy)
-        if t == 0:
-            act("p40 p41 p42 p43 oQ4", "c4", T.c4[:], T.p4[:, 0:4].indirect(T.oQ4[:]), F.Copy)
-        op("v", "rep", "rpt", lambda: V.transpose(T.rpt[:], T.rep[:]))
-        cp("tn10 tn11", "oM", T.oM[:], T.tn[:, 10:12])
         cp("rpt oHalf", "dat", T.dat[:, 0:16], T.rpt[:].indirect(T.oHalf[:, 0:1]))
+        cp("tn10 tn11", "oM", T.oM[:], T.tn[:, 10:12])
         cp("dat dat0 oM MW", "MW", T.MW[:].indirect(T.oM[:]), T.dat[:])
         scan("MW", "PT", T.PT[:], T.MW[:, 400:784], T.MW[:, 400:784], -193.0, A.add, A.add)
         wrap16("plrow", "oP", T.oP[:], T.plrow[:], C)
         act("PT oP", "porow", T.porow[:, 0:192], T.PT[:].indirect(T.oP[:, 0:12]), F.Copy)
         cp("PT oP", "porow2", T.porow[:, 192:C], T.PT[:].indirect(T.oP[:, 12:24]))
+        if t == 0:
+            act("p40 p41 p42 p43 oQ4", "c4", T.c4[:], T.p4[:, 0:4].indirect(T.oQ4[:]), F.Copy)
         act("X", "Xh", T.Xh[:], T.X[:], F.Identity, scale=0.5)
         wrap16("porow porow2", "oPos", T.oPos[:], T.porow[:], C)
         cp("oPos iotaC", "AB", T.AB[:].indirect(T.oPos[:]), T.iotaC[:])
         wrap4("AB", "oAB4", T.oAB4[:], T.AB[:], C)
         for k, (a, b) in enumerate(ZC):
-            act("Xh oAB4", "Bh%d" % k, T.ABh[:, 768 + 16 * a:768 + 16 * b],
-                T.Xh[:].indirect(T.oAB4[:, 48 + a:48 + b]), F.Copy)
+            bh, src = T.ABh[:, 768 + 16 * a:768 + 16 * b], T.Xh[:].indirect(T.oAB4[:, 48 + a:48 + b])
+            if k == 0:
+                cp("Xh oAB4", "Bh0 nB0", bh, src)
+            else:
+                act("Xh oAB4", "Bh%d nB%d" % (k, k), bh, src, F.Copy)
         for k, (a, b) in enumerate(ZC):
             tt("Xh oAB4 Bh%d" % k, "Z%d" % k, T.Z[:, 16 * a:16 * b],
                T.Xh[:].indirect(T.oAB4[:, a:b]), T.ABh[:, 768 + 16 * a:768 + 16 * b], A.add)
-        act("Xh oAB4", "Ah0", T.ABh[:, 0:384], T.Xh[:].indirect(T.oAB4[:, 0:24]), F.Copy)
+        act("Xh oAB4", "Ah", T.ABh[:, 0:768], T.Xh[:].indirect(T.oAB4[:, 0:48]), F.Copy)
         quant("Z0 Z1 Z2 Z3", "qz", T.qz[:], T.sz[:], T.Z[:])
         for b in range(4):
             mm("qw qz", "P%d" % (4 + b), T["P%d" % (4 + b)][:, 0:192], T.qw[:, 128 * b:128 * b + 128],
                T.sw[:, 128 * b:128 * b + 128], T.qz[:], T.sz[:])
         wrap4("porow porow2", "oPos4", T.oPos4[:], T.porow[:], C)
+        if t == 0:
+            quant("zt", "qs2", T.qs[:, 128:256], T.ss[:, 128:256], T.zt[:])
+            pair_constants()
         for b in range(4):
             pb = "P%d" % (4 + b)
             if b % 2 == 0:
@@ -414,37 +435,39 @@ def rank_program(g, core, T, topo):
                 ts(pb, "H%d" % b, T.Hpm[:, b:768:4], T[pb][:, 0:192], 0.03125, A.mult)
         quant(HH, "qh", T.qh[:], T.sh[:], T.Hpm[:, 0:768])
         mm("qr sr qh", "P3", T.P3[:, 0:192], T.qr[:], T.sr[:], T.qh[:], T.sh[:])
-        act(HH, "Hm", T.Hpm[:, 768:1536], T.Hpm[:, 0:768], F.Identity, scale=-1.0)
+        act(HH, "Hh", T.Hpm[:, 768:1536], T.Hpm[:, 0:768], F.Identity, scale=0.5)
+        dma("g", "Hh Ah", "Ah", T.ABh[:, 0:768], T.Hpm[:, 768:1536], "ga", accum_op=A.add)
+
+        def newb(k):
+            a = 768 + 192 * k
+            tt("Hh Bh0 Bh1 Bh2 Bh3 Z0 Z1 Z2 Z3", "nB%d" % k, T.ABh[:, a:a + 192], T.ABh[:, a:a + 192],
+               T.Hpm[:, a:a + 192], A.subtract)
         wrap16("PT", "oPP", T.oPP[:], T.PT[:], C, "wrc")
         ts("P3", "WL0", T.WL[:, 0:192], T.P3[:, 0:192], 0.0, A.is_gt)
         ts("P3", "WL1", T.WL[:, 192:C], T.P3[:, 0:192], 0.0, A.is_le)
-        cp("WL0 WL1 oPP", "win", T.cat[:, 2 * C:2 * C + 192], T.WL[:].indirect(T.oPP[:, 0:12]))
-        act("WL0 WL1 oPP", "win2", T.cat[:, 2 * C + 192:3 * C], T.WL[:].indirect(T.oPP[:, 12:24]), F.Copy)
-        act(HH + " Hm oPos4", "Hg", T.Hg[:, 0:HX], T.Hpm[:].indirect(T.oPos4[:, 0:HX // 16]), F.Copy)
-        dma("g", "Hg Xh qx", "Xa", T.X[:, 0:HX], T.Hg[:, 0:HX], "ga", accum_op=A.add)
+        cp("WL0 WL1 oPP", "win", T.win[:, 1:193], T.WL[:].indirect(T.oPP[:, 0:12]))
+        act("WL0 WL1 oPP", "win2", T.win[:, 193:C + 1], T.WL[:].indirect(T.oPP[:, 12:24]), F.Copy)
         act("WL0 WL1 oPos", "gain", T.gain[:], T.WL[:].indirect(T.oPos[:]), F.Copy)
         dma("g", "gain pp", "pp", T.pp[:], T.gain[:], "gb", accum_op=A.add)
-        act("Xh oAB4", "Ah1", T.ABh[:, 384:768], T.Xh[:].indirect(T.oAB4[:, 24:48]), F.Copy)
-        scan("MW win win2", "om", T.cat[:, 2 * C - 1:C - 1:-1], T.MW[:, C:0:-1], T.cat[:, 3 * C - 1:2 * C - 1:-1],
-             0.0, A.mult, A.subtract)
-        scan("MW win win2", "la", T.cat[:, 0:C], T.MW[:, 800:800 + C], T.cat[:, 2 * C:3 * C], 193.0, A.min, A.subtract)
-        wrap16("win win2 om la", "", None, T.cat[:], 3 * C)
-        ts("wr cX1", "sm1", T.sm1[:], T.wr[:, 2 * C + 15:3 * C:16], 512.0, A.mult, col("cX1"), A.add)
-        tt("rp wr", "kk", T.kk[:], T.wr[:, C + 15:2 * C:16], T.rp[:], A.add)
-        tt("wr sm1", "sm1", T.sm1[:], T.sm1[:], T.wr[:, 15:C:16], A.add)
-        tt("kk sm1", "sm1", T.sm1[:], T.sm1[:], T.kk[:], A.max)
-        cp("sm1", "oL", T.oL[:], T.sm1[:])
+        newb(0)
+        scan("MW win2", "la", T.LJ[:, LA:C], T.MW[:, 800 + LA:800 + C], T.win[:, 1 + LA:1 + C], 512.0,
+             A.min, A.subtract)
+        scan("MW win win2", "om", T.cat[:, 2 * C:0:-2], T.MW[:, C:0:-1], T.win[:, C:0:-1], 0.0, A.mult, A.subtract)
+        tt("win win2 la LJ", "lw", T.cat[:, 3:2 * C + 2:2], T.win[:, 1:C + 1], T.LJ[:], A.mult)
+        newb(1)
+        scan("om lw c32a c32b", "wr3", T.wr3[:], T.cat[:, 2:2 * C + 2], T.c32[:], -2048.0, A.max, A.add)
+        newb(2)
+        ts("wr3 cO", "oL", T.oL[:], T.wr3[:, 31:2 * C:32], col("cO"), A.subtract)
+        newb(3)
         cp("oL PT", "LW", T.LW[:].indirect(T.oL[:]), T.PT[:])
         wrap4("LW", "oL4", T.oL4[:], T.LW[:, 0:L], L)
-        for k in range(2):
-            act("Ah0 Ah1 Bh0 Bh1 Bh2 Bh3 oL4", "sab%d" % k, T.sab[:, 128 * k:128 * k + 128],
-                T.ABh[:].indirect(T.oL4[:, 8 * k:8 * k + 8]), F.Identity, scale=2.0)
-        wrap16("LW", "oL16", T.oL16[:], T.LW[:, 0:L], L)
-        act("AB oL16", "crow", T.crow[:], T.AB[:].indirect(T.oL16[:]), F.Copy)
-        for k in range(2):
-            tt(HH + " Hm oL4 sab%d" % k, "ST%d" % k, T.ST[:, 128 * k:128 * k + 128],
-               T.Hpm[:].indirect(T.oL4[:, 8 * k:8 * k + 8]), T.sab[:, 128 * k:128 * k + 128], A.add)
+        wrap16("LW", "", None, T.LW[:, 0:L], L)
+        NB = "Ah nB0 nB1 nB2 nB3 "
+        act(NB + "oL4", "ST0", T.ST[:, 0:128], T.ABh[:].indirect(T.oL4[:, 0:8]), F.Identity, scale=2.0)
+        ts(NB + "oL4", "ST1", T.ST[:, 128:256], T.ABh[:].indirect(T.oL4[:, 8:16]), 2.0, A.mult)
+        ts("wr cOC", "oL16", T.oL16[:], T.wr[:, 15:L:16], col("cOC"), A.subtract)
         quant("ST0 ST1 STz", "qs", T.qs[:, 0:128], T.ss[:, 0:128], T.ST[:])
+        act("AB oL16", "crow", T.crow[:], T.AB[:].indirect(T.oL16[:]), F.Copy)
         deps("g", ["qs", "qs2"], [])
         g.remote_dma_fused([
             RemoteDMATransfer(dst_ids=[DstId(rid=rid, pnc=pid)], dma_engine_mask=lo_mask, remote_sem=T.sem["arc%d" % t],
@@ -462,8 +485,12 @@ def rank_program(g, core, T, topo):
         deps("g", ["sp"], [])
         g.remote_dma(T["lp%d" % t][:], T.sp[:], T.sem["arp%d" % t], T.sem.ls, pid, rid, lo_mask | hi_mask)
         note(("ls", total["ls"]), ["sp"], [])
-        wrap4("crow", "oC4", T.oC4[:], T.crow[:], L)
-        tt(HH + " Hm oPos4 X", "X", T.X[:, HX:], T.Hpm[:].indirect(T.oPos4[:, HX // 16:]), T.X[:, HX:], A.add)
+        for b in range(4):
+            ts("oC16", "oC4%d" % b, T.oC4[:, 4 * b:4 * b + 4], T.oC16[:], 4.0, A.mult, float(b), A.add)
+        if t == 0:
+            quant("zt", "zl0", T.ql0[:, 0:128], T.sl0[:, 0:128], T.zt[:])
+        ts(NB + "oPos4", "X", T.X[:, HX:], T.ABh[:].indirect(T.oPos4[:, HX // 16:]), 2.0, A.mult)
+        act(NB + "oPos4 Xh qx", "Xa", T.X[:, 0:HX], T.ABh[:].indirect(T.oPos4[:, 0:HX // 16]), F.Identity, scale=2.0)
         if t == 0:
             quant("ce0 ce1 ce2 ce3", "qe", T.qe[:], T.se[:], T.ce[:])
         if t == 1:
@@ -480,11 +507,13 @@ def rank_program(g, core, T, topo):
                T.se[:, 128 * b:128 * b + 128], ql[:, 64:192], sl[:, 64:192])
         for b in range(4):
             pb = "P%d" % (4 + b)
-            if b % 2 == 0:
-                act(pb, "D%d" % b, T.Dt[:, b:256:4], T[pb][:, 64:128], F.Copy)
+            if b != 1:
+                act(pb, "D%d" % b, T.Dt[:, L * b:L * b + L], T[pb][:, 64:128], F.Copy)
             else:
-                cp(pb, "D%d" % b, T.Dt[:, b:256:4], T[pb][:, 64:128])
-        cp("D0 D1 D2 D3 oC4 X Xa", "X", T.X[:].indirect(T.oC4[:]), T.Dt[:])
+                cp(pb, "D%d" % b, T.Dt[:, L * b:L * b + L], T[pb][:, 64:128])
+        for b in (0, 2):
+            cp("D%d D%d oC4%d oC4%d X Xa" % (b, b + 1, b, b + 1), "X", T.X[:].indirect(T.oC4[:, 4 * b:4 * b + 8]),
+               T.Dt[:, L * b:L * b + 2 * L])
 
     quant("X", "qx", T.qx[:], T.sx[:], T.X[:])
     dma("s", "qx", "", T.oc[:], T.qx[:].bitcast(dt.uint8))

@@ -1,5 +1,5 @@
 from concourse.bass import DstId, RemoteDMATransfer
-from concourse.mybir import dt, AluOpType, ActivationFunctionType
+from concourse.mybir import dt, AluOpType, ActivationFunctionType, AxisListType
 
 A = AluOpType
 F = ActivationFunctionType
@@ -8,6 +8,10 @@ BIG = 1e29
 WD = "float16"
 HX = 768
 LA = 256
+FV = [(2, 3, 2, 1, 5, 1, 1, 2, 1, 1, 1, 1, 1, 1), (1, 3, 2, 1, 2, 1, 1, 1, 0, 0, 0, 0, 0, 0)]
+FV.append(FV[1])
+NH = 6
+NV = 6
 NS = 4
 TW = [128, 128, 192, 256, 320, 384]
 TO = [sum(TW[:k]) for k in range(6)]
@@ -30,25 +34,25 @@ SCRATCH = {
     "kmin": _sb(C, BF), "d0": _sb(C, BF), "mk": _sb(C, F32), "hold": _sb(C, F32), "x16r": _sb(C, BF),
     "cK16": _sb(C, F32), "wrK": _sb(C, F32), "wr3": _sb(2 * C, WD),
     "dm": _sb(C, BF), "ds": _sb(C, WD), "M": _sb(4 * MWD, BF), "qm": _sb(MWD, QX), "sm": _sb(MWD, U8),
-    "tmpS": _sb(6 * C, BF), "rs": _sb(24, F32), "junk": _sb(2 * C, BF), "jr": _sb(16 * 12 * 23, BF),
-    "win": _sb(C + 16, BF), "LJ": _sb(C, WD), "c32": _sb(2 * C, WD), "rev": _sb(C, F32),
+    "tmpS": _sb(6 * C, BF), "rs": _sb(24, F32), "junk": _sb(2 * C + 2, BF), "jr": _sb(16 * 12 * 23, BF),
+    "win": _sb(C + 16, BF), "LJ": _sb(C, WD), "c32": _sb(2 * C, WD), "rev": _sb(C, WD),
+    "O": _sb(C, BF), "PI": _sb(C, WD), "wri": _sb(C, WD), "oPI": _sb(24, U16), "al2": _sb(32, F32),
     "c16": _sb(C, BF), "c4": _sb(C, BF), "wr": _sb(C, WD), "wr4": _sb(C, WD), "wrc": _sb(C, WD),
     "ci": _sb(16, I32), "cf": _sb(40, F32), "x16": _sb(16, F32), "k16": _sb(16, F32), "p16": _sb(16, F32),
-    "p4": _sb(8, F32), "t16": _sb(16, F32), "i16": _sb(24, F32), "rp": _sb(24, F32), "al32": _sb(32, F32),
-    "oRep": _sb(8, U16), "oQ": _sb(24, U16), "oQ4": _sb(24, U16), "oHalf": _sb(2, U16),
-    "oK": _sb(24, U16), "oP": _sb(24, U16), "oPos": _sb(24, U16), "oPos4": _sb(96, U16), "oAB4": _sb(96, U16),
+    "p4": _sb(8, F32), "t16": _sb(16, F32), "al32": _sb(32, F32),
+    "oRep": _sb(8, U16), "oQ": _sb(24, U16), "oQ4": _sb(24, U16), "oHalf": _sb(4, U16),
+    "oK": _sb(24, U16), "oP": _sb(24, U16), "oPos4": _sb(96, U16), "oAB4": _sb(96, U16),
     "oPP": _sb(24, U16), "oL": _sb(24, U16), "oL4": _sb(16, U16), "oL16": _sb(4, U16), "oC4": _sb(16, U16),
-    "oC16": _sb(4, U16), "oM": _sb(2, U16),
-    "base": _sb(24, F32), "kk": _sb(24, F32), "sm1": _sb(24, F32),
-    "cnt": _sb(2, F32), "tn": _sb(16, F32),
-    "rep": _sb(32, F32), "rpt": _sb(32, F32), "dat": _sb(32, BF), "tpl": _sb(1200, BF), "MW": _sb(1200, BF),
+    "oC16": _sb(4, U16), "oM": _sb(4, U16),
+    "base": _sb(24, F32), "cnt": _sb(2, F32), "tn": _sb(20, F32),
+    "rep": _sb(64, F32), "rpt": _sb(96, F32), "dat": _sb(64, BF), "tpl": _sb(1200, BF), "MW": _sb(1632, BF),
     "Wt": _sb(6 * C, BF), "Pt": _sb(6 * C, BF), "iotaC": _sb(C, BF),
     "plrow": _sb(C, BF), "porow": _sb(C, BF), "PT": _sb(C, BF), "AB": _sb(C, BF),
     "ABh": _sb(4 * C, BF), "Z": _sb(2 * C, BF), "qz": _sb(192, QX), "sz": _sb(192, U8),
     "Hpm": _sb(4 * C, BF), "qh": _sb(192, QX), "sh": _sb(192, U8),
     "WL": _sb(C, BF), "gain": _sb(C, BF), "cat": _sb(2 * C + 16, WD), "LW": _sb(2 * C, BF), "crow": _sb(L, BF),
-    "sab": _sb(4 * L, BF), "ST": _sb(512, BF), "qs": _sb(256, QX), "ss": _sb(256, U8),
-    "pp": _sb(C, BF), "sp": _sb(L, BF), "Dt": _sb(4 * L, BF), "yo": _sb(C, F32),
+    "ST": _sb(512, BF), "qs": _sb(256, QX), "ss": _sb(256, U8),
+    "pp": _sb(C + 16, BF), "sp": _sb(L, BF), "Dt": _sb(4 * L, BF), "yo": _sb(C, F32),
 }
 for _t in range(R):
     SCRATCH["ql%d" % _t] = _sb(192, QX)
@@ -61,7 +65,7 @@ NDMA = 24
 SEMAPHORES = (["nv", "na", "np_", "ng", "ls", "gw", "go", "ga", "gb"] + ["d%d" % k for k in range(NDMA)]
               + ["arc%d" % t for t in range(R)] + ["arp%d" % t for t in range(R)])
 NAMES = ("cQ cQM cO cOC cH cHM cQ4 cO4 cFL cR1 cR2 cK cTH cTL cNF cMID cBE cTHE cGJ cJ cEP "
-         "cB1 cX1 cT1 cT2 cT3 cM1 cM2 cQ5 cN1 cN2 cJ2 cO16 cJK").split()
+         "cB1 cX1 cT1 cT2 cT3 cM1 cM2 cQ5 cN1 cN2 cJ2 cO16 cJN cYA cYB cJA cJB cP32").split()
 
 
 def rank_program(g, core, T, topo):
@@ -173,7 +177,8 @@ def rank_program(g, core, T, topo):
 
     def wrap4(r, w, out, src, m):
         scan(r + " c4", "wr4", T.wr4[:, 0:m], src, T.c4[:, 0:m], -2048.0, A.max, A.add)
-        ts("wr4 cO4", w, out, T.wr4[:, 3:m:4], 4.0, A.mult, col("cO4"), A.add)
+        if out is not None:
+            ts("wr4 cO4", w, out, T.wr4[:, 3:m:4], 4.0, A.mult, col("cO4"), A.add)
 
     def mrow(i, m):
         k, e = (i - 1) // 4, (i - 1) % 4
@@ -207,7 +212,6 @@ def rank_program(g, core, T, topo):
     iota("tpl", T.tpl[:, 0:400], [[0, 400]], 1, 0)
     iota("tpl3", T.tpl[:, 800:1200], [[0, 400]], 512, 0)
     iota("iotaC", T.iotaC[:], [[1, C]], -192, 0)
-    iota("rev", T.rev[:], [[-1, C]], C - 1, 0)
     for b in range(4):
         op("g", "one", "ce%d" % b, lambda: g.affine_select(
             T.ce[:, 512 * b:512 * b + 512], T.one[:], [[-1, 512]], A.is_equal, 0.0, b, 4))
@@ -225,9 +229,8 @@ def rank_program(g, core, T, topo):
     ts("k16", "t16b", T.t16[:, 15:16], T.k16[:, 0:1], -2048.0, A.mult)
     ts("one cQ", "oQ", T.oQ[:], T.one[:, 0:24], col("cQ"), A.mult)
     tt("p16 t16a t16b", "p16", T.p16[:], T.p16[:], T.t16[:], A.add)
-    ts("x16r cQ", "kmin", T.kmin[:], T.x16r[:], col("cQ"), A.not_equal, -2 * BIG, A.mult)
-    ts("x16r", "d0", T.d0[:], T.x16r[:], 0.0, A.is_equal, -2 * BIG, A.mult)
     quant("ut", "qu", T.qu[:], T.su[:], T.ut[:])
+    ts("x16r cQ", "kmin", T.kmin[:], T.x16r[:], col("cQ"), A.not_equal, -2 * BIG, A.mult)
     cp("qu oRep", "qr", T.qr[:].bitcast(dt.uint32), T.qu[:].bitcast(dt.uint32).indirect(T.oRep[:]))
     for k in range(3):
         dma("s", "zt", "", T.Wt[:, 512 * k:512 * k + 512], T.zt[:], "d20")
@@ -252,36 +255,90 @@ def rank_program(g, core, T, topo):
     lin("cJ2", "cQ", 1.0, 1184.0)
     lin("cHM", "cR2", -95.5)
     lin("cM2", "cR1", -16777216.0)
-    lin("cM1", "cR1", 16777216.0, 0.5)
+    lin("cM1", "cR1", 16777216.0, 192.5)
+    act("qu oRep", "sr", T.sr[:], T.su[:].indirect(T.oRep[:]), F.Copy)
     lin("cBE", "cMID", 0.5)
     lin("cEP", "cMID", 96.5, "cHM")
     lin("cQM", "cJ", -1.0, 800.0)
     lin("cEP", "cN1", 384.0, "cEP")
     lin("cNF", "cMID", -0.25)
     lin("cGJ", "cR1", -400.0, "cQM")
-    act("qu oRep", "sr", T.sr[:], T.su[:].indirect(T.oRep[:]), F.Copy)
     act("p16 oQ", "c16", T.c16[:, 0:C], T.p16[:].indirect(T.oQ[:]), F.Copy)
     act("one cNF", "al32", T.al32[:], T.one[:, 0:32], F.Identity, scale=col("cNF"))
     act("p16 cB1", "cB1", col("cB1"), T.p16[:, 15:16], F.Identity, scale=16.0, bias=col("cB1"))
     act("c16", "cK16", T.cK16[:], T.c16[:, 0:C], F.Identity, scale=16.0)
 
-    def latest_constants():
-        lin("cT2", "cQ4", -1.0, "cQ")
-        lin("cQ5", "cQ4", 1.0, 4096.0 + 768.0)
-        lin("cT2", "cT2", -0.25)
-        act("x16 cT2", "t16a", T.t16[:, 0:4], T.x16[:, 0:4], F.Abs, bias=col("cT2"))
-        act("cT2", "cT1", col("cT1"), col("cT2"), F.Sign)
-        act("t16a", "t16a", T.t16[:, 0:4], T.t16[:, 0:4], F.Relu, scale=-1024.0, bias=1024.0)
-        lin("cO4", "cT1", 8192.0, "cQ5")
-        for k in range(4):
-            act("t16a", "p4%d" % k, T.p4[:, k:k + 1], T.t16[:, (k + 1) % 4:(k + 1) % 4 + 1], F.Identity, scale=-2.0,
-                bias=T.t16[:, k:k + 1])
+    def run(calls, k):
+        for _ in range(min(k, len(calls))):
+            calls.pop(0)()
 
-    def pair_constants():
-        ts("x16r cQ", "k384", T.gain[:], T.x16r[:], col("cQ"), A.is_equal)
-        cp("c16", "c32a", T.c32[:, 1:2 * C:2], T.c16[:])
-        tt("k384 rev", "c32b", T.c32[:, 0:2 * C:2], T.gain[:], T.rev[:], A.mult)
-        ts("iotaC", "LJ", T.LJ[:, 0:LA], T.iotaC[:, 0:LA], 192.0 + 512.0, A.add)
+    late = [lambda: lin("cYA", "cQ", -1.0, -400.0), lambda: lin("cYB", "cQ", -1.0, -216.0),
+            lambda: lin("cJN", "cJ2", "cN2"), lambda: lin("cJA", "cQ", 1.0, 1600.0),
+            lambda: lin("cJB", "cQ", 1.0, 1616.0), lambda: lin("cT2", "cQ4", -1.0, "cQ"),
+            lambda: act("al32", "al2", T.al2[:], T.al32[:], F.Identity, scale=-1.0),
+            lambda: lin("cYA", "cYA", "cMID"), lambda: lin("cYB", "cYB", "cMID"),
+            lambda: lin("cQ5", "cQ4", 1.0, 4096.0 + 768.0), lambda: lin("cT2", "cT2", -0.25),
+            lambda: act("x16 cT2", "t16a", T.t16[:, 0:4], T.x16[:, 0:4], F.Abs, bias=col("cT2")),
+            lambda: act("cT2", "cT1", col("cT1"), col("cT2"), F.Sign),
+            lambda: act("t16a", "t16a", T.t16[:, 0:4], T.t16[:, 0:4], F.Relu, scale=-1024.0, bias=1024.0),
+            lambda: lin("cO4", "cT1", 8192.0, "cQ5")]
+    for k in range(4):
+        late.append(lambda k=k: act("t16a", "p4%d" % k, T.p4[:, k:k + 1], T.t16[:, (k + 1) % 4:(k + 1) % 4 + 1],
+                                    F.Identity, scale=-2.0, bias=T.t16[:, k:k + 1]))
+
+    pairc = [lambda: ts("x16r cQ", "k384", T.gain[:], T.x16r[:], col("cQ"), A.is_equal),
+             lambda: ts("iotaC", "rev", T.rev[:], T.iotaC[:], -1.0, A.mult, 191.0, A.add),
+             lambda: cp("c16", "c32a", T.c32[:, 1:2 * C:2], T.c16[:]),
+             lambda: tt("k384 rev", "c32b", T.c32[:, 0:C:2], T.gain[:, 0:192], T.rev[:, 0:192], A.mult),
+             lambda: tt("k384 rev", "c32c", T.c32[:, C:2 * C:2], T.gain[:, 192:C], T.rev[:, 192:C], A.mult),
+             lambda: ts("iotaC", "LJ", T.LJ[:, 0:LA], T.iotaC[:, 0:LA], 192.0 + 512.0, A.add),
+             lambda: quant("zt", "qs2", T.qs[:, 128:256], T.ss[:, 128:256], T.zt[:])]
+
+    def tn(k):
+        return T.tn[:, k:k + 1]
+
+    def borders(k):
+        if k == 0:
+            act("pp cTH", "junk0 cnt0", T.junk[:, 0:C + 1], T.pp[:, 0:C + 1], F.Sign, bias=col("cTH"),
+                accum_out=T.cnt[:, 0:1])
+            act("pp cTL", "junk1 cnt1", T.junk[:, C + 1:], T.pp[:, 0:C + 1], F.Sign, bias=col("cTL"),
+                accum_out=T.cnt[:, 1:2])
+        if k == 1:
+            act("cnt0 cnt1 cM1", "tn2", T.tn[:, 2:4], T.cnt[:], F.Identity, scale=0.5, bias=col("cM1"))
+        if k == 2:
+            act("tn2 cM2", "tn4", T.tn[:, 4:6], T.tn[:, 2:4], F.Identity, bias=col("cM2"))
+        if k == 3:
+            act("tn4", "tn6", tn(6), tn(5), F.Identity, scale=-1.0, bias=tn(4))
+            act("tn4 cTHE", "tn7", tn(7), tn(5), F.Sign, bias=col("cTHE"))
+            act("tn4 cN2 cEP", "tn12", tn(12), tn(5), F.Identity, scale=col("cN2"), bias=col("cEP"))
+            act("tn4 cGJ", "tn0", tn(0), tn(5), F.Identity, bias=col("cGJ"))
+            act("tn4 cN1 cJN", "tn13", tn(13), tn(5), F.Identity, scale=col("cN1"), bias=col("cJN"))
+            act("tn4 cBE cYA", "tn14", tn(14), tn(4), F.Identity, scale=col("cBE"), bias=col("cYA"))
+            act("tn4 cBE cYB", "tn15", tn(15), tn(5), F.Identity, scale=col("cBE"), bias=col("cYB"))
+        if k == 4:
+            act("tn6 tn7", "tn9", tn(9), tn(6), F.Sign, scale=tn(7))
+            act("tn6 tn0 cBE", "tn8", tn(8), tn(6), F.Identity, scale=col("cBE"), bias=tn(0))
+            act("al32 tn6 tn12", "rep", T.rep[:, 0:32], T.al32[:], F.Identity, scale=tn(6), bias=tn(12))
+            act("al2 tn6", "rep2", T.rep[:, 32:64], T.al2[:], F.Identity, scale=tn(6), bias=0.5)
+
+    def tables():
+        def offs(j, a, c):
+            return lambda: ts("tn%d tn9 %s" % (a, c), "oM%d" % j, T.oM[:, j:j + 1], tn(a), tn(9), A.mult, col(c), A.add)
+        return [lambda: op("v", "rep rep2", "rpt", lambda: V.transpose(T.rpt[:, 0:64], T.rep[:])),
+                offs(0, 8, "cJ"), offs(1, 13, "cJ2"), offs(2, 14, "cJA"), offs(3, 15, "cJB"),
+                lambda: cp("rpt rpz oHalf oHalf1 oHalf2", "dat", T.dat[:], T.rpt[:].indirect(T.oHalf[:])),
+                lambda: cp("dat oM0 oM1 oM2 oM3 MW", "MW", T.MW[:].indirect(T.oM[:]), T.dat[:]),
+                lambda: scan("MW", "PIa", T.PI[:, 0:192], T.MW[:, 1200:1392], T.MW[:, 1200:1392], -1.0, A.add, A.add),
+                lambda: scan("MW", "PIb", T.PI[:, 192:C], T.MW[:, 1400:1592], T.MW[:, 1400:1592], -1.0, A.add, A.add),
+                lambda: wrap16("PIa PIb", "", None, T.PI[:], C, "wri"),
+                lambda: ts("wri cO", "oPI", T.oPI[:], T.wri[:, 15:C:16], col("cO"), A.subtract),
+                lambda: scan("MW", "PT", T.PT[:], T.MW[:, 400:784], T.MW[:, 400:784], -193.0, A.add, A.add)]
+
+    def blank_marks():
+        dma("s", "tpl tpl2 tpl3", "MW", T.MW[:, 0:1200], T.tpl[:], "d19")
+        total["d19"] += 16
+        g.sync.dma_start(T.MW[:, 1200:1600], T.tpl[:, 400:800]).then_inc(T.sem.d19, 16)
+        note(("d19", total["d19"]), ["tpl2"], ["MW"])
 
     eng = topo.engines(core, nxt)
     ne, ne_in = len(eng), len(topo.engines(prv, core))
@@ -298,21 +355,27 @@ def rank_program(g, core, T, topo):
         mm("qr sr qx", "P1", T.P1[:, 0:C], T.qr[:], T.sr[:], T.qx[:], T.sx[:])
         if t == 0:
             mm("qu qx", "P3", T.P3[:, 0:C], T.qu[:], T.su[:], T.qx[:], T.sx[:])
+            ts("x16r", "d0", T.d0[:], T.x16r[:], 0.0, A.is_equal, -2 * BIG, A.mult)
             ts("cQ cT1", "cFL", col("cFL"), col("cQ"), 3.5, A.is_lt, col("cT1"), A.mult)
             mset("rs0", T.rs[:, 0:1], 0.0)
             ts("ci0", "ci2", T.ci[:, 2:3], T.ci[:, 0:1], 3, A.bitwise_and)
             ts("ci0", "ci3", T.ci[:, 3:4], T.ci[:, 0:1], 31, A.bitwise_and)
-            mset("dat0", T.dat[:, 16:32], 0.0)
+            mset("ppz", T.pp[:, C:C + 1], -100.0)
             mset("tpl2", T.tpl[:, 400:800], 0.5)
+            fill = [lambda: mset("rpz", T.rpt[:, 64:96], 0.0),
+                    lambda: ts("one cQ4", "oQ4", T.oQ4[:], T.one[:, 0:24], col("cQ4"), A.mult),
+                    lambda: cp("ci3", "oHalf", T.oHalf[:, 0:1], T.ci[:, 3:4]),
+                    lambda: mset("oHalf1", T.oHalf[:, 1:2], 64),
+                    lambda: ts("cP32 one", "oHalf2", T.oHalf[:, 2:4], T.one[:, 0:2], col("cP32"), A.mult, 32.0, A.add),
+                    ] + pairc[:3] + tables() + pairc[3:]
         else:
-            cp("lp%d oC16 pp" % (t - 1), "pp", T.pp[:].indirect(T.oC16[:]), T["lp%d" % (t - 1)][:])
-        e = 16 * (24 - NS)
+            wrap16("pp", "", None, T.pp[:, 0:C], C, "wrc")
+            fill = tables()
+        e = 16 * (24 - NH)
         for a, b, h in ((e, C, "hi"), (0, e, "lo")):
             tt("P0 kmin", "mk" + h, T.mk[:, a:b], T.P0[:, a:b], T.kmin[:, a:b], A.add)
         for a, b, h in ((e, C, "hi"), (0, e, "lo")):
             scan("d0 mk" + h, h, T.hold[:, a:b], T.d0[:, a:b], T.mk[:, a:b], 0.0, A.add, A.max)
-        if t > 0:
-            wrap16("pp", "", None, T.pp[:], C, "wrc")
 
         def pass1(k):
             i = 23 - k
@@ -333,29 +396,32 @@ def rank_program(g, core, T, topo):
             mm("qb qm5", "P4", T.P4[:, 0:C], T.qb[:], T.sb[:], T.qm[:, a:MWD], T.sm[:, a:MWD])
             for k in range(NS):
                 pass2(k)
-            act("P4", "pp", T.pp[:], T.P4[:, 0:C], F.Copy)
+            act("P4 ppz", "pp", T.pp[:, 0:C], T.P4[:, 0:C], F.Copy)
         else:
             pass1(0)
             for k in range(NS):
                 if k + 1 < NS:
                     pass1(k + 1)
                 pass2(k)
-        tt("P0 hi lo", "m24", mrow(24, C), T.hold[:], T.P0[:, 0:C], A.is_ge)
         if t == 0:
-            dma("s", "tpl tpl2 tpl3", "MW", T.MW[:], T.tpl[:])
+            blank_marks()
         for i in range(23 - NS, 0, -1):
-            ts("P0 lo mz", "m%d" % i, mrow(i, 16 * i), T.P0[:, 0:16 * i], T.hold[:, 16 * i + 15:16 * i + 16], A.is_lt)
-            act("m%d" % i, "rs%d jr%d" % (i, i), T.jr[:, 8 * i * (i - 1):8 * i * (i + 1)], mrow(i, 16 * i), F.Copy,
-                accum_out=T.rs[:, i:i + 1])
+            if i == 22 - NS:
+                tt("P0 hi lo", "m24", mrow(24, C), T.hold[:], T.P0[:, 0:C], A.is_ge)
+            ts("P0 mz " + ("hi" if i >= 24 - NH else "lo"), "m%d" % i, mrow(i, 16 * i), T.P0[:, 0:16 * i],
+               T.hold[:, 16 * i + 15:16 * i + 16], A.is_lt)
+            if i > NV:
+                act("m%d" % i, "rs%d jr%d" % (i, i), T.jr[:, 8 * i * (i - 1):8 * i * (i + 1)], mrow(i, 16 * i), F.Copy,
+                    accum_out=T.rs[:, i:i + 1])
             if i == 17:
                 scan("m24 dm", "ds", T.ds[:], T.dm[:], mrow(24, C), 0.0, A.max, A.subtract)
-            if i == 13:
+            if i == 12:
                 qtile(5)
                 qtile(4)
             if i == 11:
                 qtile(3)
             if i == 9 and t == 0:
-                wrap16("pp", "", None, T.pp[:], C, "wrc")
+                wrap16("pp", "", None, T.pp[:, 0:C], C, "wrc")
             if i == 8:
                 qtile(2)
             if i == 7:
@@ -364,69 +430,70 @@ def rank_program(g, core, T, topo):
                 tt("base ds", "base", T.base[:], T.base[:], T.ds[:, 15:C:16], A.add)
         qtile(1)
         qtile(0)
+        for i in range(NV, 0, -1):
+            op("v", "m%d" % i, "rs%d" % i, lambda: V.tensor_reduce(T.rs[:, i:i + 1], mrow(i, 16 * i), AxisListType.X, A.add))
         if t == 0:
             cp("ci2", "cQ4", col("cQ4"), T.ci[:, 2:3])
-            cp("ci3", "oHalf", T.oHalf[:, 0:1], T.ci[:, 3:4])
+            cp("ci3", "cP32", col("cP32"), T.ci[:, 3:4])
         rd = " ".join("rs%d" % i for i in range(24))
+        if t == 0:
+            for k in range(5):
+                borders(k)
+                run(late, (7, 2, 2, 2, 9)[k])
+        run(fill, FV[t][0])
         tt("base " + rd, "cK16", T.cK16[:, 15:C:16], T.base[:], T.rs[:], A.subtract)
-        scan("P2 cK16", "wrK", T.wrK[:], T.P2[:, 0:C], T.cK16[:], -65536.0, A.max, A.add)
-        ts("wrK cO16", "oK", T.oK[:], T.wrK[:, 15:C:16], col("cO16"), A.subtract, float(C * top), A.add)
-        tn = lambda k: T.tn[:, k:k + 1]
-        act("pp cTH", "junk0 cnt0", T.junk[:, 0:C], T.pp[:], F.Sign, bias=col("cTH"), accum_out=T.cnt[:, 0:1])
-        act("pp cTL", "junk1 cnt1", T.junk[:, C:], T.pp[:], F.Sign, bias=col("cTL"), accum_out=T.cnt[:, 1:2])
-        act("cnt0 cnt1", "tn0", T.tn[:, 0:2], T.cnt[:], F.Identity, scale=0.5, bias=191.5)
-        act("tn0 cM1", "tn2", T.tn[:, 2:4], T.tn[:, 0:2], F.Identity, bias=col("cM1"))
-        act("tn2 cM2", "tn4", T.tn[:, 4:6], T.tn[:, 2:4], F.Identity, bias=col("cM2"))
-        act("tn4", "tn6", tn(6), tn(5), F.Identity, scale=-1.0, bias=tn(4))
-        act("tn4 cTHE", "tn7", tn(7), tn(5), F.Sign, bias=col("cTHE"))
-        act("tn6 tn4 cBE", "tn8", tn(8), tn(6), F.Identity, scale=col("cBE"), bias=tn(5))
-        act("tn6 tn7", "tn9", tn(9), tn(6), F.Sign, scale=tn(7))
-        act("tn4 cN2 cEP", "tn12", tn(12), tn(5), F.Identity, scale=col("cN2"), bias=col("cEP"))
-        act("tn4 cJ2", "tn13", tn(13), tn(5), F.Identity, scale=-1.0, bias=col("cJ2"))
-        act("tn9 cN2", "tn14", tn(14), tn(9), F.Identity, scale=col("cN2"))
-        act("al32 tn6 tn12", "rep", T.rep[:], T.al32[:], F.Identity, scale=tn(6), bias=tn(12))
-        act("tn13 tn14 cJ2", "tn11", tn(11), tn(13), F.Identity, scale=tn(14), bias=col("cJ2"))
-        act("tn8 cGJ", "tn8", tn(8), tn(8), F.Identity, bias=col("cGJ"))
-        act("tn8 tn9 cJ", "tn10", tn(10), tn(8), F.Identity, scale=tn(9), bias=col("cJ"))
-        if t == 0:
-            latest_constants()
-        cp("oK tpl2 Wt", "Wt", T.Wt[:, 0:tw].indirect(T.oK[:]), T.tpl[:, 400:400 + C])
-        op("v", "rep", "rpt", lambda: V.transpose(T.rpt[:], T.rep[:]))
-        if t == 0:
-            ts("one cQ4", "oQ4", T.oQ4[:], T.one[:, 0:24], col("cQ4"), A.mult)
-        scan("Wt", "Pt", T.Pt[:, 0:tw], T.Wt[:, 0:tw], T.Wt[:, 0:tw], -193.0, A.add, A.add)
-        act("Pt oK", "plrow", T.plrow[:], T.Pt[:, 0:tw].indirect(T.oK[:]), F.Copy)
-        cp("rpt oHalf", "dat", T.dat[:, 0:16], T.rpt[:].indirect(T.oHalf[:, 0:1]))
-        cp("tn10 tn11", "oM", T.oM[:], T.tn[:, 10:12])
-        cp("dat dat0 oM MW", "MW", T.MW[:].indirect(T.oM[:]), T.dat[:])
-        scan("MW", "PT", T.PT[:], T.MW[:, 400:784], T.MW[:, 400:784], -193.0, A.add, A.add)
-        wrap16("plrow", "oP", T.oP[:], T.plrow[:], C)
-        act("PT oP", "porow", T.porow[:, 0:192], T.PT[:].indirect(T.oP[:, 0:12]), F.Copy)
-        cp("PT oP", "porow2", T.porow[:, 192:C], T.PT[:].indirect(T.oP[:, 12:24]))
         if t == 0:
             act("p40 p41 p42 p43 oQ4", "c4", T.c4[:], T.p4[:, 0:4].indirect(T.oQ4[:]), F.Copy)
-        act("X", "Xh", T.Xh[:], T.X[:], F.Identity, scale=0.5)
-        wrap16("porow porow2", "oPos", T.oPos[:], T.porow[:], C)
-        cp("oPos iotaC", "AB", T.AB[:].indirect(T.oPos[:]), T.iotaC[:])
-        wrap4("AB", "oAB4", T.oAB4[:], T.AB[:], C)
+        else:
+            act("X", "Xh", T.Xh[:], T.X[:], F.Identity, scale=0.5)
+        run(fill, FV[t][1])
+        scan("P2 cK16", "wrK", T.wrK[:], T.P2[:, 0:C], T.cK16[:], -65536.0, A.max, A.add)
+        run(fill, FV[t][2])
+        ts("wrK cO16", "oK", T.oK[:], T.wrK[:, 15:C:16], col("cO16"), A.subtract, float(C * top), A.add)
+        run(fill, FV[t][3])
+        cp("oK tpl2 Wt", "Wt", T.Wt[:, 0:tw].indirect(T.oK[:]), T.tpl[:, 400:400 + C])
+        run(fill, FV[t][4])
+        scan("Wt", "Pt", T.Pt[:, 0:tw], T.Wt[:, 0:tw], T.Wt[:, 0:tw], -193.0, A.add, A.add)
+        run(fill, FV[t][5])
+        act("Pt oK", "plrow", T.plrow[:, 0:192], T.Pt[:, 0:tw].indirect(T.oK[:, 0:12]), F.Copy)
+        cp("Pt oK", "plrow2", T.plrow[:, 192:C], T.Pt[:, 0:tw].indirect(T.oK[:, 12:24]))
+        run(fill, FV[t][6])
+        wrap16("plrow plrow2", "", None, T.plrow[:], C)
+        run(fill, FV[t][7])
+        ts("wr cOC", "oP", T.oP[:], T.wr[:, 15:C:16], col("cOC"), A.subtract)
+        run(fill, FV[t][8])
+        cp("oP iotaC", "O", T.O[:].indirect(T.oP[:]), T.iotaC[:])
+        if t == 0:
+            act("X", "Xh", T.Xh[:], T.X[:], F.Identity, scale=0.5)
+        run(fill, FV[t][9])
+        if t > 0:
+            act("PT oP", "porow", T.porow[:], T.PT[:].indirect(T.oP[:]), F.Copy)
+        act("O oPI", "AB", T.AB[:, 0:192], T.O[:].indirect(T.oPI[:, 0:12]), F.Copy)
+        cp("O oPI", "AB2", T.AB[:, 192:C], T.O[:].indirect(T.oPI[:, 12:24]))
+        run(fill, FV[t][10])
+        if t == 0:
+            act("PT oP", "porow", T.porow[:], T.PT[:].indirect(T.oP[:]), F.Copy)
+        wrap4("AB AB2", "", None, T.AB[:], C)
+        run(fill, FV[t][11])
+        ts("wr4 cO4", "oAB4", T.oAB4[:], T.wr4[:, 3:C:4], 4.0, A.mult, col("cO4"), A.add)
+        run(fill, FV[t][12])
         for k, (a, b) in enumerate(ZC):
             bh, src = T.ABh[:, 768 + 16 * a:768 + 16 * b], T.Xh[:].indirect(T.oAB4[:, 48 + a:48 + b])
             if k == 0:
                 cp("Xh oAB4", "Bh0 nB0", bh, src)
             else:
                 act("Xh oAB4", "Bh%d nB%d" % (k, k), bh, src, F.Copy)
+        run(fill, FV[t][13])
         for k, (a, b) in enumerate(ZC):
             tt("Xh oAB4 Bh%d" % k, "Z%d" % k, T.Z[:, 16 * a:16 * b],
                T.Xh[:].indirect(T.oAB4[:, a:b]), T.ABh[:, 768 + 16 * a:768 + 16 * b], A.add)
+        run(fill, len(fill))
         act("Xh oAB4", "Ah", T.ABh[:, 0:768], T.Xh[:].indirect(T.oAB4[:, 0:48]), F.Copy)
         quant("Z0 Z1 Z2 Z3", "qz", T.qz[:], T.sz[:], T.Z[:])
         for b in range(4):
             mm("qw qz", "P%d" % (4 + b), T["P%d" % (4 + b)][:, 0:192], T.qw[:, 128 * b:128 * b + 128],
                T.sw[:, 128 * b:128 * b + 128], T.qz[:], T.sz[:])
-        wrap4("porow porow2", "oPos4", T.oPos4[:], T.porow[:], C)
-        if t == 0:
-            quant("zt", "qs2", T.qs[:, 128:256], T.ss[:, 128:256], T.zt[:])
-            pair_constants()
+        wrap4("porow", "oPos4", T.oPos4[:], T.porow[:], C)
         for b in range(4):
             pb = "P%d" % (4 + b)
             if b % 2 == 0:
@@ -445,17 +512,18 @@ def rank_program(g, core, T, topo):
         wrap16("PT", "oPP", T.oPP[:], T.PT[:], C, "wrc")
         ts("P3", "WL0", T.WL[:, 0:192], T.P3[:, 0:192], 0.0, A.is_gt)
         ts("P3", "WL1", T.WL[:, 192:C], T.P3[:, 0:192], 0.0, A.is_le)
-        cp("WL0 WL1 oPP", "win", T.win[:, 1:193], T.WL[:].indirect(T.oPP[:, 0:12]))
-        act("WL0 WL1 oPP", "win2", T.win[:, 193:C + 1], T.WL[:].indirect(T.oPP[:, 12:24]), F.Copy)
-        act("WL0 WL1 oPos", "gain", T.gain[:], T.WL[:].indirect(T.oPos[:]), F.Copy)
-        dma("g", "gain pp", "pp", T.pp[:], T.gain[:], "gb", accum_op=A.add)
+        cp("WL0 WL1 oPP", "win", T.win[:, 16:208], T.WL[:].indirect(T.oPP[:, 0:12]))
+        act("WL0 WL1 oPP", "win2", T.win[:, 208:C + 16], T.WL[:].indirect(T.oPP[:, 12:24]), F.Copy)
+        act("win win2 oP", "gain k384", T.gain[:], T.win[:, 16:C + 16].indirect(T.oP[:]), F.Copy)
+        dma("g", "gain pp", "pp", T.pp[:, 0:C], T.gain[:], "gb", accum_op=A.add)
         newb(0)
-        scan("MW win2", "la", T.LJ[:, LA:C], T.MW[:, 800 + LA:800 + C], T.win[:, 1 + LA:1 + C], 512.0,
+        scan("MW win2", "la", T.LJ[:, LA:C], T.MW[:, 800 + LA:800 + C], T.win[:, 16 + LA:16 + C], 512.0,
              A.min, A.subtract)
-        scan("MW win win2", "om", T.cat[:, 2 * C:0:-2], T.MW[:, C:0:-1], T.win[:, C:0:-1], 0.0, A.mult, A.subtract)
-        tt("win win2 la LJ", "lw", T.cat[:, 3:2 * C + 2:2], T.win[:, 1:C + 1], T.LJ[:], A.mult)
+        scan("MW win win2", "om", T.cat[:, 2 * C:0:-2], T.MW[:, C:0:-1], T.win[:, C + 15:15:-1], 0.0,
+             A.mult, A.subtract)
+        tt("win win2 la LJ", "lw", T.cat[:, 3:2 * C + 2:2], T.win[:, 16:C + 16], T.LJ[:], A.mult)
         newb(1)
-        scan("om lw c32a c32b", "wr3", T.wr3[:], T.cat[:, 2:2 * C + 2], T.c32[:], -2048.0, A.max, A.add)
+        scan("om lw c32a c32b c32c", "wr3", T.wr3[:], T.cat[:, 2:2 * C + 2], T.c32[:], -2048.0, A.max, A.add)
         newb(2)
         ts("wr3 cO", "oL", T.oL[:], T.wr3[:, 31:2 * C:32], col("cO"), A.subtract)
         newb(3)
@@ -467,7 +535,7 @@ def rank_program(g, core, T, topo):
         ts(NB + "oL4", "ST1", T.ST[:, 128:256], T.ABh[:].indirect(T.oL4[:, 8:16]), 2.0, A.mult)
         ts("wr cOC", "oL16", T.oL16[:], T.wr[:, 15:L:16], col("cOC"), A.subtract)
         quant("ST0 ST1 STz", "qs", T.qs[:, 0:128], T.ss[:, 0:128], T.ST[:])
-        act("AB oL16", "crow", T.crow[:], T.AB[:].indirect(T.oL16[:]), F.Copy)
+        act("AB AB2 oL16", "crow", T.crow[:], T.AB[:].indirect(T.oL16[:]), F.Copy)
         deps("g", ["qs", "qs2"], [])
         g.remote_dma_fused([
             RemoteDMATransfer(dst_ids=[DstId(rid=rid, pnc=pid)], dma_engine_mask=lo_mask, remote_sem=T.sem["arc%d" % t],
@@ -481,7 +549,7 @@ def rank_program(g, core, T, topo):
         lastw["lp%d" % t] = ("arp%d" % t, ne_in)
         total["arc%d" % t] = total["arp%d" % t] = ne_in
         wrap16("crow", "oC16", T.oC16[:], T.crow[:], L)
-        act("pp oC16", "sp", T.sp[:], T.pp[:].indirect(T.oC16[:]), F.Copy)
+        act("pp oC16", "sp", T.sp[:], T.pp[:, 0:C].indirect(T.oC16[:]), F.Copy)
         deps("g", ["sp"], [])
         g.remote_dma(T["lp%d" % t][:], T.sp[:], T.sem["arp%d" % t], T.sem.ls, pid, rid, lo_mask | hi_mask)
         note(("ls", total["ls"]), ["sp"], [])
@@ -499,7 +567,7 @@ def rank_program(g, core, T, topo):
             z = "%d" % (t + 1)
             quant("zt", "zl" + z, T["ql" + z][:, 0:128], T["sl" + z][:, 0:128], T.zt[:])
             iota("Wt", T.Wt[:, 0:tw + C], [[0, tw + C]], 0, 0)
-            dma("s", "tpl tpl2 tpl3", "MW", T.MW[:], T.tpl[:])
+            blank_marks()
         ql, sl = T["ql%d" % t], T["sl%d" % t]
         for b in range(4):
             pb = "P%d" % (4 + b)
@@ -514,19 +582,24 @@ def rank_program(g, core, T, topo):
         for b in (0, 2):
             cp("D%d D%d oC4%d oC4%d X Xa" % (b, b + 1, b, b + 1), "X", T.X[:].indirect(T.oC4[:, 4 * b:4 * b + 8]),
                T.Dt[:, L * b:L * b + 2 * L])
+            if b == 0:
+                cp("lp%d oC16 pp" % t, "pp", T.pp[:, 0:C].indirect(T.oC16[:]), T["lp%d" % t][:])
+        if t + 1 < R:
+            for k in range(5):
+                borders(k)
 
-    quant("X", "qx", T.qx[:], T.sx[:], T.X[:])
-    dma("s", "qx", "", T.oc[:], T.qx[:].bitcast(dt.uint8))
-    h = C // 2
-    mm("qv qx", "P0", T.P0[:, 0:h], T.qv[:], T.sv[:], T.qx[:, 0:h], T.sx[:, 0:h])
-    mm("qv qx", "P1", T.P1[:, 0:h], T.qv[:], T.sv[:], T.qx[:, h:C], T.sx[:, h:C])
-    cp("lp%d oC16 pp" % (R - 1), "pp", T.pp[:].indirect(T.oC16[:]), T["lp%d" % (R - 1)][:])
-    act("P0", "y0", T.yo[:, 0:h], T.P0[:, 0:h], F.Copy)
-    cp("P1", "y1", T.yo[:, h:C], T.P1[:, 0:h])
-    dma("a", "y0", "", T.y[:, 0:h], T.yo[:, 0:h])
-    dma("g", "pp", "", T.pts[:], T.pp[0:128:16, :], "go")
+    dma("g", "pp", "", T.pts[:], T.pp[0:128:16, 0:C], "go")
+    for k in range(3):
+        a, b = 128 * k, 128 * k + 128
+        quant("X", "qx qx%d" % k if k == 0 else "qx%d" % k, T.qx[:, a:b], T.sx[:, a:b], T.X[:, 4 * a:4 * b])
+        mm("qv qx%d" % k, "P%d" % k, T["P%d" % k][:, 0:128], T.qv[:], T.sv[:], T.qx[:, a:b], T.sx[:, a:b])
+    dma("s", "qx0 qx1 qx2", "", T.oc[:], T.qx[:].bitcast(dt.uint8))
     for k in range(4):
-        dma("s", "qx", "", T.osc[4 * k:4 * k + 4, :], T.sx[32 * k:32 * k + 4, :])
-    dma("a", "y1", "", T.y[:, h:C], T.yo[:, h:C])
+        dma("s", "qx0 qx1 qx2", "", T.osc[4 * k:4 * k + 4, :], T.sx[32 * k:32 * k + 4, :])
+    act("P0", "y0", T.yo[:, 0:128], T.P0[:, 0:128], F.Copy)
+    cp("P1", "y1", T.yo[:, 128:256], T.P1[:, 0:128])
+    act("P2", "y2", T.yo[:, 256:C], T.P2[:, 0:128], F.Copy)
+    dma("s", "y0 y1", "", T.y[:, 0:256], T.yo[:, 0:256])
+    dma("a", "y2", "", T.y[:, 256:C], T.yo[:, 256:C])
     for s in total:
         wait("g", (s, total[s]))

@@ -8,15 +8,19 @@ BIG = 1e29
 WD = "float16"
 HX = 768
 LA = 256
-FV = [(2, 3, 2, 1, 5, 1, 1, 2, 1, 1, 1, 1, 1, 1), (1, 3, 2, 1, 2, 1, 1, 1, 0, 0, 0, 0, 0, 0)]
+FV = [(3, 3, 1, 1, 5, 1, 1, 2, 1, 1, 1, 1, 1, 1), (3, 2, 1, 0, 1, 2, 1, 1, 1, 0, 0, 0, 0, 0)]
 FV.append(FV[1])
-NH = 6
+NH = 8
 NV = 6
 NS = 4
+NS1, NV1, Q5 = 5, 6, 8
 TW = [128, 128, 192, 256, 320, 384]
 TO = [sum(TW[:k]) for k in range(6)]
+QO = TO[:5] + [TO[5] + 64]
 MWD = sum(TW)
-ZC = [(0, 8), (8, 24), (24, 40), (40, 48)]
+FW = 1024.0
+ROUND = 12582912.0
+ZC = [(0, 8), (8, 20), (20, 32), (32, 48)]
 
 
 def _sb(n, d):
@@ -30,11 +34,11 @@ SCRATCH = {
     "qr": _sb(128, QX), "sr": _sb(128, U8), "qv": _sb(128, QX), "sv": _sb(128, U8),
     "qw": _sb(512, QX), "sw": _sb(512, U8),
     "one": _sb(512, BF), "cb": _sb(512, BF), "qb": _sb(128, QX), "sb": _sb(128, U8),
-    "ce": _sb(2048, BF), "qe": _sb(512, QX), "se": _sb(512, U8), "zt": _sb(512, BF),
+    "ce": _sb(3072, BF), "qe": _sb(768, QX), "se": _sb(768, U8), "zt": _sb(512, BF),
     "kmin": _sb(C, BF), "d0": _sb(C, BF), "mk": _sb(C, F32), "hold": _sb(C, F32), "x16r": _sb(C, BF),
     "cK16": _sb(C, F32), "wrK": _sb(C, F32), "wr3": _sb(2 * C, WD),
-    "dm": _sb(C, BF), "ds": _sb(C, WD), "M": _sb(4 * MWD, BF), "qm": _sb(MWD, QX), "sm": _sb(MWD, U8),
-    "tmpS": _sb(6 * C, BF), "rs": _sb(24, F32), "junk": _sb(2 * C + 2, BF), "jr": _sb(16 * 12 * 23, BF),
+    "dm": _sb(C, BF), "ds": _sb(C, WD), "M": _sb(4 * MWD, BF), "qm": _sb(MWD + 64, QX), "sm": _sb(MWD + 64, U8),
+    "tmpS": _sb(6 * C, BF), "rs": _sb(32, F32), "junk": _sb(2 * C + 2, BF), "jr": _sb(16 * 12 * 23, BF),
     "win": _sb(C + 16, BF), "LJ": _sb(C, WD), "c32": _sb(2 * C, WD), "rev": _sb(C, WD),
     "O": _sb(C, BF), "PI": _sb(C, WD), "wri": _sb(C, WD), "oPI": _sb(24, U16), "al2": _sb(32, F32),
     "c16": _sb(C, BF), "c4": _sb(C, BF), "wr": _sb(C, WD), "wr4": _sb(C, WD), "wrc": _sb(C, WD),
@@ -48,8 +52,8 @@ SCRATCH = {
     "rep": _sb(64, F32), "rpt": _sb(96, F32), "dat": _sb(64, BF), "tpl": _sb(1200, BF), "MW": _sb(1632, BF),
     "Wt": _sb(6 * C, BF), "Pt": _sb(6 * C, BF), "iotaC": _sb(C, BF),
     "plrow": _sb(C, BF), "porow": _sb(C, BF), "PT": _sb(C, BF), "AB": _sb(C, BF),
-    "ABh": _sb(4 * C, BF), "Z": _sb(2 * C, BF), "qz": _sb(192, QX), "sz": _sb(192, U8),
-    "Hpm": _sb(4 * C, BF), "qh": _sb(192, QX), "sh": _sb(192, U8),
+    "ABh": _sb(4 * C, BF), "Z": _sb(2 * C, BF), "qz": _sb(256, QX), "sz": _sb(256, U8),
+    "Hpm": _sb(4 * C, BF), "qh": _sb(256, QX), "sh": _sb(256, U8),
     "WL": _sb(C, BF), "gain": _sb(C, BF), "cat": _sb(2 * C + 16, WD), "LW": _sb(2 * C, BF), "crow": _sb(L, BF),
     "ST": _sb(512, BF), "qs": _sb(256, QX), "ss": _sb(256, U8),
     "pp": _sb(C + 16, BF), "sp": _sb(L, BF), "Dt": _sb(4 * L, BF), "yo": _sb(C, F32),
@@ -184,11 +188,25 @@ def rank_program(g, core, T, topo):
         k, e = (i - 1) // 4, (i - 1) % 4
         return T.M[:, 4 * TO[k] + e:4 * (TO[k] + m):4]
 
-    def qtile(k):
-        a, b = TO[k], TO[k] + TW[k]
-        rd = " ".join("m%d" % i for i in range(4 * k + 1, 4 * k + 5)) + " mz"
-        quant(rd, "qm%d" % k, T.qm[:, a:b], T.sm[:, a:b], T.M[:, 4 * a:4 * b])
+    def sumtile(k):
+        a, b = QO[k], QO[k] + TW[k]
         mm("qb qm%d" % k, "P2", T.P2[:, 0:TW[k]], T.qb[:], T.sb[:], T.qm[:, a:b], T.sm[:, a:b], k == 5, k == 0)
+
+    def qtile(k, now=True):
+        a, b = QO[k], QO[k] + TW[k]
+        rd = " ".join("m%d" % i for i in range(4 * k + 1, 4 * k + 5)) + " mz"
+        quant(rd, "qm%d" % k, T.qm[:, a:b], T.sm[:, a:b], T.M[:, 4 * TO[k]:4 * (TO[k] + TW[k])])
+        if now:
+            sumtile(k)
+
+    def fold(m, k, h, pieces):
+        pb, w = "P%d" % (4 + m), 512 + 128 * h
+        for j in range(pieces):
+            a = QO[k] + 128 * j
+            mm("qf qmz qm%d" % k, pb, T[pb][:, 0:128], T.qe[:, w:w + 128], T.se[:, w:w + 128], T.qm[:, a:a + 128],
+               T.sm[:, a:a + 128], j == 0, j == pieces - 1)
+        act(pb, "pk%d jf%d" % (m, m), T.jr[:, 2048 + 128 * m:2176 + 128 * m], T[pb][:, 0:128], F.Copy,
+            accum_out=T.rs[:, 24 + m:25 + m])
 
     dma("a", "", "ut", T.ut[:], T.u[:])
     dma("s", "", "X", T.X[:], T.x[:])
@@ -215,6 +233,10 @@ def rank_program(g, core, T, topo):
     for b in range(4):
         op("g", "one", "ce%d" % b, lambda: g.affine_select(
             T.ce[:, 512 * b:512 * b + 512], T.one[:], [[-1, 512]], A.is_equal, 0.0, b, 4))
+    for h in range(2):
+        op("g", "ce%d" % (2 * h), "cf%d" % h, lambda: g.affine_select(
+            T.ce[:, 2048 + 512 * h:2560 + 512 * h], T.ce[:, 1024 * h:1024 * h + 512], [[-1, 512]], A.not_equal, FW,
+            2 * h + 1, 4))
     for k in range(3):
         e = 4 * TO[5] + 512 * k
         dma("s", "zt", "mz5" if k == 2 else "", T.M[:, e:e + 512], T.zt[:], "d21")
@@ -288,11 +310,18 @@ def rank_program(g, core, T, topo):
 
     pairc = [lambda: ts("x16r cQ", "k384", T.gain[:], T.x16r[:], col("cQ"), A.is_equal),
              lambda: ts("iotaC", "rev", T.rev[:], T.iotaC[:], -1.0, A.mult, 191.0, A.add),
-             lambda: cp("c16", "c32a", T.c32[:, 1:2 * C:2], T.c16[:]),
-             lambda: tt("k384 rev", "c32b", T.c32[:, 0:C:2], T.gain[:, 0:192], T.rev[:, 0:192], A.mult),
-             lambda: tt("k384 rev", "c32c", T.c32[:, C:2 * C:2], T.gain[:, 192:C], T.rev[:, 192:C], A.mult),
-             lambda: ts("iotaC", "LJ", T.LJ[:, 0:LA], T.iotaC[:, 0:LA], 192.0 + 512.0, A.add),
+             lambda: tt("k384 rev", "LJ", T.LJ[:, 0:LA], T.gain[:, 0:LA], T.rev[:, 0:LA], A.mult),
+             lambda: tt("k384 rev", "c32b", T.c32[:, 2 * LA:2 * C:2], T.gain[:, LA:], T.rev[:, LA:], A.mult),
+             lambda: tt("LJ c16", "c32a", T.c32[:, 1:2 * LA:2], T.LJ[:, 0:LA], T.c16[:, 0:LA], A.add),
+             lambda: cp("c16", "c32c", T.c32[:, 2 * LA + 1:2 * C:2], T.c16[:, LA:]),
+             lambda: cp("zt", "c32d", T.c32[:, 0:2 * LA:2], T.zt[:, 0:LA]),
              lambda: quant("zt", "qs2", T.qs[:, 128:256], T.ss[:, 128:256], T.zt[:])]
+    unit = [lambda k=k: quant("ce%d" % k, "qe%d" % k, T.qe[:, 128 * k:128 * k + 128], T.se[:, 128 * k:128 * k + 128],
+                              T.ce[:, 512 * k:512 * k + 512]) for k in range(4)]
+    unit.append(lambda: quant("cf0 cf1", "qf", T.qe[:, 512:768], T.se[:, 512:768], T.ce[:, 2048:3072]))
+
+    def base():
+        ts("wrc cB1", "base", T.base[:], T.wrc[:, 15:C:16], -384.0, A.mult, col("cB1"), A.add)
 
     def tn(k):
         return T.tn[:, k:k + 1]
@@ -345,37 +374,40 @@ def rank_program(g, core, T, topo):
     lo_mask = sum(1 << e for e in eng[:ne // 2])
     hi_mask = sum(1 << e for e in eng[ne // 2:])
     rid, pid = topo.addr(nxt)[0], topo.addr(nxt)[1]
-    HH = "H0 H1 H2 H3"
+    HH = "H0 H1 H2 H3 H4 H5 H6 H7"
 
     for t in range(R):
         top = 3 + t
         tw = (top + 1) * C
-        quant("X", "qx", T.qx[:], T.sx[:], T.X[:])
-        mm("qr sr qx", "P0", T.P0[:, 0:C], T.qr[:], T.sr[:], T.qx[:], T.sx[:])
-        mm("qr sr qx", "P1", T.P1[:, 0:C], T.qr[:], T.sr[:], T.qx[:], T.sx[:])
+        ns, nv = (NS1, NV1) if t else (NS, NV)
+        e = 16 * (24 - NH)
+        quant("X", "qxh", T.qx[:, e:C], T.sx[:, e:C], T.X[:, 4 * e:])
+        quant("X", "qx", T.qx[:, 0:e], T.sx[:, 0:e], T.X[:, 0:4 * e])
+        mm("qr sr qxh", "P7", T.P7[:, 0:C - e], T.qr[:], T.sr[:], T.qx[:, e:C], T.sx[:, e:C])
+        mm("qr sr qx qxh", "P0", T.P0[:, 0:C], T.qr[:], T.sr[:], T.qx[:], T.sx[:])
+        mm("qr sr qx qxh", "P1", T.P1[:, 0:C], T.qr[:], T.sr[:], T.qx[:], T.sx[:])
         if t == 0:
-            mm("qu qx", "P3", T.P3[:, 0:C], T.qu[:], T.su[:], T.qx[:], T.sx[:])
+            mm("qu qx qxh", "P3", T.P3[:, 0:C], T.qu[:], T.su[:], T.qx[:], T.sx[:])
             ts("x16r", "d0", T.d0[:], T.x16r[:], 0.0, A.is_equal, -2 * BIG, A.mult)
             ts("cQ cT1", "cFL", col("cFL"), col("cQ"), 3.5, A.is_lt, col("cT1"), A.mult)
-            mset("rs0", T.rs[:, 0:1], 0.0)
             ts("ci0", "ci2", T.ci[:, 2:3], T.ci[:, 0:1], 3, A.bitwise_and)
-            ts("ci0", "ci3", T.ci[:, 3:4], T.ci[:, 0:1], 31, A.bitwise_and)
-            mset("ppz", T.pp[:, C:C + 1], -100.0)
-            mset("tpl2", T.tpl[:, 400:800], 0.5)
-            fill = [lambda: mset("rpz", T.rpt[:, 64:96], 0.0),
+            fill = [lambda: cp("ci3", "cP32", col("cP32"), T.ci[:, 3:4]),
+                    lambda: mset("rpz", T.rpt[:, 64:96], 0.0),
                     lambda: ts("one cQ4", "oQ4", T.oQ4[:], T.one[:, 0:24], col("cQ4"), A.mult),
                     lambda: cp("ci3", "oHalf", T.oHalf[:, 0:1], T.ci[:, 3:4]),
                     lambda: mset("oHalf1", T.oHalf[:, 1:2], 64),
                     lambda: ts("cP32 one", "oHalf2", T.oHalf[:, 2:4], T.one[:, 0:2], col("cP32"), A.mult, 32.0, A.add),
-                    ] + pairc[:3] + tables() + pairc[3:]
+                    ] + pairc[:2] + tables() + pairc[2:]
         else:
             wrap16("pp", "", None, T.pp[:, 0:C], C, "wrc")
             fill = tables()
-        e = 16 * (24 - NH)
-        for a, b, h in ((e, C, "hi"), (0, e, "lo")):
-            tt("P0 kmin", "mk" + h, T.mk[:, a:b], T.P0[:, a:b], T.kmin[:, a:b], A.add)
-        for a, b, h in ((e, C, "hi"), (0, e, "lo")):
-            scan("d0 mk" + h, h, T.hold[:, a:b], T.d0[:, a:b], T.mk[:, a:b], 0.0, A.add, A.max)
+        tt("P7 kmin", "mkhi", T.mk[:, e:C], T.P7[:, 0:C - e], T.kmin[:, e:C], A.add)
+        if t > 0:
+            base()
+        else:
+            mset("tpl2", T.tpl[:, 400:800], 0.5)
+        scan("d0 mkhi", "hi", T.hold[:, e:C], T.d0[:, e:C], T.mk[:, e:C], 0.0, A.add, A.max)
+        tt("P0 kmin", "mklo", T.mk[:, 0:e], T.P0[:, 0:e], T.kmin[:, 0:e], A.add)
 
         def pass1(k):
             i = 23 - k
@@ -387,61 +419,95 @@ def rank_program(g, core, T, topo):
             act("tmp%d mz mz5" % k, "m%d rs%d" % (i, i), mrow(i, 16 * i), T.tmpS[:, C * k:C * k + 16 * i], F.Relu,
                 accum_out=T.rs[:, i:i + 1])
         if t == 0:
-            a = TO[5]
-            for k in range(NS):
-                pass1(k)
-            ts("P3 cFL mz5", "m24", mrow(24, C), T.P3[:, 0:C], 0.0, A.is_gt, col("cFL"), A.mult)
-            quant("m21 m22 m23 m24 mz5", "qm5", T.qm[:, a:MWD], T.sm[:, a:MWD], T.M[:, 4 * a:4 * MWD])
-            quant("cb", "qb", T.qb[:], T.sb[:], T.cb[:])
-            mm("qb qm5", "P4", T.P4[:, 0:C], T.qb[:], T.sb[:], T.qm[:, a:MWD], T.sm[:, a:MWD])
-            for k in range(NS):
-                pass2(k)
-            act("P4 ppz", "pp", T.pp[:, 0:C], T.P4[:, 0:C], F.Copy)
-        else:
+            act("P3", "tmp5", T.tmpS[:, 5 * C:], T.P3[:, 0:C], F.Sign)
             pass1(0)
-            for k in range(NS):
-                if k + 1 < NS:
-                    pass1(k + 1)
-                pass2(k)
+            act("tmp5 cFL mz5", "m24", mrow(24, C), T.tmpS[:, 5 * C:], F.Relu, scale=col("cFL"))
+            for k in range(1, NS):
+                pass1(k)
+        else:
+            for ks in (range(ns - 1, 2, -1), range(2, -1, -1)):
+                for k in ks:
+                    pass1(k)
+                for k in ks:
+                    pass2(k)
         if t == 0:
             blank_marks()
-        for i in range(23 - NS, 0, -1):
-            if i == 22 - NS:
+        sums = []
+        for i in range(23 - ns, 0, -1):
+            if i == 22 - ns:
+                scan("d0 mklo", "lo", T.hold[:, 0:e], T.d0[:, 0:e], T.mk[:, 0:e], 0.0, A.add, A.max)
+            if i == 20 - NS and t == 0:
+                mset("rs0", T.rs[:, 0:1], 0.0)
+                ts("ci0", "ci3", T.ci[:, 3:4], T.ci[:, 0:1], 31, A.bitwise_and)
+                mset("ppz", T.pp[:, C:C + 1], -100.0)
+                cp("ci2", "cQ4", col("cQ4"), T.ci[:, 2:3])
+                quant("m21 m22 m23 m24 mz5", "qm5", T.qm[:, QO[5]:], T.sm[:, QO[5]:], T.M[:, 4 * TO[5]:])
+                quant("cb", "qb", T.qb[:], T.sb[:], T.cb[:])
+                mm("qb qm5", "P4", T.P4[:, 0:C], T.qb[:], T.sb[:], T.qm[:, QO[5]:], T.sm[:, QO[5]:])
+                for k in range(NS):
+                    pass2(k)
+                act("P4 ppz", "pp", T.pp[:, 0:C], T.P4[:, 0:C], F.Copy)
+                run(sums, len(sums))
+            if i == (16 if t else 19 - NS):
                 tt("P0 hi lo", "m24", mrow(24, C), T.hold[:], T.P0[:, 0:C], A.is_ge)
             ts("P0 mz " + ("hi" if i >= 24 - NH else "lo"), "m%d" % i, mrow(i, 16 * i), T.P0[:, 0:16 * i],
                T.hold[:, 16 * i + 15:16 * i + 16], A.is_lt)
-            if i > NV:
-                act("m%d" % i, "rs%d jr%d" % (i, i), T.jr[:, 8 * i * (i - 1):8 * i * (i + 1)], mrow(i, 16 * i), F.Copy,
-                    accum_out=T.rs[:, i:i + 1])
-            if i == 17:
+            if nv < i and (t == 0 or i < 13):
+                sums.append(lambda i=i: act("m%d" % i, "rs%d jr%d" % (i, i), T.jr[:, 8 * i * (i - 1):8 * i * (i + 1)],
+                                            mrow(i, 16 * i), F.Copy, accum_out=T.rs[:, i:i + 1]))
+                if t > 0 or i <= 20 - NS:
+                    run(sums, 1)
+                if t > 0 and i < 12:
+                    run(unpack, 2)
+            if i == (15 if t else 13):
                 scan("m24 dm", "ds", T.ds[:], T.dm[:], mrow(24, C), 0.0, A.max, A.subtract)
-            if i == 12:
-                qtile(5)
-                qtile(4)
-            if i == 11:
-                qtile(3)
-            if i == 9 and t == 0:
-                wrap16("pp", "", None, T.pp[:, 0:C], C, "wrc")
-            if i == 8:
-                qtile(2)
+            if t == 0:
+                if i == 12:
+                    qtile(5)
+                    qtile(4)
+                if i == 11:
+                    qtile(3)
+                if i == 9:
+                    wrap16("pp", "", None, T.pp[:, 0:C], C, "wrc")
+                if i == 6:
+                    base()
+            else:
+                if i == 14:
+                    qtile(4, False)
+                    fold(2, 4, 0, 3)
+                if i == 12:
+                    qtile(3, False)
+                    fold(0, 3, 0, 2)
+                    fold(1, 3, 1, 2)
+                    unpack = [lambda: act("pk0 pk1 pk2", "pkb", T.rs[:, 28:31], T.rs[:, 24:27], F.Identity,
+                                          scale=1.0 / FW, bias=ROUND), lambda: None,
+                              lambda: act("pkb", "rs14 rs16 rs18", T.rs[:, 14:19:2], T.rs[:, 28:31], F.Identity,
+                                          bias=-ROUND), lambda: None]
+                    for m in range(3):
+                        a = 13 + 2 * m
+                        unpack.append(lambda m=m, a=a: act(
+                            "rs%d pk%d" % (a + 1, m), "rs%d" % a, T.rs[:, a:a + 1], T.rs[:, a + 1:a + 2], F.Identity,
+                            scale=-FW, bias=T.rs[:, 24 + m:25 + m]))
+                if i == Q5:
+                    qtile(5)
+                    sumtile(4)
+                    sumtile(3)
             if i == 7:
-                ts("wrc cB1", "base", T.base[:], T.wrc[:, 15:C:16], -384.0, A.mult, col("cB1"), A.add)
+                qtile(2)
             if i == 3:
                 tt("base ds", "base", T.base[:], T.base[:], T.ds[:, 15:C:16], A.add)
         qtile(1)
-        qtile(0)
-        for i in range(NV, 0, -1):
+        for i in range(nv, 0, -1):
+            if i == nv - 1:
+                qtile(0)
             op("v", "m%d" % i, "rs%d" % i, lambda: V.tensor_reduce(T.rs[:, i:i + 1], mrow(i, 16 * i), AxisListType.X, A.add))
-        if t == 0:
-            cp("ci2", "cQ4", col("cQ4"), T.ci[:, 2:3])
-            cp("ci3", "cP32", col("cP32"), T.ci[:, 3:4])
         rd = " ".join("rs%d" % i for i in range(24))
         if t == 0:
             for k in range(5):
                 borders(k)
                 run(late, (7, 2, 2, 2, 9)[k])
         run(fill, FV[t][0])
-        tt("base " + rd, "cK16", T.cK16[:, 15:C:16], T.base[:], T.rs[:], A.subtract)
+        tt("base " + rd, "cK16", T.cK16[:, 15:C:16], T.base[:], T.rs[:, 0:24], A.subtract)
         if t == 0:
             act("p40 p41 p42 p43 oQ4", "c4", T.c4[:], T.p4[:, 0:4].indirect(T.oQ4[:]), F.Copy)
         else:
@@ -484,24 +550,50 @@ def rank_program(g, core, T, topo):
             else:
                 act("Xh oAB4", "Bh%d nB%d" % (k, k), bh, src, F.Copy)
         run(fill, FV[t][13])
-        for k, (a, b) in enumerate(ZC):
+
+        def zsum(k):
+            a, b = ZC[k]
             tt("Xh oAB4 Bh%d" % k, "Z%d" % k, T.Z[:, 16 * a:16 * b],
                T.Xh[:].indirect(T.oAB4[:, a:b]), T.ABh[:, 768 + 16 * a:768 + 16 * b], A.add)
-        run(fill, len(fill))
+
+        def layer(h, rd):
+            c = 128 * h
+            quant(rd, "qz%d" % h, T.qz[:, c:c + 128], T.sz[:, c:c + 128], T.Z[:, 256 * h:256 * h + 512])
+            for b in range(4):
+                pb = "P%d" % (4 - 4 * h + b)
+                mm("qw qz%d" % h, pb, T[pb][:, 0:128], T.qw[:, 128 * b:128 * b + 128],
+                   T.sw[:, 128 * b:128 * b + 128], T.qz[:, c:c + 128], T.sz[:, c:c + 128])
+
+        def verdicts(h, rd):
+            c, pb = 128 * h, "P%d" % (4 + h)
+            quant(rd, "qh%d" % h, T.qh[:, c:c + 128], T.sh[:, c:c + 128], T.Hpm[:, 256 * h:256 * h + 512])
+            mm("qr sr qh%d" % h, pb, T[pb][:, 0:128], T.qr[:], T.sr[:], T.qh[:, c:c + 128], T.sh[:, c:c + 128])
+
+        def flags(h):
+            a, b, pb = 128 * h, 128 + 64 * h, "P%d" % (4 + h)
+            ts(pb, "WL0%d" % h, T.WL[:, a:b], T[pb][:, 64 * h:128], 0.0, A.is_gt)
+            ts(pb, "WL1%d" % h, T.WL[:, 192 + a:192 + b], T[pb][:, 64 * h:128], 0.0, A.is_le)
+        for k in range(3):
+            zsum(k)
+        wrap4("porow", "", None, T.porow[:], C)
         act("Xh oAB4", "Ah", T.ABh[:, 0:768], T.Xh[:].indirect(T.oAB4[:, 0:48]), F.Copy)
-        quant("Z0 Z1 Z2 Z3", "qz", T.qz[:], T.sz[:], T.Z[:])
+        layer(0, "Z0 Z1 Z2")
+        zsum(3)
+        ts("wr4 cO4", "oPos4", T.oPos4[:], T.wr4[:, 3:C:4], 4.0, A.mult, col("cO4"), A.add)
+        run(fill, len(fill))
+        layer(1, "Z1 Z2 Z3")
+        wrap16("PT", "oPP", T.oPP[:], T.PT[:], C, "wrc")
         for b in range(4):
-            mm("qw qz", "P%d" % (4 + b), T["P%d" % (4 + b)][:, 0:192], T.qw[:, 128 * b:128 * b + 128],
-               T.sw[:, 128 * b:128 * b + 128], T.qz[:], T.sz[:])
-        wrap4("porow", "oPos4", T.oPos4[:], T.porow[:], C)
+            act("P%d" % (4 + b), "H%d" % b, T.Hpm[:, b:512:4], T["P%d" % (4 + b)][:, 0:128], F.Identity, scale=0.03125)
+        verdicts(0, "H0 H1 H2 H3")
         for b in range(4):
-            pb = "P%d" % (4 + b)
+            pb = "P%d" % b
             if b % 2 == 0:
-                act(pb, "H%d" % b, T.Hpm[:, b:768:4], T[pb][:, 0:192], F.Identity, scale=0.03125)
+                act(pb, "H%d" % (4 + b), T.Hpm[:, 512 + b:768:4], T[pb][:, 64:128], F.Identity, scale=0.03125)
             else:
-                ts(pb, "H%d" % b, T.Hpm[:, b:768:4], T[pb][:, 0:192], 0.03125, A.mult)
-        quant(HH, "qh", T.qh[:], T.sh[:], T.Hpm[:, 0:768])
-        mm("qr sr qh", "P3", T.P3[:, 0:192], T.qr[:], T.sr[:], T.qh[:], T.sh[:])
+                ts(pb, "H%d" % (4 + b), T.Hpm[:, 512 + b:768:4], T[pb][:, 64:128], 0.03125, A.mult)
+        verdicts(1, HH)
+        flags(0)
         act(HH, "Hh", T.Hpm[:, 768:1536], T.Hpm[:, 0:768], F.Identity, scale=0.5)
         dma("g", "Hh Ah", "Ah", T.ABh[:, 0:768], T.Hpm[:, 768:1536], "ga", accum_op=A.add)
 
@@ -509,11 +601,9 @@ def rank_program(g, core, T, topo):
             a = 768 + 192 * k
             tt("Hh Bh0 Bh1 Bh2 Bh3 Z0 Z1 Z2 Z3", "nB%d" % k, T.ABh[:, a:a + 192], T.ABh[:, a:a + 192],
                T.Hpm[:, a:a + 192], A.subtract)
-        wrap16("PT", "oPP", T.oPP[:], T.PT[:], C, "wrc")
-        ts("P3", "WL0", T.WL[:, 0:192], T.P3[:, 0:192], 0.0, A.is_gt)
-        ts("P3", "WL1", T.WL[:, 192:C], T.P3[:, 0:192], 0.0, A.is_le)
-        cp("WL0 WL1 oPP", "win", T.win[:, 16:208], T.WL[:].indirect(T.oPP[:, 0:12]))
-        act("WL0 WL1 oPP", "win2", T.win[:, 208:C + 16], T.WL[:].indirect(T.oPP[:, 12:24]), F.Copy)
+        flags(1)
+        cp("WL00 WL01 WL10 WL11 oPP", "win", T.win[:, 16:208], T.WL[:].indirect(T.oPP[:, 0:12]))
+        act("WL00 WL01 WL10 WL11 oPP", "win2", T.win[:, 208:C + 16], T.WL[:].indirect(T.oPP[:, 12:24]), F.Copy)
         act("win win2 oP", "gain k384", T.gain[:], T.win[:, 16:C + 16].indirect(T.oP[:]), F.Copy)
         dma("g", "gain pp", "pp", T.pp[:, 0:C], T.gain[:], "gb", accum_op=A.add)
         newb(0)
@@ -521,15 +611,20 @@ def rank_program(g, core, T, topo):
              A.min, A.subtract)
         scan("MW win win2", "om", T.cat[:, 2 * C:0:-2], T.MW[:, C:0:-1], T.win[:, C + 15:15:-1], 0.0,
              A.mult, A.subtract)
-        tt("win win2 la LJ", "lw", T.cat[:, 3:2 * C + 2:2], T.win[:, 16:C + 16], T.LJ[:], A.mult)
+        ts("win win2", "lw0", T.cat[:, 3:2 * LA + 2:2], T.win[:, 16:LA + 16], 640.0, A.mult, 256.0, A.subtract)
+        tt("win2 la", "lw", T.cat[:, 2 * LA + 3:2 * C + 2:2], T.win[:, LA + 16:C + 16], T.LJ[:, LA:], A.mult)
         newb(1)
-        scan("om lw c32a c32b c32c", "wr3", T.wr3[:], T.cat[:, 2:2 * C + 2], T.c32[:], -2048.0, A.max, A.add)
+        scan("om lw0 lw c32a c32b c32c c32d", "wr3", T.wr3[:], T.cat[:, 2:2 * C + 2], T.c32[:], -2048.0, A.max, A.add)
         newb(2)
         ts("wr3 cO", "oL", T.oL[:], T.wr3[:, 31:2 * C:32], col("cO"), A.subtract)
         newb(3)
         cp("oL PT", "LW", T.LW[:].indirect(T.oL[:]), T.PT[:])
-        wrap4("LW", "oL4", T.oL4[:], T.LW[:, 0:L], L)
+        run(unit, 1)
+        wrap4("LW", "", None, T.LW[:, 0:L], L)
         wrap16("LW", "", None, T.LW[:, 0:L], L)
+        run(unit, 1)
+        ts("wr4 cO4", "oL4", T.oL4[:], T.wr4[:, 3:L:4], 4.0, A.mult, col("cO4"), A.add)
+        run(unit, 1)
         NB = "Ah nB0 nB1 nB2 nB3 "
         act(NB + "oL4", "ST0", T.ST[:, 0:128], T.ABh[:].indirect(T.oL4[:, 0:8]), F.Identity, scale=2.0)
         ts(NB + "oL4", "ST1", T.ST[:, 128:256], T.ABh[:].indirect(T.oL4[:, 8:16]), 2.0, A.mult)
@@ -548,6 +643,7 @@ def rank_program(g, core, T, topo):
         lastw["land%d" % t] = ("arc%d" % t, ne_in)
         lastw["lp%d" % t] = ("arp%d" % t, ne_in)
         total["arc%d" % t] = total["arp%d" % t] = ne_in
+        run(unit, 2)
         wrap16("crow", "oC16", T.oC16[:], T.crow[:], L)
         act("pp oC16", "sp", T.sp[:], T.pp[:, 0:C].indirect(T.oC16[:]), F.Copy)
         deps("g", ["sp"], [])
@@ -558,9 +654,10 @@ def rank_program(g, core, T, topo):
         if t == 0:
             quant("zt", "zl0", T.ql0[:, 0:128], T.sl0[:, 0:128], T.zt[:])
         ts(NB + "oPos4", "X", T.X[:, HX:], T.ABh[:].indirect(T.oPos4[:, HX // 16:]), 2.0, A.mult)
-        act(NB + "oPos4 Xh qx", "Xa", T.X[:, 0:HX], T.ABh[:].indirect(T.oPos4[:, 0:HX // 16]), F.Identity, scale=2.0)
+        act(NB + "oPos4 Xh qx qxh", "Xa", T.X[:, 0:HX], T.ABh[:].indirect(T.oPos4[:, 0:HX // 16]), F.Identity, scale=2.0)
         if t == 0:
-            quant("ce0 ce1 ce2 ce3", "qe", T.qe[:], T.se[:], T.ce[:])
+            a = QO[5] - 128
+            quant("zt", "qm4 qmz", T.qm[:, a:a + 128], T.sm[:, a:a + 128], T.zt[:])
         if t == 1:
             quant("vt", "qv", T.qv[:], T.sv[:], T.vt[:])
         if t + 1 < R:
@@ -571,19 +668,14 @@ def rank_program(g, core, T, topo):
         ql, sl = T["ql%d" % t], T["sl%d" % t]
         for b in range(4):
             pb = "P%d" % (4 + b)
-            mm("qe zl%d land%d" % (t, t), pb, T[pb][:, 0:128], T.qe[:, 128 * b:128 * b + 128],
+            mm("qe%d zl%d land%d" % (b, t, t), pb, T[pb][:, 0:128], T.qe[:, 128 * b:128 * b + 128],
                T.se[:, 128 * b:128 * b + 128], ql[:, 64:192], sl[:, 64:192])
         for b in range(4):
             pb = "P%d" % (4 + b)
-            if b != 1:
-                act(pb, "D%d" % b, T.Dt[:, L * b:L * b + L], T[pb][:, 64:128], F.Copy)
-            else:
-                cp(pb, "D%d" % b, T.Dt[:, L * b:L * b + L], T[pb][:, 64:128])
-        for b in (0, 2):
-            cp("D%d D%d oC4%d oC4%d X Xa" % (b, b + 1, b, b + 1), "X", T.X[:].indirect(T.oC4[:, 4 * b:4 * b + 8]),
-               T.Dt[:, L * b:L * b + 2 * L])
-            if b == 0:
-                cp("lp%d oC16 pp" % t, "pp", T.pp[:, 0:C].indirect(T.oC16[:]), T["lp%d" % t][:])
+            act(pb, "D%d" % b, T.Dt[:, L * b:L * b + L], T[pb][:, 64:128], F.Copy)
+        cp("D0 oC40 X Xa", "X", T.X[:].indirect(T.oC4[:, 0:4]), T.Dt[:, 0:L])
+        cp("lp%d oC16 pp" % t, "pp", T.pp[:, 0:C].indirect(T.oC16[:]), T["lp%d" % t][:])
+        cp("D1 D2 D3 oC41 oC42 oC43 X", "X", T.X[:].indirect(T.oC4[:, 4:16]), T.Dt[:, L:])
         if t + 1 < R:
             for k in range(5):
                 borders(k)
@@ -591,7 +683,7 @@ def rank_program(g, core, T, topo):
     dma("g", "pp", "", T.pts[:], T.pp[0:128:16, 0:C], "go")
     for k in range(3):
         a, b = 128 * k, 128 * k + 128
-        quant("X", "qx qx%d" % k if k == 0 else "qx%d" % k, T.qx[:, a:b], T.sx[:, a:b], T.X[:, 4 * a:4 * b])
+        quant("X", "qx qxh qx0" if k == 0 else "qx%d" % k, T.qx[:, a:b], T.sx[:, a:b], T.X[:, 4 * a:4 * b])
         mm("qv qx%d" % k, "P%d" % k, T["P%d" % k][:, 0:128], T.qv[:], T.sv[:], T.qx[:, a:b], T.sx[:, a:b])
     dma("s", "qx0 qx1 qx2", "", T.oc[:], T.qx[:].bitcast(dt.uint8))
     for k in range(4):

@@ -1,4 +1,3 @@
-from concourse.bass import DstId, RemoteDMATransfer
 from concourse.mybir import dt, AluOpType, ActivationFunctionType, AxisListType
 
 A = AluOpType
@@ -6,21 +5,22 @@ F = ActivationFunctionType
 C, L, R = 384, 64, 3
 BIG = 1e29
 WD = "float16"
-HX = 768
+HX = 1280
+NL = 128
 LA = 256
 FV = [(3, 3, 1, 1, 5, 1, 1, 2, 1, 1, 1, 1, 1, 1), (3, 2, 1, 0, 1, 2, 1, 1, 1, 0, 0, 0, 0, 0)]
 FV.append(FV[1])
 NH = 8
-NV = 6
+NV = 7
 NS = 4
-NS1, NV1, Q5 = 5, 6, 8
+NS1, NV1, Q5 = 5, 5, 8
 TW = [128, 128, 192, 256, 320, 384]
 TO = [sum(TW[:k]) for k in range(6)]
 QO = TO[:5] + [TO[5] + 64]
 MWD = sum(TW)
 FW = 1024.0
 ROUND = 12582912.0
-ZC = [(0, 8), (8, 20), (20, 32), (32, 48)]
+ZC = [(16, 24), (24, 36), (36, 48), (0, 8), (8, 16)]
 
 
 def _sb(n, d):
@@ -38,7 +38,7 @@ SCRATCH = {
     "kmin": _sb(C, BF), "d0": _sb(C, BF), "mk": _sb(C, F32), "hold": _sb(C, F32), "x16r": _sb(C, BF),
     "cK16": _sb(C, F32), "wrK": _sb(C, F32), "wr3": _sb(2 * C, WD),
     "dm": _sb(C, BF), "ds": _sb(C, WD), "M": _sb(4 * MWD, BF), "qm": _sb(MWD + 64, QX), "sm": _sb(MWD + 64, U8),
-    "tmpS": _sb(6 * C, BF), "rs": _sb(32, F32), "junk": _sb(2 * C + 2, BF), "jr": _sb(16 * 12 * 23, BF),
+    "tmpS": _sb(6 * C, BF), "rs": _sb(32, F32), "junk": _sb(2 * C + 2 + 4 * L, BF), "jr": _sb(16 * 12 * 23, BF),
     "win": _sb(C + 16, BF), "LJ": _sb(C, WD), "c32": _sb(2 * C, WD), "rev": _sb(C, WD),
     "O": _sb(C, BF), "PI": _sb(C, WD), "wri": _sb(C, WD), "oPI": _sb(24, U16), "al2": _sb(32, F32),
     "c16": _sb(C, BF), "c4": _sb(C, BF), "wr": _sb(C, WD), "wr4": _sb(C, WD), "wrc": _sb(C, WD),
@@ -48,28 +48,24 @@ SCRATCH = {
     "oK": _sb(24, U16), "oP": _sb(24, U16), "oPos4": _sb(96, U16), "oAB4": _sb(96, U16),
     "oPP": _sb(24, U16), "oL": _sb(24, U16), "oL4": _sb(16, U16), "oL16": _sb(4, U16), "oC4": _sb(16, U16),
     "oC16": _sb(4, U16), "oM": _sb(4, U16),
-    "base": _sb(24, F32), "cnt": _sb(2, F32), "tn": _sb(20, F32),
+    "base": _sb(24, F32), "cnt": _sb(8, F32), "tn": _sb(20, F32),
     "rep": _sb(64, F32), "rpt": _sb(96, F32), "dat": _sb(64, BF), "tpl": _sb(1200, BF), "MW": _sb(1632, BF),
     "Wt": _sb(6 * C, BF), "Pt": _sb(6 * C, BF), "iotaC": _sb(C, BF),
     "plrow": _sb(C, BF), "porow": _sb(C, BF), "PT": _sb(C, BF), "AB": _sb(C, BF),
-    "ABh": _sb(4 * C, BF), "Z": _sb(2 * C, BF), "qz": _sb(256, QX), "sz": _sb(256, U8),
-    "Hpm": _sb(4 * C, BF), "qh": _sb(256, QX), "sh": _sb(256, U8),
+    "AB4": _sb(4 * C, BF), "Bh": _sb(2 * C, BF), "Z": _sb(2 * C, BF), "qz": _sb(512, QX), "sz": _sb(512, U8),
+    "Hpm": _sb(2 * C, BF), "qh": _sb(256, QX), "sh": _sb(256, U8),
     "WL": _sb(C, BF), "gain": _sb(C, BF), "cat": _sb(2 * C + 16, WD), "LW": _sb(2 * C, BF), "crow": _sb(L, BF),
-    "ST": _sb(512, BF), "qs": _sb(256, QX), "ss": _sb(256, U8),
-    "pp": _sb(C + 16, BF), "sp": _sb(L, BF), "Dt": _sb(4 * L, BF), "yo": _sb(C, F32),
+    "ql": _sb(256 * R, QX), "sl": _sb(256 * R, U8), "lo": _sb(16 * R, U16), "lp": _sb(L * R, BF),
+    "Df": _sb(1024, BF), "oR": _sb(4, U16), "pp": _sb(C + 16, BF), "sp": _sb(3 * L, BF), "Dt": _sb(4 * L, BF), "yo": _sb(C, F32),
 }
-for _t in range(R):
-    SCRATCH["ql%d" % _t] = _sb(192, QX)
-    SCRATCH["sl%d" % _t] = _sb(384, U8)
-    SCRATCH["lp%d" % _t] = _sb(L, BF)
 for _b in range(8):
     SCRATCH["P%d" % _b] = ("psum", [128, 512], F32)
 
 NDMA = 24
-SEMAPHORES = (["nv", "na", "np_", "ng", "ls", "gw", "go", "ga", "gb"] + ["d%d" % k for k in range(NDMA)]
-              + ["arc%d" % t for t in range(R)] + ["arp%d" % t for t in range(R)])
+SEMAPHORES = (["nv", "na", "np_", "ng", "ls"] + ["d%d" % k for k in range(NDMA)]
+              + [s + str(t) for s in ("ara", "arb", "arl", "arp") for t in range(R)])
 NAMES = ("cQ cQM cO cOC cH cHM cQ4 cO4 cFL cR1 cR2 cK cTH cTL cNF cMID cBE cTHE cGJ cJ cEP "
-         "cB1 cX1 cT1 cT2 cT3 cM1 cM2 cQ5 cN1 cN2 cJ2 cO16 cJN cYA cYB cJA cJB cP32").split()
+         "cB1 cX1 cT1 cT2 cT3 cM1 cM2 cQ5 cN1 cN2 cJ2 cO16 cJN cYA cYB cJA cJB cP32 cO5").split()
 
 
 def rank_program(g, core, T, topo):
@@ -81,7 +77,7 @@ def rank_program(g, core, T, topo):
     V, S, P = g.vector, g.scalar, g.tensor
     Q = {"v": V, "a": S, "p": P, "g": g, "s": g.sync}
     CS = {"v": "nv", "a": "na", "p": "np_", "g": "ng"}
-    total, lastw, readers = {}, {}, {}
+    total, lastw, readers, behind = {}, {}, {}, {}
     waited = {q: {} for q in Q}
     ndma = [0]
 
@@ -89,6 +85,8 @@ def rank_program(g, core, T, topo):
         if waited[q].get(tok[0], 0) < tok[1]:
             Q[q].wait_ge(T.sem[tok[0]], tok[1])
             waited[q][tok[0]] = tok[1]
+            for s, v in behind.get(tok, {}).items():
+                waited[q][s] = max(waited[q].get(s, 0), v)
 
     def deps(q, reads, writes):
         need = {}
@@ -104,7 +102,7 @@ def rank_program(g, core, T, topo):
         for t in toks:
             if t is not None:
                 need[t[0]] = max(need.get(t[0], 0), t[1])
-        for s in need:
+        for s in sorted(need, key=lambda s: -len(behind.get((s, need[s]), ()))):
             wait(q, (s, need[s]))
 
     def note(tok, reads, writes):
@@ -120,6 +118,7 @@ def rank_program(g, core, T, topo):
         s = CS[q]
         total[s] = total.get(s, 0) + 1
         fn().then_inc(T.sem[s], 1)
+        behind[(s, total[s])] = dict(waited[q])
         note((s, total[s]), reads, writes)
 
     def dma(q, reads, writes, out, in_, sem=None, **kw):
@@ -199,6 +198,9 @@ def rank_program(g, core, T, topo):
         if now:
             sumtile(k)
 
+    def rowsum(i):
+        op("v", "m%d" % i, "rs%d" % i, lambda: V.tensor_reduce(T.rs[:, i:i + 1], mrow(i, 16 * i), AxisListType.X, A.add))
+
     def fold(m, k, h, pieces):
         pb, w = "P%d" % (4 + m), 512 + 128 * h
         for j in range(pieces):
@@ -209,24 +211,24 @@ def rank_program(g, core, T, topo):
             accum_out=T.rs[:, 24 + m:25 + m])
 
     dma("a", "", "ut", T.ut[:], T.u[:])
-    dma("s", "", "X", T.X[:], T.x[:])
+    dma("s", "", "X2", T.X[:, 1024:], T.x[:, 1024:])
+    dma("s", "", "X1", T.X[:, 512:1024], T.x[:, 512:1024])
+    dma("s", "", "X", T.X[:, 0:512], T.x[:, 0:512])
     iota("ci0", T.ci[:, 0:1], [[0, 1]], 0, 1, False)
     iota("ci8", T.ci[:, 8:16], [[16, 8]], 0, 0, False)
     iota("x16", T.x16[:], [[1, 16]], 0, 0)
     iota("x16r", T.x16r[:], [[0, 24], [1, 16]], 0, 0)
     mset("zt", T.zt[:], 0.0)
     ts("ci0", "ci1", T.ci[:, 1:2], T.ci[:, 0:1], 15, A.bitwise_and)
-    cp("ci8", "oRep", T.oRep[:], T.ci[:, 8:16])
+    mset("one", T.one[:], 1.0)
     cp("ci1", "cQ", col("cQ"), T.ci[:, 1:2])
+    mset("tpl2", T.tpl[:, 400:800], 0.5)
     ts("cQ", "cT1", col("cT1"), col("cQ"), 0.0, A.is_gt)
     ts("cQ", "cR1", col("cR1"), col("cQ"), 4.5, A.is_gt)
     ts("cQ", "cR2", col("cR2"), col("cQ"), 10.5, A.is_gt)
-    mset("one", T.one[:], 1.0)
     op("g", "one", "cb", lambda: g.affine_select(T.cb[:], T.one[:], [[-16, 8], [0, 64]], A.is_ge, 0.0, 0, 1))
     op("g", "cb", "cb", lambda: g.affine_select(T.cb[:], T.cb[:], [[16, 8], [0, 64]], A.is_ge, 0.0, 15, -1))
     iota("dm", T.dm[:], [[16, 24], [-512, 16]], 0, 0)
-    dma("g", "", "", T.qw[:].bitcast(dt.uint8), T.wc[:], "gw")
-    dma("g", "", "qw", T.sw[:], T.ws[:], "gw")
     iota("tpl", T.tpl[:, 0:400], [[0, 400]], 1, 0)
     iota("tpl3", T.tpl[:, 800:1200], [[0, 400]], 512, 0)
     iota("iotaC", T.iotaC[:], [[1, C]], -192, 0)
@@ -246,19 +248,25 @@ def rank_program(g, core, T, topo):
         dma("s", "zt", "mz" if k == 4 else "", T.M[:, e - 192:e], T.zt[:, 0:192], "d23")
 
     ts("x16 cQ", "k16", T.k16[:], T.x16[:], col("cQ"), A.is_equal)
+    cp("ci8", "oRep", T.oRep[:], T.ci[:, 8:16])
+    ts("one cQ", "oQ", T.oQ[:], T.one[:, 0:24], col("cQ"), A.mult)
+    ts("ci0", "ci2", T.ci[:, 2:3], T.ci[:, 0:1], 3, A.bitwise_and)
     ts("k16", "p16", T.p16[:], T.k16[:], 1024.0, A.mult)
     ts("k16", "t16a", T.t16[:, 0:15], T.k16[:, 1:16], -2048.0, A.mult)
     ts("k16", "t16b", T.t16[:, 15:16], T.k16[:, 0:1], -2048.0, A.mult)
-    ts("one cQ", "oQ", T.oQ[:], T.one[:, 0:24], col("cQ"), A.mult)
-    tt("p16 t16a t16b", "p16", T.p16[:], T.p16[:], T.t16[:], A.add)
-    quant("ut", "qu", T.qu[:], T.su[:], T.ut[:])
     ts("x16r cQ", "kmin", T.kmin[:], T.x16r[:], col("cQ"), A.not_equal, -2 * BIG, A.mult)
-    cp("qu oRep", "qr", T.qr[:].bitcast(dt.uint32), T.qu[:].bitcast(dt.uint32).indirect(T.oRep[:]))
+    tt("p16 t16a t16b", "p16", T.p16[:], T.p16[:], T.t16[:], A.add)
+    ts("x16r", "d0", T.d0[:], T.x16r[:], 0.0, A.is_equal, -2 * BIG, A.mult)
+    quant("ut", "qu", T.qu[:], T.su[:], T.ut[:])
+
+    def pick_u():
+        cp("qu oRep", "qr", T.qr[:].bitcast(dt.uint32), T.qu[:].bitcast(dt.uint32).indirect(T.oRep[:]))
     for k in range(3):
-        dma("s", "zt", "", T.Wt[:, 512 * k:512 * k + 512], T.zt[:], "d20")
+        dma("s", "zt X X1 X2", "", T.Wt[:, 512 * k:512 * k + 512], T.zt[:], "d20")
     dma("s", "zt", "", T.LW[:, 0:512], T.zt[:], "d20")
-    dma("s", "zt", "", T.LW[:, 512:768], T.zt[:, 0:256], "d20")
-    dma("s", "zt", "Wt LW STz", T.ST[:, 256:512], T.zt[:, 0:256], "d20")
+    dma("s", "zt", "Wt LW", T.LW[:, 512:768], T.zt[:, 0:256], "d20")
+    dma("s", "", "", T.qw[:].bitcast(dt.uint8), T.wc[:], "d22")
+    dma("s", "", "qw", T.sw[:], T.ws[:], "d22")
     dma("s", "", "vt", T.vt[:], T.v[:])
     lin("cH", "cQ", -1.0, 15.0)
     lin("cO", "cT1", 2048.0, -1024.0)
@@ -288,7 +296,6 @@ def rank_program(g, core, T, topo):
     act("p16 oQ", "c16", T.c16[:, 0:C], T.p16[:].indirect(T.oQ[:]), F.Copy)
     act("one cNF", "al32", T.al32[:], T.one[:, 0:32], F.Identity, scale=col("cNF"))
     act("p16 cB1", "cB1", col("cB1"), T.p16[:, 15:16], F.Identity, scale=16.0, bias=col("cB1"))
-    act("c16", "cK16", T.cK16[:], T.c16[:, 0:C], F.Identity, scale=16.0)
 
     def run(calls, k):
         for _ in range(min(k, len(calls))):
@@ -307,6 +314,7 @@ def rank_program(g, core, T, topo):
     for k in range(4):
         late.append(lambda k=k: act("t16a", "p4%d" % k, T.p4[:, k:k + 1], T.t16[:, (k + 1) % 4:(k + 1) % 4 + 1],
                                     F.Identity, scale=-2.0, bias=T.t16[:, k:k + 1]))
+    late.append(lambda: lin("cO5", "cO4", 1.0, -4.0 * NL))
 
     pairc = [lambda: ts("x16r cQ", "k384", T.gain[:], T.x16r[:], col("cQ"), A.is_equal),
              lambda: ts("iotaC", "rev", T.rev[:], T.iotaC[:], -1.0, A.mult, 191.0, A.add),
@@ -314,8 +322,7 @@ def rank_program(g, core, T, topo):
              lambda: tt("k384 rev", "c32b", T.c32[:, 2 * LA:2 * C:2], T.gain[:, LA:], T.rev[:, LA:], A.mult),
              lambda: tt("LJ c16", "c32a", T.c32[:, 1:2 * LA:2], T.LJ[:, 0:LA], T.c16[:, 0:LA], A.add),
              lambda: cp("c16", "c32c", T.c32[:, 2 * LA + 1:2 * C:2], T.c16[:, LA:]),
-             lambda: cp("zt", "c32d", T.c32[:, 0:2 * LA:2], T.zt[:, 0:LA]),
-             lambda: quant("zt", "qs2", T.qs[:, 128:256], T.ss[:, 128:256], T.zt[:])]
+             lambda: cp("zt", "c32d", T.c32[:, 0:2 * LA:2], T.zt[:, 0:LA])]
     unit = [lambda k=k: quant("ce%d" % k, "qe%d" % k, T.qe[:, 128 * k:128 * k + 128], T.se[:, 128 * k:128 * k + 128],
                               T.ce[:, 512 * k:512 * k + 512]) for k in range(4)]
     unit.append(lambda: quant("cf0 cf1", "qf", T.qe[:, 512:768], T.se[:, 512:768], T.ce[:, 2048:3072]))
@@ -326,14 +333,17 @@ def rank_program(g, core, T, topo):
     def tn(k):
         return T.tn[:, k:k + 1]
 
+    def count(rd, row, j, k):
+        c, a = ("cTH", "cTL")[k], (2 * (C + 1) + L * (j - 2 + k) if j else (C + 1) * k)
+        act(rd + " " + c, "junk%d cnt%d" % (j + k, j + k), T.junk[:, a:a + row.shape[1]], row, F.Sign, bias=col(c),
+            accum_out=T.cnt[:, j + k:j + k + 1])
+
     def borders(k):
         if k == 0:
-            act("pp cTH", "junk0 cnt0", T.junk[:, 0:C + 1], T.pp[:, 0:C + 1], F.Sign, bias=col("cTH"),
-                accum_out=T.cnt[:, 0:1])
-            act("pp cTL", "junk1 cnt1", T.junk[:, C + 1:], T.pp[:, 0:C + 1], F.Sign, bias=col("cTL"),
-                accum_out=T.cnt[:, 1:2])
+            count("pp", T.pp[:, 0:C + 1], 0, 0)
+            count("pp", T.pp[:, 0:C + 1], 0, 1)
         if k == 1:
-            act("cnt0 cnt1 cM1", "tn2", T.tn[:, 2:4], T.cnt[:], F.Identity, scale=0.5, bias=col("cM1"))
+            act("cnt0 cnt1 cM1", "tn2", T.tn[:, 2:4], T.cnt[:, 0:2], F.Identity, scale=0.5, bias=col("cM1"))
         if k == 2:
             act("tn2 cM2", "tn4", T.tn[:, 4:6], T.tn[:, 2:4], F.Identity, bias=col("cM2"))
         if k == 3:
@@ -369,10 +379,8 @@ def rank_program(g, core, T, topo):
         g.sync.dma_start(T.MW[:, 1200:1600], T.tpl[:, 400:800]).then_inc(T.sem.d19, 16)
         note(("d19", total["d19"]), ["tpl2"], ["MW"])
 
-    eng = topo.engines(core, nxt)
-    ne, ne_in = len(eng), len(topo.engines(prv, core))
-    lo_mask = sum(1 << e for e in eng[:ne // 2])
-    hi_mask = sum(1 << e for e in eng[ne // 2:])
+    mask = topo.mask(core, nxt)
+    ne, ne_in = len(topo.engines(core, nxt)), len(topo.engines(prv, core))
     rid, pid = topo.addr(nxt)[0], topo.addr(nxt)[1]
     HH = "H0 H1 H2 H3 H4 H5 H6 H7"
 
@@ -381,16 +389,21 @@ def rank_program(g, core, T, topo):
         tw = (top + 1) * C
         ns, nv = (NS1, NV1) if t else (NS, NV)
         e = 16 * (24 - NH)
-        quant("X", "qxh", T.qx[:, e:C], T.sx[:, e:C], T.X[:, 4 * e:])
-        quant("X", "qx", T.qx[:, 0:e], T.sx[:, 0:e], T.X[:, 0:4 * e])
+        if t == 0:
+            quant("X2", "qxh", T.qx[:, e:C], T.sx[:, e:C], T.X[:, 4 * e:])
+            pick_u()
+            quant("X1", "", T.qx[:, 128:e], T.sx[:, 128:e], T.X[:, 512:4 * e])
+            quant("X", "qx", T.qx[:, 0:128], T.sx[:, 0:128], T.X[:, 0:512])
+        else:
+            quant("X", "qxh", T.qx[:, e:C], T.sx[:, e:C], T.X[:, 4 * e:])
+            quant("X", "qx", T.qx[:, 0:e], T.sx[:, 0:e], T.X[:, 0:4 * e])
         mm("qr sr qxh", "P7", T.P7[:, 0:C - e], T.qr[:], T.sr[:], T.qx[:, e:C], T.sx[:, e:C])
         mm("qr sr qx qxh", "P0", T.P0[:, 0:C], T.qr[:], T.sr[:], T.qx[:], T.sx[:])
         mm("qr sr qx qxh", "P1", T.P1[:, 0:C], T.qr[:], T.sr[:], T.qx[:], T.sx[:])
         if t == 0:
             mm("qu qx qxh", "P3", T.P3[:, 0:C], T.qu[:], T.su[:], T.qx[:], T.sx[:])
-            ts("x16r", "d0", T.d0[:], T.x16r[:], 0.0, A.is_equal, -2 * BIG, A.mult)
             ts("cQ cT1", "cFL", col("cFL"), col("cQ"), 3.5, A.is_lt, col("cT1"), A.mult)
-            ts("ci0", "ci2", T.ci[:, 2:3], T.ci[:, 0:1], 3, A.bitwise_and)
+            ts("ci0", "ci3", T.ci[:, 3:4], T.ci[:, 0:1], 31, A.bitwise_and)
             fill = [lambda: cp("ci3", "cP32", col("cP32"), T.ci[:, 3:4]),
                     lambda: mset("rpz", T.rpt[:, 64:96], 0.0),
                     lambda: ts("one cQ4", "oQ4", T.oQ4[:], T.one[:, 0:24], col("cQ4"), A.mult),
@@ -399,13 +412,15 @@ def rank_program(g, core, T, topo):
                     lambda: ts("cP32 one", "oHalf2", T.oHalf[:, 2:4], T.one[:, 0:2], col("cP32"), A.mult, 32.0, A.add),
                     ] + pairc[:2] + tables() + pairc[2:]
         else:
-            wrap16("pp", "", None, T.pp[:, 0:C], C, "wrc")
+            run(points, 1)
             fill = tables()
         tt("P7 kmin", "mkhi", T.mk[:, e:C], T.P7[:, 0:C - e], T.kmin[:, e:C], A.add)
         if t > 0:
-            base()
+            wrap16("pp", "", None, T.pp[:, 0:C], C, "wrc")
         else:
-            mset("tpl2", T.tpl[:, 400:800], 0.5)
+            mset("rs0", T.rs[:, 0:1], 0.0)
+            mset("ppz", T.pp[:, C:C + 1], -100.0)
+            cp("ci2", "cQ4", col("cQ4"), T.ci[:, 2:3])
         scan("d0 mkhi", "hi", T.hold[:, e:C], T.d0[:, e:C], T.mk[:, e:C], 0.0, A.add, A.max)
         tt("P0 kmin", "mklo", T.mk[:, 0:e], T.P0[:, 0:e], T.kmin[:, 0:e], A.add)
 
@@ -419,11 +434,13 @@ def rank_program(g, core, T, topo):
             act("tmp%d mz mz5" % k, "m%d rs%d" % (i, i), mrow(i, 16 * i), T.tmpS[:, C * k:C * k + 16 * i], F.Relu,
                 accum_out=T.rs[:, i:i + 1])
         if t == 0:
-            act("P3", "tmp5", T.tmpS[:, 5 * C:], T.P3[:, 0:C], F.Sign)
             pass1(0)
+            act("P3", "tmp5", T.tmpS[:, 5 * C:], T.P3[:, 0:C], F.Sign)
+            pass1(NS - 1)
             act("tmp5 cFL mz5", "m24", mrow(24, C), T.tmpS[:, 5 * C:], F.Relu, scale=col("cFL"))
-            for k in range(1, NS):
+            for k in range(1, NS - 1):
                 pass1(k)
+            pass2(NS - 1)
         else:
             for ks in (range(ns - 1, 2, -1), range(2, -1, -1)):
                 for k in ks:
@@ -436,42 +453,39 @@ def rank_program(g, core, T, topo):
         for i in range(23 - ns, 0, -1):
             if i == 22 - ns:
                 scan("d0 mklo", "lo", T.hold[:, 0:e], T.d0[:, 0:e], T.mk[:, 0:e], 0.0, A.add, A.max)
-            if i == 20 - NS and t == 0:
-                mset("rs0", T.rs[:, 0:1], 0.0)
-                ts("ci0", "ci3", T.ci[:, 3:4], T.ci[:, 0:1], 31, A.bitwise_and)
-                mset("ppz", T.pp[:, C:C + 1], -100.0)
-                cp("ci2", "cQ4", col("cQ4"), T.ci[:, 2:3])
+            if i == 18 - NS and t == 0:
+                ts("c16", "cK16", T.cK16[:], T.c16[:], 16.0, A.mult)
                 quant("m21 m22 m23 m24 mz5", "qm5", T.qm[:, QO[5]:], T.sm[:, QO[5]:], T.M[:, 4 * TO[5]:])
                 quant("cb", "qb", T.qb[:], T.sb[:], T.cb[:])
                 mm("qb qm5", "P4", T.P4[:, 0:C], T.qb[:], T.sb[:], T.qm[:, QO[5]:], T.sm[:, QO[5]:])
-                for k in range(NS):
+                for k in range(NS - 1):
                     pass2(k)
                 act("P4 ppz", "pp", T.pp[:, 0:C], T.P4[:, 0:C], F.Copy)
                 run(sums, len(sums))
-            if i == (16 if t else 19 - NS):
+            if i == (16 if t else 17 - NS):
                 tt("P0 hi lo", "m24", mrow(24, C), T.hold[:], T.P0[:, 0:C], A.is_ge)
             ts("P0 mz " + ("hi" if i >= 24 - NH else "lo"), "m%d" % i, mrow(i, 16 * i), T.P0[:, 0:16 * i],
                T.hold[:, 16 * i + 15:16 * i + 16], A.is_lt)
             if nv < i and (t == 0 or i < 13):
                 sums.append(lambda i=i: act("m%d" % i, "rs%d jr%d" % (i, i), T.jr[:, 8 * i * (i - 1):8 * i * (i + 1)],
                                             mrow(i, 16 * i), F.Copy, accum_out=T.rs[:, i:i + 1]))
-                if t > 0 or i <= 20 - NS:
+                if t > 0 or i <= 18 - NS:
                     run(sums, 1)
                 if t > 0 and i < 12:
-                    run(unpack, 2)
-            if i == (15 if t else 13):
+                    run(unpack, {11: 1, 9: 1, 7: 3}.get(i, 0))
+            if i == (15 if t else 12):
                 scan("m24 dm", "ds", T.ds[:], T.dm[:], mrow(24, C), 0.0, A.max, A.subtract)
             if t == 0:
-                if i == 12:
+                if i == 11:
                     qtile(5)
                     qtile(4)
-                if i == 11:
+                if i == 10:
                     qtile(3)
                 if i == 9:
                     wrap16("pp", "", None, T.pp[:, 0:C], C, "wrc")
-                if i == 6:
-                    base()
-            else:
+            if i == 6:
+                base()
+            if t > 0:
                 if i == 14:
                     qtile(4, False)
                     fold(2, 4, 0, 3)
@@ -480,9 +494,9 @@ def rank_program(g, core, T, topo):
                     fold(0, 3, 0, 2)
                     fold(1, 3, 1, 2)
                     unpack = [lambda: act("pk0 pk1 pk2", "pkb", T.rs[:, 28:31], T.rs[:, 24:27], F.Identity,
-                                          scale=1.0 / FW, bias=ROUND), lambda: None,
+                                          scale=1.0 / FW, bias=ROUND),
                               lambda: act("pkb", "rs14 rs16 rs18", T.rs[:, 14:19:2], T.rs[:, 28:31], F.Identity,
-                                          bias=-ROUND), lambda: None]
+                                          bias=-ROUND)]
                     for m in range(3):
                         a = 13 + 2 * m
                         unpack.append(lambda m=m, a=a: act(
@@ -496,16 +510,18 @@ def rank_program(g, core, T, topo):
                 qtile(2)
             if i == 3:
                 tt("base ds", "base", T.base[:], T.base[:], T.ds[:, 15:C:16], A.add)
+            if i == 2:
+                rowsum(nv)
         qtile(1)
-        for i in range(nv, 0, -1):
-            if i == nv - 1:
+        for i in range(nv - 1, 0, -1):
+            if i == nv - 2:
                 qtile(0)
-            op("v", "m%d" % i, "rs%d" % i, lambda: V.tensor_reduce(T.rs[:, i:i + 1], mrow(i, 16 * i), AxisListType.X, A.add))
+            rowsum(i)
         rd = " ".join("rs%d" % i for i in range(24))
         if t == 0:
             for k in range(5):
                 borders(k)
-                run(late, (7, 2, 2, 2, 9)[k])
+                run(late, (7, 2, 2, 2, len(late))[k])
         run(fill, FV[t][0])
         tt("base " + rd, "cK16", T.cK16[:, 15:C:16], T.base[:], T.rs[:, 0:24], A.subtract)
         if t == 0:
@@ -530,7 +546,7 @@ def rank_program(g, core, T, topo):
         run(fill, FV[t][8])
         cp("oP iotaC", "O", T.O[:].indirect(T.oP[:]), T.iotaC[:])
         if t == 0:
-            act("X", "Xh", T.Xh[:], T.X[:], F.Identity, scale=0.5)
+            act("X X1 X2", "Xh", T.Xh[:], T.X[:], F.Identity, scale=0.5)
         run(fill, FV[t][9])
         if t > 0:
             act("PT oP", "porow", T.porow[:], T.PT[:].indirect(T.oP[:]), F.Copy)
@@ -544,21 +560,25 @@ def rank_program(g, core, T, topo):
         ts("wr4 cO4", "oAB4", T.oAB4[:], T.wr4[:, 3:C:4], 4.0, A.mult, col("cO4"), A.add)
         run(fill, FV[t][12])
         for k, (a, b) in enumerate(ZC):
-            bh, src = T.ABh[:, 768 + 16 * a:768 + 16 * b], T.Xh[:].indirect(T.oAB4[:, 48 + a:48 + b])
+            bh, src = T.Bh[:, 16 * a:16 * b], T.Xh[:].indirect(T.oAB4[:, 48 + a:48 + b])
             if k == 0:
-                cp("Xh oAB4", "Bh0 nB0", bh, src)
+                cp("Xh oAB4", "Bh0", bh, src)
             else:
-                act("Xh oAB4", "Bh%d nB%d" % (k, k), bh, src, F.Copy)
+                act("Xh oAB4", "Bh%d" % k, bh, src, F.Copy)
+        wrap16("O", "", None, T.O[:, C - 1:C - 1 - L:-1], L)
         run(fill, FV[t][13])
+
+        def side_a(w, a, b):
+            act("X X1 X2 oAB4", w, T.AB4[:, 16 * a:16 * b], T.X[:].indirect(T.oAB4[:, a:b]), F.Copy)
 
         def zsum(k):
             a, b = ZC[k]
             tt("Xh oAB4 Bh%d" % k, "Z%d" % k, T.Z[:, 16 * a:16 * b],
-               T.Xh[:].indirect(T.oAB4[:, a:b]), T.ABh[:, 768 + 16 * a:768 + 16 * b], A.add)
+               T.Xh[:].indirect(T.oAB4[:, a:b]), T.Bh[:, 16 * a:16 * b], A.add)
 
         def layer(h, rd):
             c = 128 * h
-            quant(rd, "qz%d" % h, T.qz[:, c:c + 128], T.sz[:, c:c + 128], T.Z[:, 256 * h:256 * h + 512])
+            quant(rd, "qz%d" % h, T.qz[:, c:c + 128], T.sz[:, c:c + 128], T.Z[:, 256 - 256 * h:768 - 256 * h])
             for b in range(4):
                 pb = "P%d" % (4 - 4 * h + b)
                 mm("qw qz%d" % h, pb, T[pb][:, 0:128], T.qw[:, 128 * b:128 * b + 128],
@@ -566,132 +586,176 @@ def rank_program(g, core, T, topo):
 
         def verdicts(h, rd):
             c, pb = 128 * h, "P%d" % (4 + h)
-            quant(rd, "qh%d" % h, T.qh[:, c:c + 128], T.sh[:, c:c + 128], T.Hpm[:, 256 * h:256 * h + 512])
+            quant(rd, "qh%d" % h, T.qh[:, c:c + 128], T.sh[:, c:c + 128], T.Hpm[:, 256 - 256 * h:768 - 256 * h])
             mm("qr sr qh%d" % h, pb, T[pb][:, 0:128], T.qr[:], T.sr[:], T.qh[:, c:c + 128], T.sh[:, c:c + 128])
 
         def flags(h):
-            a, b, pb = 128 * h, 128 + 64 * h, "P%d" % (4 + h)
-            ts(pb, "WL0%d" % h, T.WL[:, a:b], T[pb][:, 64 * h:128], 0.0, A.is_gt)
-            ts(pb, "WL1%d" % h, T.WL[:, 192 + a:192 + b], T[pb][:, 64 * h:128], 0.0, A.is_le)
-        for k in range(3):
+            a, b, pb = 64 - 64 * h, 192 - 128 * h, "P%d" % (4 + h)
+            ts(pb, "WL0%d" % h, T.WL[:, a:b], T[pb][:, 0:b - a], 0.0, A.is_gt)
+            ts(pb, "WL1%d" % h, T.WL[:, 192 + a:192 + b], T[pb][:, 0:b - a], 0.0, A.is_le)
+
+        def play(w, rd, a, b):
+            h = a % 768
+            tt("H0 H1 H2 H3 " + rd, w, T.AB4[:, a:b], T.AB4[:, a:b], T.Hpm[:, h:h + b - a], A.add if a < 768 else A.subtract)
+
+        z = 256 * t
+        lo, lp = T.lo[:, 16 * t:16 * t + 16], T.lp[:, L * t:L * t + L]
+        total["ls"] = total.get("ls", 0) + 6 * ne
+        for sem, calls in (("ara", 2), ("arb", 2), ("arl", 1), ("arp", 1)):
+            total[sem + str(t)] = calls * ne_in
+            lastw[sem + str(t)] = (sem + str(t), calls * ne_in)
+
+        def send(rd, dst, src, sem):
+            deps("g", [rd], [])
+            g.remote_dma(dst, src, T.sem[sem + str(t)], T.sem.ls, pid, rid, mask)
+            note(("ls", total["ls"]), [rd], [])
+
+        def ahead(h, rd):
+            c, w = 128 * h, "qs%d" % h
+            q, s = T.qz[:, 256 + c:384 + c], T.sz[:, 256 + c:384 + c]
+            quant(rd, w, q, s, T.AB4[:, 4 * (NL + c):4 * (NL + c) + 512])
+            send(w, T.ql[:, z + c:z + c + 128].bitcast(dt.uint8), q.bitcast(dt.uint8), "ar" + "ab"[h])
+            send(w, T.sl[:, z + c:z + c + 128], s, "ar" + "ab"[h])
+
+        def unpack(h):
+            c = z + 128 * h
+            for b in range(4):
+                pb = "P%d" % (4 * h + b)
+                mm("qe%d ar%s%d" % (b, "ab"[h], t), pb, T[pb][:, 0:128], T.qe[:, 128 * b:128 * b + 128],
+                   T.se[:, 128 * b:128 * b + 128], T.ql[:, c:c + 128], T.sl[:, c:c + 128])
+                out = T.Df[:, 512 * h + b:512 * h + 512:4]
+                if h or b % 2 == 0:
+                    act(pb, "D%d" % (4 * h + b), out, T[pb][:, 0:128], F.Copy)
+                else:
+                    cp(pb, "D%d" % (4 * h + b), out, T[pb][:, 0:128])
+        for k in range(4):
             zsum(k)
-        wrap4("porow", "", None, T.porow[:], C)
-        act("Xh oAB4", "Ah", T.ABh[:, 0:768], T.Xh[:].indirect(T.oAB4[:, 0:48]), F.Copy)
+        act("Bh0 Bh1 Bh2", "nB1 nB2", T.AB4[:, 1024:], T.Bh[:, 256:], F.Identity, scale=2.0)
+        side_a("gA1 nA1", 16, 24)
         layer(0, "Z0 Z1 Z2")
-        zsum(3)
+        zsum(4)
+        ts("wr cOC", "oR", T.oR[:], T.wr[:, 15:L:16], col("cOC"), A.subtract)
+        run(unit, 1)
+        layer(1, "Z0 Z1 Z3 Z4")
+        wrap4("porow", "", None, T.porow[:], C)
+        wrap16("PT", "", None, T.PT[:], C, "wrc")
         ts("wr4 cO4", "oPos4", T.oPos4[:], T.wr4[:, 3:C:4], 4.0, A.mult, col("cO4"), A.add)
         run(fill, len(fill))
-        layer(1, "Z1 Z2 Z3")
-        wrap16("PT", "oPP", T.oPP[:], T.PT[:], C, "wrc")
+        ts("wrc cOC", "oPP", T.oPP[:], T.wrc[:, 15:C:16], col("cOC"), A.subtract)
         for b in range(4):
-            act("P%d" % (4 + b), "H%d" % b, T.Hpm[:, b:512:4], T["P%d" % (4 + b)][:, 0:128], F.Identity, scale=0.03125)
+            pb = "P%d" % (4 + b)
+            act(pb, "H%d" % b, T.Hpm[:, 256 + b:768:4], T[pb][:, 0:128], F.Identity, scale=0.03125)
         verdicts(0, "H0 H1 H2 H3")
         for b in range(4):
             pb = "P%d" % b
-            if b % 2 == 0:
-                act(pb, "H%d" % (4 + b), T.Hpm[:, 512 + b:768:4], T[pb][:, 64:128], F.Identity, scale=0.03125)
+            if b == 0:
+                act(pb, "H%d" % (4 + b), T.Hpm[:, b:256:4], T[pb][:, 0:64], F.Identity, scale=0.03125)
             else:
-                ts(pb, "H%d" % (4 + b), T.Hpm[:, 512 + b:768:4], T[pb][:, 64:128], 0.03125, A.mult)
+                ts(pb, "H%d" % (4 + b), T.Hpm[:, b:256:4], T[pb][:, 0:64], 0.03125, A.mult)
+        side_a("nA3 nA4", 32, 48)
+        act("Bh3 Bh4", "nB0", T.AB4[:, 768:1024], T.Bh[:, 0:256], F.Identity, scale=2.0)
+        side_a("gA0 nA0", 0, 16)
+        side_a("gA2 nA2", 24, 32)
+        act("pp oR", "pold", T.sp[:, L:2 * L], T.pp[:, 0:C].indirect(T.oR[:]), F.Copy)
+        play("nB1", "nB1", 1024, 1248)
         verdicts(1, HH)
         flags(0)
-        act(HH, "Hh", T.Hpm[:, 768:1536], T.Hpm[:, 0:768], F.Identity, scale=0.5)
-        dma("g", "Hh Ah", "Ah", T.ABh[:, 0:768], T.Hpm[:, 768:1536], "ga", accum_op=A.add)
-
-        def newb(k):
-            a = 768 + 192 * k
-            tt("Hh Bh0 Bh1 Bh2 Bh3 Z0 Z1 Z2 Z3", "nB%d" % k, T.ABh[:, a:a + 192], T.ABh[:, a:a + 192],
-               T.Hpm[:, a:a + 192], A.subtract)
+        play("nB2", "nB2", 1248, 1536)
         flags(1)
+        play("nA4", "nA3", 688, 768)
+        ahead(1, "nB1 nB2")
         cp("WL00 WL01 WL10 WL11 oPP", "win", T.win[:, 16:208], T.WL[:].indirect(T.oPP[:, 0:12]))
         act("WL00 WL01 WL10 WL11 oPP", "win2", T.win[:, 208:C + 16], T.WL[:].indirect(T.oPP[:, 12:24]), F.Copy)
         act("win win2 oP", "gain k384", T.gain[:], T.win[:, 16:C + 16].indirect(T.oP[:]), F.Copy)
-        dma("g", "gain pp", "pp", T.pp[:, 0:C], T.gain[:], "gb", accum_op=A.add)
-        newb(0)
+        play("nA3", "nA3", 512, 688)
+        play("nB0", HH + " nB0", 768, 1024)
         scan("MW win2", "la", T.LJ[:, LA:C], T.MW[:, 800 + LA:800 + C], T.win[:, 16 + LA:16 + C], 512.0,
              A.min, A.subtract)
         scan("MW win win2", "om", T.cat[:, 2 * C:0:-2], T.MW[:, C:0:-1], T.win[:, C + 15:15:-1], 0.0,
              A.mult, A.subtract)
         ts("win win2", "lw0", T.cat[:, 3:2 * LA + 2:2], T.win[:, 16:LA + 16], 640.0, A.mult, 256.0, A.subtract)
         tt("win2 la", "lw", T.cat[:, 2 * LA + 3:2 * C + 2:2], T.win[:, LA + 16:C + 16], T.LJ[:, LA:], A.mult)
-        newb(1)
+        ahead(0, "nA3 nA4 nB0")
+        play("nA2", "gA2 nA2", 432, 512)
         scan("om lw0 lw c32a c32b c32c c32d", "wr3", T.wr3[:], T.cat[:, 2:2 * C + 2], T.c32[:], -2048.0, A.max, A.add)
-        newb(2)
+        play("nA1", HH + " gA0 gA1 gA2 nA1", 224, 432)
         ts("wr3 cO", "oL", T.oL[:], T.wr3[:, 31:2 * C:32], col("cO"), A.subtract)
-        newb(3)
+        play("nA0", HH + " nA0", 0, 224)
+        NB = "nA0 nA1 nA2 nA3 nA4 nB0 nB1 nB2 "
+        act(NB + "oPos4 Xh qx qxh", "Xa", T.X[:, 0:HX], T.AB4[:].indirect(T.oPos4[:, 0:HX // 16]), F.Copy)
         cp("oL PT", "LW", T.LW[:].indirect(T.oL[:]), T.PT[:])
         run(unit, 1)
         wrap4("LW", "", None, T.LW[:, 0:L], L)
         wrap16("LW", "", None, T.LW[:, 0:L], L)
         run(unit, 1)
-        ts("wr4 cO4", "oL4", T.oL4[:], T.wr4[:, 3:L:4], 4.0, A.mult, col("cO4"), A.add)
-        run(unit, 1)
-        NB = "Ah nB0 nB1 nB2 nB3 "
-        act(NB + "oL4", "ST0", T.ST[:, 0:128], T.ABh[:].indirect(T.oL4[:, 0:8]), F.Identity, scale=2.0)
-        ts(NB + "oL4", "ST1", T.ST[:, 128:256], T.ABh[:].indirect(T.oL4[:, 8:16]), 2.0, A.mult)
+        ts("wr4 cO5", "oL4", T.oL4[:], T.wr4[:, 3:L:4], 4.0, A.mult, col("cO5"), A.add)
         ts("wr cOC", "oL16", T.oL16[:], T.wr[:, 15:L:16], col("cOC"), A.subtract)
-        quant("ST0 ST1 STz", "qs", T.qs[:, 0:128], T.ss[:, 0:128], T.ST[:])
+        send("oL4", lo, T.oL4[:], "arl")
+        tt("gain pp", "pp", T.pp[:, 0:C], T.pp[:, 0:C], T.gain[:], A.add)
+        cp(NB + "oPos4", "Xb", T.X[:, HX:HX + 128], T.AB4[:].indirect(T.oPos4[:, HX // 16:HX // 16 + 8]))
+        act("WL00 WL01 WL10 WL11 oL16", "wat", T.sp[:, 2 * L:], T.WL[:].indirect(T.oL16[:]), F.Copy)
         act("AB AB2 oL16", "crow", T.crow[:], T.AB[:].indirect(T.oL16[:]), F.Copy)
-        deps("g", ["qs", "qs2"], [])
-        g.remote_dma_fused([
-            RemoteDMATransfer(dst_ids=[DstId(rid=rid, pnc=pid)], dma_engine_mask=lo_mask, remote_sem=T.sem["arc%d" % t],
-                              src=T.qs[:, 0:L].bitcast(dt.uint8), dst=T["ql%d" % t][:, 128:192].bitcast(dt.uint8)),
-            RemoteDMATransfer(dst_ids=[DstId(rid=rid, pnc=pid)], dma_engine_mask=hi_mask, remote_sem=T.sem["arc%d" % t],
-                              src=T.ss[:], dst=T["sl%d" % t][:, 128:384]),
-        ], local_sem=T.sem.ls)
-        total["ls"] = total.get("ls", 0) + 2 * ne
-        note(("ls", total["ls"]), ["qs"], [])
-        lastw["land%d" % t] = ("arc%d" % t, ne_in)
-        lastw["lp%d" % t] = ("arp%d" % t, ne_in)
-        total["arc%d" % t] = total["arp%d" % t] = ne_in
-        run(unit, 2)
-        wrap16("crow", "oC16", T.oC16[:], T.crow[:], L)
-        act("pp oC16", "sp", T.sp[:], T.pp[:, 0:C].indirect(T.oC16[:]), F.Copy)
-        deps("g", ["sp"], [])
-        g.remote_dma(T["lp%d" % t][:], T.sp[:], T.sem["arp%d" % t], T.sem.ls, pid, rid, lo_mask | hi_mask)
-        note(("ls", total["ls"]), ["sp"], [])
-        for b in range(4):
-            ts("oC16", "oC4%d" % b, T.oC4[:, 4 * b:4 * b + 4], T.oC16[:], 4.0, A.mult, float(b), A.add)
-        if t == 0:
-            quant("zt", "zl0", T.ql0[:, 0:128], T.sl0[:, 0:128], T.zt[:])
-        ts(NB + "oPos4", "X", T.X[:, HX:], T.ABh[:].indirect(T.oPos4[:, HX // 16:]), 2.0, A.mult)
-        act(NB + "oPos4 Xh qx qxh", "Xa", T.X[:, 0:HX], T.ABh[:].indirect(T.oPos4[:, 0:HX // 16]), F.Identity, scale=2.0)
+        run(unit, 1)
+        tt("pold wat", "sp", T.sp[:, 0:L], T.sp[:, L:2 * L], T.sp[:, 2 * L:], A.add)
+        send("sp", lp, T.sp[:, 0:L], "arp")
+        wrap4("crow", "", None, T.crow[:], L)
+        wrap16("crow", "", None, T.crow[:], L)
+        unpack(1)
         if t == 0:
             a = QO[5] - 128
             quant("zt", "qm4 qmz", T.qm[:, a:a + 128], T.sm[:, a:a + 128], T.zt[:])
         if t == 1:
             quant("vt", "qv", T.qv[:], T.sv[:], T.vt[:])
+        ts("wr4 cO4", "oC4", T.oC4[:], T.wr4[:, 3:L:4], 4.0, A.mult, col("cO4"), A.add)
+        ts("wr cOC", "oC16", T.oC16[:], T.wr[:, 15:L:16], col("cOC"), A.subtract)
+        cp(NB + "oPos4", "X", T.X[:, HX + 128:], T.AB4[:].indirect(T.oPos4[:, HX // 16 + 8:]))
         if t + 1 < R:
-            z = "%d" % (t + 1)
-            quant("zt", "zl" + z, T["ql" + z][:, 0:128], T["sl" + z][:, 0:128], T.zt[:])
             iota("Wt", T.Wt[:, 0:tw + C], [[0, tw + C]], 0, 0)
-            blank_marks()
-        ql, sl = T["ql%d" % t], T["sl%d" % t]
-        for b in range(4):
-            pb = "P%d" % (4 + b)
-            mm("qe%d zl%d land%d" % (b, t, t), pb, T[pb][:, 0:128], T.qe[:, 128 * b:128 * b + 128],
-               T.se[:, 128 * b:128 * b + 128], ql[:, 64:192], sl[:, 64:192])
-        for b in range(4):
-            pb = "P%d" % (4 + b)
-            act(pb, "D%d" % b, T.Dt[:, L * b:L * b + L], T[pb][:, 64:128], F.Copy)
-        cp("D0 oC40 X Xa", "X", T.X[:].indirect(T.oC4[:, 0:4]), T.Dt[:, 0:L])
-        cp("lp%d oC16 pp" % t, "pp", T.pp[:, 0:C].indirect(T.oC16[:]), T["lp%d" % t][:])
-        cp("D1 D2 D3 oC41 oC42 oC43 X", "X", T.X[:].indirect(T.oC4[:, 4:16]), T.Dt[:, L:])
+        unpack(0)
+        run(unit, 1)
         if t + 1 < R:
-            for k in range(5):
+            count("sp", T.sp[:, 0:L], 2, 0)
+            count("sp", T.sp[:, 0:L], 2, 1)
+            count("pp", T.pp[:, 0:C + 1], 0, 0)
+        rd = "D0 D1 D2 D3 D4 D5 D6 D7 arl%d" % t
+        act(rd, "Dt0", T.Dt[:, 0:128], T.Df[:].indirect(T.lo[:, 16 * t:16 * t + 8]), F.Copy)
+        if t + 1 < R:
+            count("pp", T.pp[:, 0:C + 1], 0, 1)
+            for k in range(2):
+                act("cnt%d cnt%d" % (k, 2 + k), "cnt%d" % (6 + k), T.cnt[:, 6 + k:7 + k], T.cnt[:, 2 + k:3 + k],
+                    F.Identity, scale=-1.0, bias=T.cnt[:, k:k + 1])
+        else:
+            act("pp", "wrK", T.wrK[:], T.pp[:, 0:C], F.Copy)
+        cp(rd, "Dt1", T.Dt[:, 128:], T.Df[:].indirect(T.lo[:, 16 * t + 8:16 * t + 16]))
+        cp("Dt0 Dt1 oC4 X Xa Xb", "X", T.X[:].indirect(T.oC4[:]), T.Dt[:])
+        if t + 1 < R:
+            wait("s", ("ls", total["ls"]))
+            blank_marks()
+        pb = "pp" if t + 1 < R else "wrK"
+        points = [lambda t=t, lp=lp, pb=pb: cp("arp%d oC16 " % t + pb, pb, T[pb][:, 0:C].indirect(T.oC16[:]), lp)]
+        if t + 1 < R:
+            for k in range(2):
+                count("arp%d" % t, lp, 4, k)
+            for k in range(2):
+                act("cnt%d cnt%d" % (6 + k, 4 + k), "cnt%d" % k, T.cnt[:, k:k + 1], T.cnt[:, 4 + k:5 + k], F.Identity,
+                    bias=T.cnt[:, 6 + k:7 + k])
+            for k in range(1, 5):
                 borders(k)
 
-    dma("g", "pp", "", T.pts[:], T.pp[0:128:16, 0:C], "go")
     for k in range(3):
         a, b = 128 * k, 128 * k + 128
         quant("X", "qx qxh qx0" if k == 0 else "qx%d" % k, T.qx[:, a:b], T.sx[:, a:b], T.X[:, 4 * a:4 * b])
         mm("qv qx%d" % k, "P%d" % k, T["P%d" % k][:, 0:128], T.qv[:], T.sv[:], T.qx[:, a:b], T.sx[:, a:b])
-    dma("s", "qx0 qx1 qx2", "", T.oc[:], T.qx[:].bitcast(dt.uint8))
+        dma("s", "qx%d" % k, "", T.oc[:, 4 * a:4 * b], T.qx[:, a:b].bitcast(dt.uint8))
+    run(points, 1)
     for k in range(4):
         dma("s", "qx0 qx1 qx2", "", T.osc[4 * k:4 * k + 4, :], T.sx[32 * k:32 * k + 4, :])
+    dma("s", "wrK", "", T.pts[:], T.wrK[0:128:16, :])
     act("P0", "y0", T.yo[:, 0:128], T.P0[:, 0:128], F.Copy)
-    cp("P1", "y1", T.yo[:, 128:256], T.P1[:, 0:128])
-    act("P2", "y2", T.yo[:, 256:C], T.P2[:, 0:128], F.Copy)
-    dma("s", "y0 y1", "", T.y[:, 0:256], T.yo[:, 0:256])
-    dma("a", "y2", "", T.y[:, 256:C], T.yo[:, 256:C])
-    for s in total:
+    act("P1", "y1", T.yo[:, 128:256], T.P1[:, 0:128], F.Copy)
+    cp("P2", "y2", T.yo[:, 256:C], T.P2[:, 0:128])
+    dma("a", "y0", "", T.y[:, 0:128], T.yo[:, 0:128])
+    dma("a", "y1", "", T.y[:, 128:256], T.yo[:, 128:256])
+    dma("s", "y2", "", T.y[:, 256:C], T.yo[:, 256:C])
+    for s in sorted(total, key=lambda s: (s, total[s]) not in behind):
         wait("g", (s, total[s]))

from concourse.mybir import dt, AluOpType, ActivationFunctionType, AxisListType

A = AluOpType
F = ActivationFunctionType
C, L, R = 384, 64, 3
BIG = 1e29
WD = "float16"
HX = 1280
NL = 128
LA = 256
FV = [(3, 3, 1, 1, 5, 1, 1, 2, 1, 1, 1, 1, 1, 1), (3, 2, 1, 0, 1, 2, 1, 1, 1, 0, 0, 0, 0, 0)]
FV.append(FV[1])
NH = 8
NV = 7
NS = 4
NS1, NV1, Q5 = 5, 5, 8
TW = [128, 128, 192, 256, 320, 384]
TO = [sum(TW[:k]) for k in range(6)]
QO = TO[:5] + [TO[5] + 64]
MWD = sum(TW)
FW = 1024.0
ROUND = 12582912.0
ZC = [(16, 24), (24, 36), (36, 48), (0, 8), (8, 16)]


def _sb(n, d):
    return ("sbuf", [128, n], d)


BF, F32, U16, I32, QX, U8 = "bfloat16", "float32", "uint16", "int32", "float8_e4m3fn_x4", "uint8"
SCRATCH = {
    "X": _sb(4 * C, BF), "Xh": _sb(4 * C, BF), "qx": _sb(C, QX), "sx": _sb(C, U8),
    "ut": _sb(512, BF), "vt": _sb(512, BF), "qu": _sb(128, QX), "su": _sb(128, U8),
    "qr": _sb(128, QX), "sr": _sb(128, U8), "qv": _sb(128, QX), "sv": _sb(128, U8),
    "qw": _sb(512, QX), "sw": _sb(512, U8),
    "one": _sb(512, BF), "cb": _sb(512, BF), "qb": _sb(128, QX), "sb": _sb(128, U8),
    "ce": _sb(3072, BF), "qe": _sb(768, QX), "se": _sb(768, U8), "zt": _sb(512, BF),
    "kmin": _sb(C, BF), "d0": _sb(C, BF), "mk": _sb(C, F32), "hold": _sb(C, F32), "x16r": _sb(C, BF),
    "cK16": _sb(C, F32), "wrK": _sb(C, F32), "wr3": _sb(2 * C, WD),
    "dm": _sb(C, BF), "ds": _sb(C, WD), "M": _sb(4 * MWD, BF), "qm": _sb(MWD + 64, QX), "sm": _sb(MWD + 64, U8),
    "tmpS": _sb(6 * C, BF), "rs": _sb(32, F32), "junk": _sb(2 * C + 2 + 4 * L, BF), "jr": _sb(16 * 12 * 23, BF),
    "win": _sb(C + 16, BF), "LJ": _sb(C, WD), "c32": _sb(2 * C, WD), "rev": _sb(C, WD),
    "O": _sb(C, BF), "PI": _sb(C, WD), "wri": _sb(C, WD), "oPI": _sb(24, U16), "al2": _sb(32, F32),
    "c16": _sb(C, BF), "c4": _sb(C, BF), "wr": _sb(C, WD), "wr4": _sb(C, WD), "wrc": _sb(C, WD),
    "ci": _sb(16, I32), "cf": _sb(40, F32), "x16": _sb(16, F32), "k16": _sb(16, F32), "p16": _sb(16, F32),
    "p4": _sb(8, F32), "t16": _sb(16, F32), "al32": _sb(32, F32),
    "oRep": _sb(8, U16), "oQ": _sb(24, U16), "oQ4": _sb(24, U16), "oHalf": _sb(4, U16),
    "oK": _sb(24, U16), "oP": _sb(24, U16), "oPos4": _sb(96, U16), "oAB4": _sb(96, U16),
    "oPP": _sb(24, U16), "oL": _sb(24, U16), "oL4": _sb(16, U16), "oL16": _sb(4, U16), "oC4": _sb(16, U16),
    "oC16": _sb(4, U16), "oM": _sb(4, U16),
    "base": _sb(24, F32), "cnt": _sb(8, F32), "tn": _sb(20, F32),
    "rep": _sb(64, F32), "rpt": _sb(96, F32), "dat": _sb(64, BF), "tpl": _sb(1200, BF), "MW": _sb(1632, BF),
    "Wt": _sb(6 * C, BF), "Pt": _sb(6 * C, BF), "iotaC": _sb(C, BF),
    "plrow": _sb(C, BF), "porow": _sb(C, BF), "PT": _sb(C, BF), "AB": _sb(C, BF),
    "AB4": _sb(4 * C, BF), "Bh": _sb(2 * C, BF), "Z": _sb(2 * C, BF), "qz": _sb(512, QX), "sz": _sb(512, U8),
    "Hpm": _sb(2 * C, BF), "qh": _sb(256, QX), "sh": _sb(256, U8),
    "WL": _sb(C, BF), "gain": _sb(C, BF), "cat": _sb(2 * C + 16, WD), "LW": _sb(2 * C, BF), "crow": _sb(L, BF),
    "ql": _sb(256 * R, QX), "sl": _sb(256 * R, U8), "lo": _sb(16 * R, U16), "lp": _sb(L * R, BF),
    "Df": _sb(1024, BF), "oR": _sb(4, U16), "pp": _sb(C + 16, BF), "sp": _sb(3 * L, BF), "Dt": _sb(4 * L, BF), "yo": _sb(C, F32),
}
for _b in range(8):
    SCRATCH["P%d" % _b] = ("psum", [128, 512], F32)

NDMA = 24
SEMAPHORES = (["nv", "na", "np_", "ng", "ls"] + ["d%d" % k for k in range(NDMA)]
              + [s + str(t) for s in ("ara", "arb", "arl", "arp") for t in range(R)])
NAMES = ("cQ cQM cO cOC cH cHM cQ4 cO4 cFL cR1 cR2 cK cTH cTL cNF cMID cBE cTHE cGJ cJ cEP "
         "cB1 cX1 cT1 cT2 cT3 cM1 cM2 cQ5 cN1 cN2 cJ2 cO16 cJN cYA cYB cJA cJB cP32 cO5").split()


def rank_program(g, core, T, topo):
    rank = T.rank_of(core)
    if rank is None:
        return
    n = len(T.cores)
    nxt, prv = T.cores[(rank + 1) % n], T.cores[(rank - 1) % n]
    V, S, P = g.vector, g.scalar, g.tensor
    Q = {"v": V, "a": S, "p": P, "g": g, "s": g.sync}
    CS = {"v": "nv", "a": "na", "p": "np_", "g": "ng"}
    total, lastw, readers, behind = {}, {}, {}, {}
    waited = {q: {} for q in Q}
    ndma = [0]

    def wait(q, tok):
        if waited[q].get(tok[0], 0) < tok[1]:
            Q[q].wait_ge(T.sem[tok[0]], tok[1])
            waited[q][tok[0]] = tok[1]
            for s, v in behind.get(tok, {}).items():
                waited[q][s] = max(waited[q].get(s, 0), v)

    def deps(q, reads, writes):
        need = {}
        toks = []
        for k in reads:
            toks.append(lastw.get(k))
            if k[0] == "P" and k[1:].isdigit():
                toks += [t for t in readers.get(k, []) if t[0] != CS.get(q)]
        for k in writes:
            if not (q == "p" and lastw.get(k) and lastw[k][0] == "np_"):
                toks.append(lastw.get(k))
            toks += readers.get(k, [])
        for t in toks:
            if t is not None:
                need[t[0]] = max(need.get(t[0], 0), t[1])
        for s in sorted(need, key=lambda s: -len(behind.get((s, need[s]), ()))):
            wait(q, (s, need[s]))

    def note(tok, reads, writes):
        for k in reads:
            readers.setdefault(k, []).append(tok)
        for k in writes:
            lastw[k] = tok
            readers[k] = []

    def op(q, reads, writes, fn):
        reads, writes = reads.split(), writes.split()
        deps(q, reads, writes)
        s = CS[q]
        total[s] = total.get(s, 0) + 1
        fn().then_inc(T.sem[s], 1)
        behind[(s, total[s])] = dict(waited[q])
        note((s, total[s]), reads, writes)

    def dma(q, reads, writes, out, in_, sem=None, **kw):
        reads, writes = reads.split(), writes.split()
        deps(q, reads, writes)
        if sem is None:
            sem = "d%d" % ndma[0]
            ndma[0] += 1
        total[sem] = total.get(sem, 0) + 16
        Q[q].dma_start(out, in_, **kw).then_inc(T.sem[sem], 16)
        note((sem, total[sem]), reads, writes)

    def ts(r, w, out, in0, s1, o0, s2=None, o1=None):
        if s2 is None:
            op("v", r, w, lambda: V.tensor_scalar(out, in0, s1, None, o0))
        else:
            op("v", r, w, lambda: V.tensor_scalar(out, in0, s1, s2, o0, o1))

    def tt(r, w, out, in0, in1, o):
        op("v", r, w, lambda: V.tensor_tensor(out, in0, in1, o))

    def cp(r, w, out, in_):
        op("v", r, w, lambda: V.tensor_copy(out, in_))

    def scan(r, w, out, d0, d1, init, o0, o1):
        op("v", r, w, lambda: V.tensor_tensor_scan(out, d0, d1, init, o0, o1))

    def mset(w, ap, val):
        op("v", "", w, lambda: V.memset(ap, val))

    def quant(r, w, q, s, in_):
        op("v", r, w, lambda: V.quantize_mx(q, s, in_))

    def act(r, w, out, in_, f, **kw):
        op("a", r, w, lambda: S.activation(out, in_, f, **kw))

    def mm(r, w, out, lq, ls_, rq, rs_, start=True, stop=True):
        op("p", r, w, lambda: P.matmul_mx(out, lq, ls_, rq, rs_, start, stop))

    def iota(w, out, pat, base, cm, fl=True):
        if fl:
            op("g", "", w, lambda: g.iota(out, pat, base, cm, allow_small_or_imprecise_dtypes=True))
        else:
            op("g", "", w, lambda: g.iota(out, pat, base, cm))

    def col(name):
        k = NAMES.index(name)
        return T.cf[:, k:k + 1]

    def lin(w, a, scale=1.0, bias=0.0):
        rd = " ".join(k for k in (a, scale, bias) if isinstance(k, str))
        act(rd, w, col(w), col(a), F.Identity, scale=col(scale) if isinstance(scale, str) else scale,
            bias=col(bias) if isinstance(bias, str) else bias)

    def wrap16(r, w, out, src, m, buf="wr"):
        scan(r + " c16", buf, T[buf][:, 0:m], src, T.c16[:, 0:m], -2048.0, A.max, A.add)
        if out is not None:
            ts(buf + " cOC", w, out, T[buf][:, 15:m:16], col("cOC"), A.subtract)

    def wrap4(r, w, out, src, m):
        scan(r + " c4", "wr4", T.wr4[:, 0:m], src, T.c4[:, 0:m], -2048.0, A.max, A.add)
        if out is not None:
            ts("wr4 cO4", w, out, T.wr4[:, 3:m:4], 4.0, A.mult, col("cO4"), A.add)

    def mrow(i, m):
        k, e = (i - 1) // 4, (i - 1) % 4
        return T.M[:, 4 * TO[k] + e:4 * (TO[k] + m):4]

    def sumtile(k):
        a, b = QO[k], QO[k] + TW[k]
        mm("qb qm%d" % k, "P2", T.P2[:, 0:TW[k]], T.qb[:], T.sb[:], T.qm[:, a:b], T.sm[:, a:b], k == 5, k == 0)

    def qtile(k, now=True):
        a, b = QO[k], QO[k] + TW[k]
        rd = " ".join("m%d" % i for i in range(4 * k + 1, 4 * k + 5)) + " mz"
        quant(rd, "qm%d" % k, T.qm[:, a:b], T.sm[:, a:b], T.M[:, 4 * TO[k]:4 * (TO[k] + TW[k])])
        if now:
            sumtile(k)

    def rowsum(i):
        op("v", "m%d" % i, "rs%d" % i, lambda: V.tensor_reduce(T.rs[:, i:i + 1], mrow(i, 16 * i), AxisListType.X, A.add))

    def fold(m, k, h, pieces):
        pb, w = "P%d" % (4 + m), 512 + 128 * h
        for j in range(pieces):
            a = QO[k] + 128 * j
            mm("qf qmz qm%d" % k, pb, T[pb][:, 0:128], T.qe[:, w:w + 128], T.se[:, w:w + 128], T.qm[:, a:a + 128],
               T.sm[:, a:a + 128], j == 0, j == pieces - 1)
        act(pb, "pk%d jf%d" % (m, m), T.jr[:, 2048 + 128 * m:2176 + 128 * m], T[pb][:, 0:128], F.Copy,
            accum_out=T.rs[:, 24 + m:25 + m])

    dma("a", "", "ut", T.ut[:], T.u[:])
    dma("s", "", "X2", T.X[:, 1024:], T.x[:, 1024:])
    dma("s", "", "X1", T.X[:, 512:1024], T.x[:, 512:1024])
    dma("s", "", "X", T.X[:, 0:512], T.x[:, 0:512])
    iota("ci0", T.ci[:, 0:1], [[0, 1]], 0, 1, False)
    iota("ci8", T.ci[:, 8:16], [[16, 8]], 0, 0, False)
    iota("x16", T.x16[:], [[1, 16]], 0, 0)
    iota("x16r", T.x16r[:], [[0, 24], [1, 16]], 0, 0)
    mset("zt", T.zt[:], 0.0)
    ts("ci0", "ci1", T.ci[:, 1:2], T.ci[:, 0:1], 15, A.bitwise_and)
    mset("one", T.one[:], 1.0)
    cp("ci1", "cQ", col("cQ"), T.ci[:, 1:2])
    mset("tpl2", T.tpl[:, 400:800], 0.5)
    ts("cQ", "cT1", col("cT1"), col("cQ"), 0.0, A.is_gt)
    ts("cQ", "cR1", col("cR1"), col("cQ"), 4.5, A.is_gt)
    ts("cQ", "cR2", col("cR2"), col("cQ"), 10.5, A.is_gt)
    op("g", "one", "cb", lambda: g.affine_select(T.cb[:], T.one[:], [[-16, 8], [0, 64]], A.is_ge, 0.0, 0, 1))
    op("g", "cb", "cb", lambda: g.affine_select(T.cb[:], T.cb[:], [[16, 8], [0, 64]], A.is_ge, 0.0, 15, -1))
    iota("dm", T.dm[:], [[16, 24], [-512, 16]], 0, 0)
    iota("tpl", T.tpl[:, 0:400], [[0, 400]], 1, 0)
    iota("tpl3", T.tpl[:, 800:1200], [[0, 400]], 512, 0)
    iota("iotaC", T.iotaC[:], [[1, C]], -192, 0)
    for b in range(4):
        op("g", "one", "ce%d" % b, lambda: g.affine_select(
            T.ce[:, 512 * b:512 * b + 512], T.one[:], [[-1, 512]], A.is_equal, 0.0, b, 4))
    for h in range(2):
        op("g", "ce%d" % (2 * h), "cf%d" % h, lambda: g.affine_select(
            T.ce[:, 2048 + 512 * h:2560 + 512 * h], T.ce[:, 1024 * h:1024 * h + 512], [[-1, 512]], A.not_equal, FW,
            2 * h + 1, 4))
    for k in range(3):
        e = 4 * TO[5] + 512 * k
        dma("s", "zt", "mz5" if k == 2 else "", T.M[:, e:e + 512], T.zt[:], "d21")
    dma("s", "zt", "", T.M[:, 0:512], T.zt[:], "d23")
    for k in range(1, 5):
        e = 4 * (TO[k] + TW[k])
        dma("s", "zt", "mz" if k == 4 else "", T.M[:, e - 192:e], T.zt[:, 0:192], "d23")

    ts("x16 cQ", "k16", T.k16[:], T.x16[:], col("cQ"), A.is_equal)
    cp("ci8", "oRep", T.oRep[:], T.ci[:, 8:16])
    ts("one cQ", "oQ", T.oQ[:], T.one[:, 0:24], col("cQ"), A.mult)
    ts("ci0", "ci2", T.ci[:, 2:3], T.ci[:, 0:1], 3, A.bitwise_and)
    ts("k16", "p16", T.p16[:], T.k16[:], 1024.0, A.mult)
    ts("k16", "t16a", T.t16[:, 0:15], T.k16[:, 1:16], -2048.0, A.mult)
    ts("k16", "t16b", T.t16[:, 15:16], T.k16[:, 0:1], -2048.0, A.mult)
    ts("x16r cQ", "kmin", T.kmin[:], T.x16r[:], col("cQ"), A.not_equal, -2 * BIG, A.mult)
    tt("p16 t16a t16b", "p16", T.p16[:], T.p16[:], T.t16[:], A.add)
    ts("x16r", "d0", T.d0[:], T.x16r[:], 0.0, A.is_equal, -2 * BIG, A.mult)
    quant("ut", "qu", T.qu[:], T.su[:], T.ut[:])

    def pick_u():
        cp("qu oRep", "qr", T.qr[:].bitcast(dt.uint32), T.qu[:].bitcast(dt.uint32).indirect(T.oRep[:]))
    for k in range(3):
        dma("s", "zt X X1 X2", "", T.Wt[:, 512 * k:512 * k + 512], T.zt[:], "d20")
    dma("s", "zt", "", T.LW[:, 0:512], T.zt[:], "d20")
    dma("s", "zt", "Wt LW", T.LW[:, 512:768], T.zt[:, 0:256], "d20")
    dma("s", "", "", T.qw[:].bitcast(dt.uint8), T.wc[:], "d22")
    dma("s", "", "qw", T.sw[:], T.ws[:], "d22")
    dma("s", "", "vt", T.vt[:], T.v[:])
    lin("cH", "cQ", -1.0, 15.0)
    lin("cO", "cT1", 2048.0, -1024.0)
    lin("cT2", "cR1", -5.0, "cQ")
    lin("cK", "cR2", -6.0, "cT2")
    lin("cOC", "cO", 1.0, -192.0)
    lin("cB1", "cO", 384.0, "cH")
    lin("cO16", "cO", 16.0)
    lin("cTH", "cK", -1.0, 0.5)
    lin("cTL", "cK", -1.0, -0.5)
    lin("cMID", "cR2", -1.0, "cR1")
    lin("cTHE", "cR2", -1.0, 1.0)
    lin("cJ", "cQ", 1.0, 784.0)
    lin("cN1", "cR1", -1.0, 1.0)
    lin("cN2", "cR1", 1.0, -1.0)
    lin("cJ2", "cQ", 1.0, 1184.0)
    lin("cHM", "cR2", -95.5)
    lin("cM2", "cR1", -16777216.0)
    lin("cM1", "cR1", 16777216.0, 192.5)
    act("qu oRep", "sr", T.sr[:], T.su[:].indirect(T.oRep[:]), F.Copy)
    lin("cBE", "cMID", 0.5)
    lin("cEP", "cMID", 96.5, "cHM")
    lin("cQM", "cJ", -1.0, 800.0)
    lin("cEP", "cN1", 384.0, "cEP")
    lin("cNF", "cMID", -0.25)
    lin("cGJ", "cR1", -400.0, "cQM")
    act("p16 oQ", "c16", T.c16[:, 0:C], T.p16[:].indirect(T.oQ[:]), F.Copy)
    act("one cNF", "al32", T.al32[:], T.one[:, 0:32], F.Identity, scale=col("cNF"))
    act("p16 cB1", "cB1", col("cB1"), T.p16[:, 15:16], F.Identity, scale=16.0, bias=col("cB1"))

    def run(calls, k):
        for _ in range(min(k, len(calls))):
            calls.pop(0)()

    late = [lambda: lin("cYA", "cQ", -1.0, -400.0), lambda: lin("cYB", "cQ", -1.0, -216.0),
            lambda: lin("cJN", "cJ2", "cN2"), lambda: lin("cJA", "cQ", 1.0, 1600.0),
            lambda: lin("cJB", "cQ", 1.0, 1616.0), lambda: lin("cT2", "cQ4", -1.0, "cQ"),
            lambda: act("al32", "al2", T.al2[:], T.al32[:], F.Identity, scale=-1.0),
            lambda: lin("cYA", "cYA", "cMID"), lambda: lin("cYB", "cYB", "cMID"),
            lambda: lin("cQ5", "cQ4", 1.0, 4096.0 + 768.0), lambda: lin("cT2", "cT2", -0.25),
            lambda: act("x16 cT2", "t16a", T.t16[:, 0:4], T.x16[:, 0:4], F.Abs, bias=col("cT2")),
            lambda: act("cT2", "cT1", col("cT1"), col("cT2"), F.Sign),
            lambda: act("t16a", "t16a", T.t16[:, 0:4], T.t16[:, 0:4], F.Relu, scale=-1024.0, bias=1024.0),
            lambda: lin("cO4", "cT1", 8192.0, "cQ5")]
    for k in range(4):
        late.append(lambda k=k: act("t16a", "p4%d" % k, T.p4[:, k:k + 1], T.t16[:, (k + 1) % 4:(k + 1) % 4 + 1],
                                    F.Identity, scale=-2.0, bias=T.t16[:, k:k + 1]))
    late.append(lambda: lin("cO5", "cO4", 1.0, -4.0 * NL))

    pairc = [lambda: ts("x16r cQ", "k384", T.gain[:], T.x16r[:], col("cQ"), A.is_equal),
             lambda: ts("iotaC", "rev", T.rev[:], T.iotaC[:], -1.0, A.mult, 191.0, A.add),
             lambda: tt("k384 rev", "LJ", T.LJ[:, 0:LA], T.gain[:, 0:LA], T.rev[:, 0:LA], A.mult),
             lambda: tt("k384 rev", "c32b", T.c32[:, 2 * LA:2 * C:2], T.gain[:, LA:], T.rev[:, LA:], A.mult),
             lambda: tt("LJ c16", "c32a", T.c32[:, 1:2 * LA:2], T.LJ[:, 0:LA], T.c16[:, 0:LA], A.add),
             lambda: cp("c16", "c32c", T.c32[:, 2 * LA + 1:2 * C:2], T.c16[:, LA:]),
             lambda: cp("zt", "c32d", T.c32[:, 0:2 * LA:2], T.zt[:, 0:LA])]
    unit = [lambda k=k: quant("ce%d" % k, "qe%d" % k, T.qe[:, 128 * k:128 * k + 128], T.se[:, 128 * k:128 * k + 128],
                              T.ce[:, 512 * k:512 * k + 512]) for k in range(4)]
    unit.append(lambda: quant("cf0 cf1", "qf", T.qe[:, 512:768], T.se[:, 512:768], T.ce[:, 2048:3072]))

    def base():
        ts("wrc cB1", "base", T.base[:], T.wrc[:, 15:C:16], -384.0, A.mult, col("cB1"), A.add)

    def tn(k):
        return T.tn[:, k:k + 1]

    def count(rd, row, j, k):
        c, a = ("cTH", "cTL")[k], (2 * (C + 1) + L * (j - 2 + k) if j else (C + 1) * k)
        act(rd + " " + c, "junk%d cnt%d" % (j + k, j + k), T.junk[:, a:a + row.shape[1]], row, F.Sign, bias=col(c),
            accum_out=T.cnt[:, j + k:j + k + 1])

    def borders(k):
        if k == 0:
            count("pp", T.pp[:, 0:C + 1], 0, 0)
            count("pp", T.pp[:, 0:C + 1], 0, 1)
        if k == 1:
            act("cnt0 cnt1 cM1", "tn2", T.tn[:, 2:4], T.cnt[:, 0:2], F.Identity, scale=0.5, bias=col("cM1"))
        if k == 2:
            act("tn2 cM2", "tn4", T.tn[:, 4:6], T.tn[:, 2:4], F.Identity, bias=col("cM2"))
        if k == 3:
            act("tn4", "tn6", tn(6), tn(5), F.Identity, scale=-1.0, bias=tn(4))
            act("tn4 cTHE", "tn7", tn(7), tn(5), F.Sign, bias=col("cTHE"))
            act("tn4 cN2 cEP", "tn12", tn(12), tn(5), F.Identity, scale=col("cN2"), bias=col("cEP"))
            act("tn4 cGJ", "tn0", tn(0), tn(5), F.Identity, bias=col("cGJ"))
            act("tn4 cN1 cJN", "tn13", tn(13), tn(5), F.Identity, scale=col("cN1"), bias=col("cJN"))
            act("tn4 cBE cYA", "tn14", tn(14), tn(4), F.Identity, scale=col("cBE"), bias=col("cYA"))
            act("tn4 cBE cYB", "tn15", tn(15), tn(5), F.Identity, scale=col("cBE"), bias=col("cYB"))
        if k == 4:
            act("tn6 tn7", "tn9", tn(9), tn(6), F.Sign, scale=tn(7))
            act("tn6 tn0 cBE", "tn8", tn(8), tn(6), F.Identity, scale=col("cBE"), bias=tn(0))
            act("al32 tn6 tn12", "rep", T.rep[:, 0:32], T.al32[:], F.Identity, scale=tn(6), bias=tn(12))
            act("al2 tn6", "rep2", T.rep[:, 32:64], T.al2[:], F.Identity, scale=tn(6), bias=0.5)

    def tables():
        def offs(j, a, c):
            return lambda: ts("tn%d tn9 %s" % (a, c), "oM%d" % j, T.oM[:, j:j + 1], tn(a), tn(9), A.mult, col(c), A.add)
        return [lambda: op("v", "rep rep2", "rpt", lambda: V.transpose(T.rpt[:, 0:64], T.rep[:])),
                offs(0, 8, "cJ"), offs(1, 13, "cJ2"), offs(2, 14, "cJA"), offs(3, 15, "cJB"),
                lambda: cp("rpt rpz oHalf oHalf1 oHalf2", "dat", T.dat[:], T.rpt[:].indirect(T.oHalf[:])),
                lambda: cp("dat oM0 oM1 oM2 oM3 MW", "MW", T.MW[:].indirect(T.oM[:]), T.dat[:]),
                lambda: scan("MW", "PIa", T.PI[:, 0:192], T.MW[:, 1200:1392], T.MW[:, 1200:1392], -1.0, A.add, A.add),
                lambda: scan("MW", "PIb", T.PI[:, 192:C], T.MW[:, 1400:1592], T.MW[:, 1400:1592], -1.0, A.add, A.add),
                lambda: wrap16("PIa PIb", "", None, T.PI[:], C, "wri"),
                lambda: ts("wri cO", "oPI", T.oPI[:], T.wri[:, 15:C:16], col("cO"), A.subtract),
                lambda: scan("MW", "PT", T.PT[:], T.MW[:, 400:784], T.MW[:, 400:784], -193.0, A.add, A.add)]

    def blank_marks():
        dma("s", "tpl tpl2 tpl3", "MW", T.MW[:, 0:1200], T.tpl[:], "d19")
        total["d19"] += 16
        g.sync.dma_start(T.MW[:, 1200:1600], T.tpl[:, 400:800]).then_inc(T.sem.d19, 16)
        note(("d19", total["d19"]), ["tpl2"], ["MW"])

    mask = topo.mask(core, nxt)
    ne, ne_in = len(topo.engines(core, nxt)), len(topo.engines(prv, core))
    rid, pid = topo.addr(nxt)[0], topo.addr(nxt)[1]
    HH = "H0 H1 H2 H3 H4 H5 H6 H7"

    for t in range(R):
        top = 3 + t
        tw = (top + 1) * C
        ns, nv = (NS1, NV1) if t else (NS, NV)
        e = 16 * (24 - NH)
        if t == 0:
            quant("X2", "qxh", T.qx[:, e:C], T.sx[:, e:C], T.X[:, 4 * e:])
            pick_u()
            quant("X1", "", T.qx[:, 128:e], T.sx[:, 128:e], T.X[:, 512:4 * e])
            quant("X", "qx", T.qx[:, 0:128], T.sx[:, 0:128], T.X[:, 0:512])
        else:
            quant("X", "qxh", T.qx[:, e:C], T.sx[:, e:C], T.X[:, 4 * e:])
            quant("X", "qx", T.qx[:, 0:e], T.sx[:, 0:e], T.X[:, 0:4 * e])
        mm("qr sr qxh", "P7", T.P7[:, 0:C - e], T.qr[:], T.sr[:], T.qx[:, e:C], T.sx[:, e:C])
        mm("qr sr qx qxh", "P0", T.P0[:, 0:C], T.qr[:], T.sr[:], T.qx[:], T.sx[:])
        mm("qr sr qx qxh", "P1", T.P1[:, 0:C], T.qr[:], T.sr[:], T.qx[:], T.sx[:])
        if t == 0:
            mm("qu qx qxh", "P3", T.P3[:, 0:C], T.qu[:], T.su[:], T.qx[:], T.sx[:])
            ts("cQ cT1", "cFL", col("cFL"), col("cQ"), 3.5, A.is_lt, col("cT1"), A.mult)
            ts("ci0", "ci3", T.ci[:, 3:4], T.ci[:, 0:1], 31, A.bitwise_and)
            fill = [lambda: cp("ci3", "cP32", col("cP32"), T.ci[:, 3:4]),
                    lambda: mset("rpz", T.rpt[:, 64:96], 0.0),
                    lambda: ts("one cQ4", "oQ4", T.oQ4[:], T.one[:, 0:24], col("cQ4"), A.mult),
                    lambda: cp("ci3", "oHalf", T.oHalf[:, 0:1], T.ci[:, 3:4]),
                    lambda: mset("oHalf1", T.oHalf[:, 1:2], 64),
                    lambda: ts("cP32 one", "oHalf2", T.oHalf[:, 2:4], T.one[:, 0:2], col("cP32"), A.mult, 32.0, A.add),
                    ] + pairc[:2] + tables() + pairc[2:]
        else:
            run(points, 1)
            fill = tables()
        tt("P7 kmin", "mkhi", T.mk[:, e:C], T.P7[:, 0:C - e], T.kmin[:, e:C], A.add)
        if t > 0:
            wrap16("pp", "", None, T.pp[:, 0:C], C, "wrc")
        else:
            mset("rs0", T.rs[:, 0:1], 0.0)
            mset("ppz", T.pp[:, C:C + 1], -100.0)
            cp("ci2", "cQ4", col("cQ4"), T.ci[:, 2:3])
        scan("d0 mkhi", "hi", T.hold[:, e:C], T.d0[:, e:C], T.mk[:, e:C], 0.0, A.add, A.max)
        tt("P0 kmin", "mklo", T.mk[:, 0:e], T.P0[:, 0:e], T.kmin[:, 0:e], A.add)

        def pass1(k):
            i = 23 - k
            act("P1 hi", "tmp%d" % k, T.tmpS[:, C * k:C * k + 16 * i], T.P1[:, 0:16 * i], F.Sign,
                scale=-1.0, bias=T.hold[:, 16 * i + 15:16 * i + 16])

        def pass2(k):
            i = 23 - k
            act("tmp%d mz mz5" % k, "m%d rs%d" % (i, i), mrow(i, 16 * i), T.tmpS[:, C * k:C * k + 16 * i], F.Relu,
                accum_out=T.rs[:, i:i + 1])
        if t == 0:
            pass1(0)
            act("P3", "tmp5", T.tmpS[:, 5 * C:], T.P3[:, 0:C], F.Sign)
            pass1(NS - 1)
            act("tmp5 cFL mz5", "m24", mrow(24, C), T.tmpS[:, 5 * C:], F.Relu, scale=col("cFL"))
            for k in range(1, NS - 1):
                pass1(k)
            pass2(NS - 1)
        else:
            for ks in (range(ns - 1, 2, -1), range(2, -1, -1)):
                for k in ks:
                    pass1(k)
                for k in ks:
                    pass2(k)
        if t == 0:
            blank_marks()
        sums = []
        for i in range(23 - ns, 0, -1):
            if i == 22 - ns:
                scan("d0 mklo", "lo", T.hold[:, 0:e], T.d0[:, 0:e], T.mk[:, 0:e], 0.0, A.add, A.max)
            if i == 18 - NS and t == 0:
                ts("c16", "cK16", T.cK16[:], T.c16[:], 16.0, A.mult)
                quant("m21 m22 m23 m24 mz5", "qm5", T.qm[:, QO[5]:], T.sm[:, QO[5]:], T.M[:, 4 * TO[5]:])
                quant("cb", "qb", T.qb[:], T.sb[:], T.cb[:])
                mm("qb qm5", "P4", T.P4[:, 0:C], T.qb[:], T.sb[:], T.qm[:, QO[5]:], T.sm[:, QO[5]:])
                for k in range(NS - 1):
                    pass2(k)
                act("P4 ppz", "pp", T.pp[:, 0:C], T.P4[:, 0:C], F.Copy)
                run(sums, len(sums))
            if i == (16 if t else 17 - NS):
                tt("P0 hi lo", "m24", mrow(24, C), T.hold[:], T.P0[:, 0:C], A.is_ge)
            ts("P0 mz " + ("hi" if i >= 24 - NH else "lo"), "m%d" % i, mrow(i, 16 * i), T.P0[:, 0:16 * i],
               T.hold[:, 16 * i + 15:16 * i + 16], A.is_lt)
            if nv < i and (t == 0 or i < 13):
                sums.append(lambda i=i: act("m%d" % i, "rs%d jr%d" % (i, i), T.jr[:, 8 * i * (i - 1):8 * i * (i + 1)],
                                            mrow(i, 16 * i), F.Copy, accum_out=T.rs[:, i:i + 1]))
                if t > 0 or i <= 18 - NS:
                    run(sums, 1)
                if t > 0 and i < 12:
                    run(unpack, {11: 1, 9: 1, 7: 3}.get(i, 0))
            if i == (15 if t else 12):
                scan("m24 dm", "ds", T.ds[:], T.dm[:], mrow(24, C), 0.0, A.max, A.subtract)
            if t == 0:
                if i == 11:
                    qtile(5)
                    qtile(4)
                if i == 10:
                    qtile(3)
                if i == 9:
                    wrap16("pp", "", None, T.pp[:, 0:C], C, "wrc")
            if i == 6:
                base()
            if t > 0:
                if i == 14:
                    qtile(4, False)
                    fold(2, 4, 0, 3)
                if i == 12:
                    qtile(3, False)
                    fold(0, 3, 0, 2)
                    fold(1, 3, 1, 2)
                    unpack = [lambda: act("pk0 pk1 pk2", "pkb", T.rs[:, 28:31], T.rs[:, 24:27], F.Identity,
                                          scale=1.0 / FW, bias=ROUND),
                              lambda: act("pkb", "rs14 rs16 rs18", T.rs[:, 14:19:2], T.rs[:, 28:31], F.Identity,
                                          bias=-ROUND)]
                    for m in range(3):
                        a = 13 + 2 * m
                        unpack.append(lambda m=m, a=a: act(
                            "rs%d pk%d" % (a + 1, m), "rs%d" % a, T.rs[:, a:a + 1], T.rs[:, a + 1:a + 2], F.Identity,
                            scale=-FW, bias=T.rs[:, 24 + m:25 + m]))
                if i == Q5:
                    qtile(5)
                    sumtile(4)
                    sumtile(3)
            if i == 7:
                qtile(2)
            if i == 3:
                tt("base ds", "base", T.base[:], T.base[:], T.ds[:, 15:C:16], A.add)
            if i == 2:
                rowsum(nv)
        qtile(1)
        for i in range(nv - 1, 0, -1):
            if i == nv - 2:
                qtile(0)
            rowsum(i)
        rd = " ".join("rs%d" % i for i in range(24))
        if t == 0:
            for k in range(5):
                borders(k)
                run(late, (7, 2, 2, 2, len(late))[k])
        run(fill, FV[t][0])
        tt("base " + rd, "cK16", T.cK16[:, 15:C:16], T.base[:], T.rs[:, 0:24], A.subtract)
        if t == 0:
            act("p40 p41 p42 p43 oQ4", "c4", T.c4[:], T.p4[:, 0:4].indirect(T.oQ4[:]), F.Copy)
        else:
            act("X", "Xh", T.Xh[:], T.X[:], F.Identity, scale=0.5)
        run(fill, FV[t][1])
        scan("P2 cK16", "wrK", T.wrK[:], T.P2[:, 0:C], T.cK16[:], -65536.0, A.max, A.add)
        run(fill, FV[t][2])
        ts("wrK cO16", "oK", T.oK[:], T.wrK[:, 15:C:16], col("cO16"), A.subtract, float(C * top), A.add)
        run(fill, FV[t][3])
        cp("oK tpl2 Wt", "Wt", T.Wt[:, 0:tw].indirect(T.oK[:]), T.tpl[:, 400:400 + C])
        run(fill, FV[t][4])
        scan("Wt", "Pt", T.Pt[:, 0:tw], T.Wt[:, 0:tw], T.Wt[:, 0:tw], -193.0, A.add, A.add)
        run(fill, FV[t][5])
        act("Pt oK", "plrow", T.plrow[:, 0:192], T.Pt[:, 0:tw].indirect(T.oK[:, 0:12]), F.Copy)
        cp("Pt oK", "plrow2", T.plrow[:, 192:C], T.Pt[:, 0:tw].indirect(T.oK[:, 12:24]))
        run(fill, FV[t][6])
        wrap16("plrow plrow2", "", None, T.plrow[:], C)
        run(fill, FV[t][7])
        ts("wr cOC", "oP", T.oP[:], T.wr[:, 15:C:16], col("cOC"), A.subtract)
        run(fill, FV[t][8])
        cp("oP iotaC", "O", T.O[:].indirect(T.oP[:]), T.iotaC[:])
        if t == 0:
            act("X X1 X2", "Xh", T.Xh[:], T.X[:], F.Identity, scale=0.5)
        run(fill, FV[t][9])
        if t > 0:
            act("PT oP", "porow", T.porow[:], T.PT[:].indirect(T.oP[:]), F.Copy)
        act("O oPI", "AB", T.AB[:, 0:192], T.O[:].indirect(T.oPI[:, 0:12]), F.Copy)
        cp("O oPI", "AB2", T.AB[:, 192:C], T.O[:].indirect(T.oPI[:, 12:24]))
        run(fill, FV[t][10])
        if t == 0:
            act("PT oP", "porow", T.porow[:], T.PT[:].indirect(T.oP[:]), F.Copy)
        wrap4("AB AB2", "", None, T.AB[:], C)
        run(fill, FV[t][11])
        ts("wr4 cO4", "oAB4", T.oAB4[:], T.wr4[:, 3:C:4], 4.0, A.mult, col("cO4"), A.add)
        run(fill, FV[t][12])
        for k, (a, b) in enumerate(ZC):
            bh, src = T.Bh[:, 16 * a:16 * b], T.Xh[:].indirect(T.oAB4[:, 48 + a:48 + b])
            if k == 0:
                cp("Xh oAB4", "Bh0", bh, src)
            else:
                act("Xh oAB4", "Bh%d" % k, bh, src, F.Copy)
        wrap16("O", "", None, T.O[:, C - 1:C - 1 - L:-1], L)
        run(fill, FV[t][13])

        def side_a(w, a, b):
            act("X X1 X2 oAB4", w, T.AB4[:, 16 * a:16 * b], T.X[:].indirect(T.oAB4[:, a:b]), F.Copy)

        def zsum(k):
            a, b = ZC[k]
            tt("Xh oAB4 Bh%d" % k, "Z%d" % k, T.Z[:, 16 * a:16 * b],
               T.Xh[:].indirect(T.oAB4[:, a:b]), T.Bh[:, 16 * a:16 * b], A.add)

        def layer(h, rd):
            c = 128 * h
            quant(rd, "qz%d" % h, T.qz[:, c:c + 128], T.sz[:, c:c + 128], T.Z[:, 256 - 256 * h:768 - 256 * h])
            for b in range(4):
                pb = "P%d" % (4 - 4 * h + b)
                mm("qw qz%d" % h, pb, T[pb][:, 0:128], T.qw[:, 128 * b:128 * b + 128],
                   T.sw[:, 128 * b:128 * b + 128], T.qz[:, c:c + 128], T.sz[:, c:c + 128])

        def verdicts(h, rd):
            c, pb = 128 * h, "P%d" % (4 + h)
            quant(rd, "qh%d" % h, T.qh[:, c:c + 128], T.sh[:, c:c + 128], T.Hpm[:, 256 - 256 * h:768 - 256 * h])
            mm("qr sr qh%d" % h, pb, T[pb][:, 0:128], T.qr[:], T.sr[:], T.qh[:, c:c + 128], T.sh[:, c:c + 128])

        def flags(h):
            a, b, pb = 64 - 64 * h, 192 - 128 * h, "P%d" % (4 + h)
            ts(pb, "WL0%d" % h, T.WL[:, a:b], T[pb][:, 0:b - a], 0.0, A.is_gt)
            ts(pb, "WL1%d" % h, T.WL[:, 192 + a:192 + b], T[pb][:, 0:b - a], 0.0, A.is_le)

        def play(w, rd, a, b):
            h = a % 768
            tt("H0 H1 H2 H3 " + rd, w, T.AB4[:, a:b], T.AB4[:, a:b], T.Hpm[:, h:h + b - a], A.add if a < 768 else A.subtract)

        z = 256 * t
        lo, lp = T.lo[:, 16 * t:16 * t + 16], T.lp[:, L * t:L * t + L]
        total["ls"] = total.get("ls", 0) + 6 * ne
        for sem, calls in (("ara", 2), ("arb", 2), ("arl", 1), ("arp", 1)):
            total[sem + str(t)] = calls * ne_in
            lastw[sem + str(t)] = (sem + str(t), calls * ne_in)

        def send(rd, dst, src, sem):
            deps("g", [rd], [])
            g.remote_dma(dst, src, T.sem[sem + str(t)], T.sem.ls, pid, rid, mask)
            note(("ls", total["ls"]), [rd], [])

        def ahead(h, rd):
            c, w = 128 * h, "qs%d" % h
            q, s = T.qz[:, 256 + c:384 + c], T.sz[:, 256 + c:384 + c]
            quant(rd, w, q, s, T.AB4[:, 4 * (NL + c):4 * (NL + c) + 512])
            send(w, T.ql[:, z + c:z + c + 128].bitcast(dt.uint8), q.bitcast(dt.uint8), "ar" + "ab"[h])
            send(w, T.sl[:, z + c:z + c + 128], s, "ar" + "ab"[h])

        def unpack(h):
            c = z + 128 * h
            for b in range(4):
                pb = "P%d" % (4 * h + b)
                mm("qe%d ar%s%d" % (b, "ab"[h], t), pb, T[pb][:, 0:128], T.qe[:, 128 * b:128 * b + 128],
                   T.se[:, 128 * b:128 * b + 128], T.ql[:, c:c + 128], T.sl[:, c:c + 128])
                out = T.Df[:, 512 * h + b:512 * h + 512:4]
                if h or b % 2 == 0:
                    act(pb, "D%d" % (4 * h + b), out, T[pb][:, 0:128], F.Copy)
                else:
                    cp(pb, "D%d" % (4 * h + b), out, T[pb][:, 0:128])
        for k in range(4):
            zsum(k)
        act("Bh0 Bh1 Bh2", "nB1 nB2", T.AB4[:, 1024:], T.Bh[:, 256:], F.Identity, scale=2.0)
        side_a("gA1 nA1", 16, 24)
        layer(0, "Z0 Z1 Z2")
        zsum(4)
        ts("wr cOC", "oR", T.oR[:], T.wr[:, 15:L:16], col("cOC"), A.subtract)
        run(unit, 1)
        layer(1, "Z0 Z1 Z3 Z4")
        wrap4("porow", "", None, T.porow[:], C)
        wrap16("PT", "", None, T.PT[:], C, "wrc")
        ts("wr4 cO4", "oPos4", T.oPos4[:], T.wr4[:, 3:C:4], 4.0, A.mult, col("cO4"), A.add)
        run(fill, len(fill))
        ts("wrc cOC", "oPP", T.oPP[:], T.wrc[:, 15:C:16], col("cOC"), A.subtract)
        for b in range(4):
            pb = "P%d" % (4 + b)
            act(pb, "H%d" % b, T.Hpm[:, 256 + b:768:4], T[pb][:, 0:128], F.Identity, scale=0.03125)
        verdicts(0, "H0 H1 H2 H3")
        for b in range(4):
            pb = "P%d" % b
            if b == 0:
                act(pb, "H%d" % (4 + b), T.Hpm[:, b:256:4], T[pb][:, 0:64], F.Identity, scale=0.03125)
            else:
                ts(pb, "H%d" % (4 + b), T.Hpm[:, b:256:4], T[pb][:, 0:64], 0.03125, A.mult)
        side_a("nA3 nA4", 32, 48)
        act("Bh3 Bh4", "nB0", T.AB4[:, 768:1024], T.Bh[:, 0:256], F.Identity, scale=2.0)
        side_a("gA0 nA0", 0, 16)
        side_a("gA2 nA2", 24, 32)
        act("pp oR", "pold", T.sp[:, L:2 * L], T.pp[:, 0:C].indirect(T.oR[:]), F.Copy)
        play("nB1", "nB1", 1024, 1248)
        verdicts(1, HH)
        flags(0)
        play("nB2", "nB2", 1248, 1536)
        flags(1)
        play("nA4", "nA3", 688, 768)
        ahead(1, "nB1 nB2")
        cp("WL00 WL01 WL10 WL11 oPP", "win", T.win[:, 16:208], T.WL[:].indirect(T.oPP[:, 0:12]))
        act("WL00 WL01 WL10 WL11 oPP", "win2", T.win[:, 208:C + 16], T.WL[:].indirect(T.oPP[:, 12:24]), F.Copy)
        act("win win2 oP", "gain k384", T.gain[:], T.win[:, 16:C + 16].indirect(T.oP[:]), F.Copy)
        play("nA3", "nA3", 512, 688)
        play("nB0", HH + " nB0", 768, 1024)
        scan("MW win2", "la", T.LJ[:, LA:C], T.MW[:, 800 + LA:800 + C], T.win[:, 16 + LA:16 + C], 512.0,
             A.min, A.subtract)
        scan("MW win win2", "om", T.cat[:, 2 * C:0:-2], T.MW[:, C:0:-1], T.win[:, C + 15:15:-1], 0.0,
             A.mult, A.subtract)
        ts("win win2", "lw0", T.cat[:, 3:2 * LA + 2:2], T.win[:, 16:LA + 16], 640.0, A.mult, 256.0, A.subtract)
        tt("win2 la", "lw", T.cat[:, 2 * LA + 3:2 * C + 2:2], T.win[:, LA + 16:C + 16], T.LJ[:, LA:], A.mult)
        ahead(0, "nA3 nA4 nB0")
        play("nA2", "gA2 nA2", 432, 512)
        scan("om lw0 lw c32a c32b c32c c32d", "wr3", T.wr3[:], T.cat[:, 2:2 * C + 2], T.c32[:], -2048.0, A.max, A.add)
        play("nA1", HH + " gA0 gA1 gA2 nA1", 224, 432)
        ts("wr3 cO", "oL", T.oL[:], T.wr3[:, 31:2 * C:32], col("cO"), A.subtract)
        play("nA0", HH + " nA0", 0, 224)
        NB = "nA0 nA1 nA2 nA3 nA4 nB0 nB1 nB2 "
        act(NB + "oPos4 Xh qx qxh", "Xa", T.X[:, 0:HX], T.AB4[:].indirect(T.oPos4[:, 0:HX // 16]), F.Copy)
        cp("oL PT", "LW", T.LW[:].indirect(T.oL[:]), T.PT[:])
        run(unit, 1)
        wrap4("LW", "", None, T.LW[:, 0:L], L)
        wrap16("LW", "", None, T.LW[:, 0:L], L)
        run(unit, 1)
        ts("wr4 cO5", "oL4", T.oL4[:], T.wr4[:, 3:L:4], 4.0, A.mult, col("cO5"), A.add)
        ts("wr cOC", "oL16", T.oL16[:], T.wr[:, 15:L:16], col("cOC"), A.subtract)
        send("oL4", lo, T.oL4[:], "arl")
        tt("gain pp", "pp", T.pp[:, 0:C], T.pp[:, 0:C], T.gain[:], A.add)
        cp(NB + "oPos4", "Xb", T.X[:, HX:HX + 128], T.AB4[:].indirect(T.oPos4[:, HX // 16:HX // 16 + 8]))
        act("WL00 WL01 WL10 WL11 oL16", "wat", T.sp[:, 2 * L:], T.WL[:].indirect(T.oL16[:]), F.Copy)
        act("AB AB2 oL16", "crow", T.crow[:], T.AB[:].indirect(T.oL16[:]), F.Copy)
        run(unit, 1)
        tt("pold wat", "sp", T.sp[:, 0:L], T.sp[:, L:2 * L], T.sp[:, 2 * L:], A.add)
        send("sp", lp, T.sp[:, 0:L], "arp")
        wrap4("crow", "", None, T.crow[:], L)
        wrap16("crow", "", None, T.crow[:], L)
        unpack(1)
        if t == 0:
            a = QO[5] - 128
            quant("zt", "qm4 qmz", T.qm[:, a:a + 128], T.sm[:, a:a + 128], T.zt[:])
        if t == 1:
            quant("vt", "qv", T.qv[:], T.sv[:], T.vt[:])
        ts("wr4 cO4", "oC4", T.oC4[:], T.wr4[:, 3:L:4], 4.0, A.mult, col("cO4"), A.add)
        ts("wr cOC", "oC16", T.oC16[:], T.wr[:, 15:L:16], col("cOC"), A.subtract)
        cp(NB + "oPos4", "X", T.X[:, HX + 128:], T.AB4[:].indirect(T.oPos4[:, HX // 16 + 8:]))
        if t + 1 < R:
            iota("Wt", T.Wt[:, 0:tw + C], [[0, tw + C]], 0, 0)
        unpack(0)
        run(unit, 1)
        if t + 1 < R:
            count("sp", T.sp[:, 0:L], 2, 0)
            count("sp", T.sp[:, 0:L], 2, 1)
            count("pp", T.pp[:, 0:C + 1], 0, 0)
        rd = "D0 D1 D2 D3 D4 D5 D6 D7 arl%d" % t
        act(rd, "Dt0", T.Dt[:, 0:128], T.Df[:].indirect(T.lo[:, 16 * t:16 * t + 8]), F.Copy)
        if t + 1 < R:
            count("pp", T.pp[:, 0:C + 1], 0, 1)
            for k in range(2):
                act("cnt%d cnt%d" % (k, 2 + k), "cnt%d" % (6 + k), T.cnt[:, 6 + k:7 + k], T.cnt[:, 2 + k:3 + k],
                    F.Identity, scale=-1.0, bias=T.cnt[:, k:k + 1])
        else:
            act("pp", "wrK", T.wrK[:], T.pp[:, 0:C], F.Copy)
        cp(rd, "Dt1", T.Dt[:, 128:], T.Df[:].indirect(T.lo[:, 16 * t + 8:16 * t + 16]))
        cp("Dt0 Dt1 oC4 X Xa Xb", "X", T.X[:].indirect(T.oC4[:]), T.Dt[:])
        if t + 1 < R:
            wait("s", ("ls", total["ls"]))
            blank_marks()
        pb = "pp" if t + 1 < R else "wrK"
        points = [lambda t=t, lp=lp, pb=pb: cp("arp%d oC16 " % t + pb, pb, T[pb][:, 0:C].indirect(T.oC16[:]), lp)]
        if t + 1 < R:
            for k in range(2):
                count("arp%d" % t, lp, 4, k)
            for k in range(2):
                act("cnt%d cnt%d" % (6 + k, 4 + k), "cnt%d" % k, T.cnt[:, k:k + 1], T.cnt[:, 4 + k:5 + k], F.Identity,
                    bias=T.cnt[:, 6 + k:7 + k])
            for k in range(1, 5):
                borders(k)

    for k in range(3):
        a, b = 128 * k, 128 * k + 128
        quant("X", "qx qxh qx0" if k == 0 else "qx%d" % k, T.qx[:, a:b], T.sx[:, a:b], T.X[:, 4 * a:4 * b])
        mm("qv qx%d" % k, "P%d" % k, T["P%d" % k][:, 0:128], T.qv[:], T.sv[:], T.qx[:, a:b], T.sx[:, a:b])
        dma("s", "qx%d" % k, "", T.oc[:, 4 * a:4 * b], T.qx[:, a:b].bitcast(dt.uint8))
    run(points, 1)
    for k in range(4):
        dma("s", "qx0 qx1 qx2", "", T.osc[4 * k:4 * k + 4, :], T.sx[32 * k:32 * k + 4, :])
    dma("s", "wrK", "", T.pts[:], T.wrK[0:128:16, :])
    act("P0", "y0", T.yo[:, 0:128], T.P0[:, 0:128], F.Copy)
    act("P1", "y1", T.yo[:, 128:256], T.P1[:, 0:128], F.Copy)
    cp("P2", "y2", T.yo[:, 256:C], T.P2[:, 0:128])
    dma("a", "y0", "", T.y[:, 0:128], T.yo[:, 0:128])
    dma("a", "y1", "", T.y[:, 128:256], T.yo[:, 128:256])
    dma("s", "y2", "", T.y[:, 256:C], T.yo[:, 256:C])
    for s in sorted(total, key=lambda s: (s, total[s]) not in behind):
        wait("g", (s, total[s]))
